import numpy as np
import ml_dtypes


def mxq(x, axis, fmt="e4m3"):
    dtype, down = {"e4m3": (ml_dtypes.float8_e4m3fn, 7), "e5m2": (ml_dtypes.float8_e5m2, 14)}[fmt]
    v = np.moveaxis(np.asarray(x, np.float32).astype(ml_dtypes.bfloat16).astype(np.float64), axis, -1)
    blocks = v.reshape(v.shape[:-1] + (-1, 32))
    amax = np.abs(blocks).max(-1, keepdims=True)
    byte = np.maximum(np.where(amax > 0, np.frexp(amax)[1] - 1 + 127, 0) - down, 1)
    scale = np.exp2(byte - 127.0)
    codes = (blocks / scale).astype(np.float32).astype(dtype).astype(np.float64)
    return np.moveaxis((codes * scale).reshape(v.shape), -1, axis)


WIDE = False


def mx_kscale(k):
    if not WIDE:
        return np.ones(k)
    levels = np.array([10, -10, 5, -5, 0])
    if k % 512:
        return np.exp2(np.random.permutation(np.resize(levels, k // 32))).repeat(32)
    a = np.empty((k // 512, 16))
    for p in range(k // 512):
        a[p, :8] = np.random.permutation(np.resize(levels, 8))
        for g in range(8):
            far = levels[np.abs(levels - a[p, g]) >= 10]
            a[p, g + 8] = far[np.random.randint(len(far))]
    return np.exp2(a.ravel()).repeat(32)


def f64(x):
    return np.asarray(x).astype(np.float64)


def striped(idx):
    return np.tile(idx.reshape(-1, 16).T, (8, 1)).astype(np.uint16)


def unstriped(offs):
    return offs[:16].T.reshape(-1).astype(np.int64)


E2M1 = np.array([0.0, 0.5, 1.0, 1.5, 2.0, 3.0, 4.0, 6.0, -0.0, -0.5, -1.0, -1.5, -2.0, -3.0, -4.0, -6.0])


def pack_weight(w, fmt):
    k, n = w.shape
    w = f64(np.asarray(w, np.float32).astype(ml_dtypes.bfloat16)).reshape(k // 32, 32, n)
    amax = np.abs(w).max(1)
    if fmt == "e4m3":
        byte = np.frexp(amax)[1] - 1 + 127 - 7
    else:
        mant, ex = np.frexp(amax / 6.0)
        byte = np.where(mant > 0.5, ex, ex - 1) + 127
    byte = np.clip(np.where(amax > 0, byte, 1), 1, 254)
    scaled = (w * np.exp2(127.0 - byte)[:, None, :]).reshape(k, n).astype(np.float32)
    by_word = np.ascontiguousarray(scaled.reshape(k // 512, 128, 4, n).transpose(0, 1, 3, 2))
    if fmt == "e4m3":
        words = by_word.astype(ml_dtypes.float8_e4m3fn).view(np.uint8)
    else:
        c = by_word.astype(ml_dtypes.float4_e2m1fn).view(np.uint8) & 0xF
        words = (c[..., 0::2] | (c[..., 1::2] << 4)).reshape(k // 512, 128, 2 * n)
    return np.ascontiguousarray(words), np.ascontiguousarray(byte.astype(np.uint8).reshape(k // 512, 16, n))


def unpack_weight(words, scales, fmt):
    g, _, n = scales.shape
    words = np.ascontiguousarray(words).reshape(g, 128, n, -1)
    if fmt == "e4m3":
        vals = words.view(ml_dtypes.float8_e4m3fn).astype(np.float64)
    else:
        nib = np.empty((g, 128, n, 4), np.uint8)
        nib[..., 0::2] = words & 0xF
        nib[..., 1::2] = words >> 4
        vals = E2M1[nib]
    vals = vals * np.repeat(np.exp2(scales.astype(np.float64) - 127.0), 8, axis=1)[..., None]
    return vals.transpose(0, 1, 3, 2).reshape(g * 512, n)


def gelu(v):
    return 0.5 * v * (1.0 + np.tanh(np.sqrt(2.0 / np.pi) * (v + 0.044715 * v**3)))


K, K2, H, N, T, T2, S = 1024, 512, 1024, 512, 2048, 1024, 512

def setup_inputs():
    n = np.random.standard_normal
    s = mx_kscale(K)[:, None]
    s2 = mx_kscale(K2)[:, None]
    u = mx_kscale(H)[:, None]
    tab_words, tab_scales = pack_weight(n((K, T)) * s, "e4m3")
    tab2_words, tab2_scales = pack_weight(n((K2, T2)) * s2, "e4m3")
    tab3_words, tab3_scales = pack_weight(n((K2, T2)) * s2, "e2m1")
    w1_words, w1_scales = pack_weight(n((K, H)) / np.sqrt(K) / s * u.T, "e2m1")
    w3_words, w3_scales = pack_weight(n((K2, H)) / np.sqrt(K2) / s2 * u.T, "e4m3")
    return {
        "tab_words": tab_words, "tab_scales": tab_scales,
        "tab2_words": tab2_words, "tab2_scales": tab2_scales,
        "tab3_words": tab3_words, "tab3_scales": tab3_scales,
        "offs": striped(np.random.permutation(T)[:S]),
        "offs2": striped(np.random.permutation(T2)[:S]),
        "offs3": striped(np.random.permutation(T2)[:S]),
        "w1_words": w1_words, "w1_scales": w1_scales,
        "w2": (n((K2, H)) / np.sqrt(K2) / s2 * u.T).astype(np.float32),
        "w3_words": w3_words, "w3_scales": w3_scales,
        "w4": (n((H, N)) / np.sqrt(H) / u).astype(np.float32),
        "base": (0.7 * n((N, S))).astype(np.float32),
    }

def reference(tab_words, tab_scales, tab2_words, tab2_scales, tab3_words, tab3_scales, offs, offs2, offs3,
              w1_words, w1_scales, w2, w3_words, w3_scales, w4, base):
    v = unpack_weight(tab_words, tab_scales, "e4m3")[:, unstriped(offs)]
    v2 = unpack_weight(tab2_words, tab2_scales, "e4m3")[:, unstriped(offs2)]
    v3 = unpack_weight(tab3_words, tab3_scales, "e2m1")[:, unstriped(offs3)]
    seed = unpack_weight(w1_words, w1_scales, "e2m1").T @ v
    soil = mxq(f64(w2), 0, "e4m3").T @ v2
    season = unpack_weight(w3_words, w3_scales, "e4m3").T @ v3
    h = np.minimum(seed, np.maximum(soil, season))
    y = mxq(f64(w4), 0, "e4m3").T @ mxq(h, 0, "e4m3")
    return y + f64(base)

@@ -1,0 +1,233 @@
+from contextlib import ExitStack
+
+import concourse.mybir as mybir
+
+K, K2, H, N, T, T2, S = 1024, 512, 1024, 512, 2048, 1024, 512
+FLOPS = 2 * S * H * (K + K2 + K2 + N)
+
+F32 = mybir.dt.float32
+BF16 = mybir.dt.bfloat16
+I32 = mybir.dt.int32
+U32 = mybir.dt.uint32
+U16 = mybir.dt.uint16
+U8 = mybir.dt.uint8
+FP8X4 = mybir.dt.float8_e4m3fn_x4
+FP4X4 = mybir.dt.float4_e2m1fn_x4
+ALU = mybir.AluOpType
+
+P = 128
+PACK = 4
+PASS = 512
+JQ = 128
+NJQ = S // JQ
+NB = H // PASS
+
+
+def tile_list_maize_hybrid_placement_kernel(
+    tc, tab_words, tab_scales, tab2_words, tab2_scales, tab3_words, tab3_scales, offs, offs2, offs3,
+    w1_words, w1_scales, w2, w3_words, w3_scales, w4, base, out,
+):
+    nc = tc.nc
+    with ExitStack() as ctx:
+        keep = ctx.enter_context(tc.tile_pool(name="keep", bufs=1))
+        psum = ctx.enter_context(tc.psum_pool(name="psum", bufs=1))
+
+        def sb(name, shape, dtype, tag=None):
+            return keep.tile(shape, dtype, name=name, tag=tag or name, align_bytes=64)
+
+        idx1 = sb("idx1", [P, S // 16], U16)
+        idx2 = sb("idx2", [P, S // 16], U16)
+        idx3 = sb("idx3", [P, S // 16], U16)
+        t1w = [sb("t1w%d" % a, [P, T], U32) for a in range(2)]
+        t2w = sb("t2w", [P, T2], U32)
+        t3w = sb("t3w", [P, T2], U16)
+        t1s = sb("t1s", [P, T], U8)
+        t2s = sb("t2s", [P, T2], U8)
+        t3s = sb("t3s", [P, T2], U8)
+        w1w_raw = sb("w1w_raw", [P, 2 * 2 * H], U8)
+        w3w_raw = sb("w3w_raw", [P, 4 * H], U8)
+        w1s_raw = sb("w1s_raw", [P, 2 * H], U8)
+        w3s_raw = sb("w3s_raw", [P, H], U8)
+        w2_raw = [sb("w2_raw%d" % b, [P, PACK, PASS], F32) for b in range(NB)]
+        g1s_hi = sb("g1s_hi", [P, S], U8)
+
+        for plane in (t3s, w3s_raw, t1s, t2s, w1s_raw, g1s_hi):
+            nc.vector.memset(plane[:].bitcast(I32), 0)
+
+        def load_scale_rows(plane, first, src):
+            for q in range(4):
+                nc.sync.dma_start(out=plane[32 * q + first : 32 * q + first + 4, :].bitcast(I32),
+                                  in_=src[4 * q : 4 * q + 4, :].bitcast(I32))
+
+        def load_w2(b, j):
+            rows = w2.rearrange("(p j) c -> p j c", j=PACK)
+            nc.sync.dma_start(out=w2_raw[b][:, j : j + 2, :], in_=rows[:, j : j + 2, PASS * b : PASS * (b + 1)])
+
+        def load_halves(dst, src):
+            half = dst.shape[1] // 2
+            for first in (0, half):
+                nc.sync.dma_start(out=dst[:, first : first + half], in_=src[:, first : first + half])
+
+        def words(src):
+            return src.rearrange("p t i -> p (t i)").bitcast(I32)
+
+        nc.sync.dma_start(idx3[:], offs3)
+        load_halves(t3w[:].bitcast(I32), tab3_words[0].bitcast(I32))
+        load_halves(w3w_raw[:].bitcast(I32), words(w3_words[0]))
+        nc.sync.dma_start(idx2[:], offs2)
+        nc.sync.dma_start(idx1[:], offs)
+        load_scale_rows(t3s, 0, tab3_scales[0])
+        nc.sync.dma_start(out=t2w[:].bitcast(I32), in_=words(tab2_words[0]))
+        load_scale_rows(w3s_raw, 0, w3_scales[0])
+        load_w2(0, 0)
+        load_w2(0, 2)
+        for q in range(4):
+            nc.sync.dma_start(out=t1s[32 * q : 32 * q + 8, :].bitcast(I32),
+                              in_=tab_scales[:, 4 * q : 4 * q + 4, :].bitcast(I32))
+        load_w2(1, 0)
+        load_scale_rows(t2s, 8, tab2_scales[0])
+        load_w2(1, 2)
+        load_halves(t1w[0][:].bitcast(I32), words(tab_words[0]))
+        nc.sync.dma_start(out=w1w_raw[:].bitcast(I32).rearrange("p (a c) -> p a c", a=2),
+                          in_=w1_words.bitcast(I32).rearrange("a p c -> p a c"))
+        for q in range(4):
+            nc.sync.dma_start(out=w1s_raw[32 * q : 32 * q + 4, :].bitcast(I32).rearrange("r (a c) -> r a c", a=2),
+                              in_=w1_scales[:, 4 * q : 4 * q + 4, :].bitcast(I32).rearrange("a r c -> r a c"))
+        nc.sync.dma_start(out=t1w[1][:].bitcast(I32), in_=words(tab_words[1]))
+
+        def load_w4(b):
+            raw = sb("w4_raw%d" % b, [P, PACK, N], F32, "w2_raw%d" % b)
+            rows = w4[PASS * b : PASS * (b + 1), :].rearrange("(g t i) n -> t g i n", t=PACK, i=8)
+            for t in range(PACK):
+                nc.sync.dma_start(out=raw[:, t, :], in_=rows[t])
+            return raw
+
+        def pick(name, window, idx, dtype, tag=None):
+            got = sb(name, [P, S], dtype, tag)
+            nc.vector.tensor_copy(got[:], window[:].indirect(idx[:]))
+            return got
+
+        def reorder(name, raw, run, tag=None):
+            done = sb(name, list(raw.shape), U8, tag)
+            nc.vector.tensor_copy(
+                out=done[:].bitcast(I32).rearrange("p (u t g w) -> p u t g w", t=PACK, g=16, w=run),
+                in_=raw[:].bitcast(I32).rearrange("p (u g t w) -> p u t g w", t=PACK, g=16, w=run))
+            return done
+
+        def quantize(name, grouped, width):
+            codes = sb(name + "_codes", [P, width], U32)
+            scales = sb(name + "_scales", [P, width], U8)
+            nc.vector.quantize_mx(out=codes[:].bitcast(FP8X4), scales=scales[:], in_=grouped[:])
+            return codes, scales
+
+        def cast_w2(b, copy, tag=None):
+            grouped = sb("w2_bf%d" % b, [P, PACK * PASS], BF16, tag)
+            dst = grouped[:].rearrange("p (t g u v j) -> p t g u j v", t=PACK, g=16, u=2, v=4)
+            src = w2_raw[b][:].rearrange("p j (g t u v) -> p t g u j v", t=PACK, u=2, v=4)
+            for t in range(PACK):
+                copy(out=dst[:, t], in_=src[:, t])
+            return grouped
+
+        def cast_w4(b, copy, tag):
+            grouped = sb("w4_bf%d" % b, [P, PACK * N], BF16, tag)
+            copy(out=grouped[:].rearrange("p (u v t) -> p u t v", v=4, t=PACK),
+                 in_=w4_raw[b][:].rearrange("p t (u v) -> p u t v", v=4))
+            return grouped
+
+        def cols(first, count=P):
+            return slice(first, first + count)
+
+        def interleaved(bank):
+            return bank[:].rearrange("p t j -> p j t")
+
+        def as_jt(ap):
+            return ap.rearrange("p (j t) -> p j t", t=PACK)
+
+        g3w = pick("g3w", t3w, idx3, U16)
+        g3s = pick("g3s", t3s, idx3, U8)
+        w3w = reorder("w3w", w3w_raw, 8)
+        w3s = reorder("w3s", w3s_raw, 2)
+
+        season = {}
+        for jq in range(NJQ):
+            for b in range(NB):
+                bank = psum.tile([P, PACK, JQ], F32, name="first", tag="first", bufs=6)
+                for t in range(PACK):
+                    c = PASS * b + P * t
+                    nc.tensor.matmul_mx(out=bank[:, t, :], lhsT=w3w[:, cols(4 * c, 4 * P)].bitcast(FP8X4),
+                                        lhsT_scale=w3s[:, cols(c)], rhs=g3w[:, cols(JQ * jq)].bitcast(FP4X4),
+                                        rhs_scale=g3s[:, cols(JQ * jq)], start=True, stop=True)
+                season[jq, b] = sb("season%d%d" % (jq, b), [P, PASS], BF16)
+                nc.scalar.copy(out=as_jt(season[jq, b][:]), in_=interleaved(bank))
+
+        g2w = pick("g2w", t2w, idx2, U32, "w3s_raw")
+        g1s = pick("g1s", t1s, idx1, U8, "t2w")
+        for q in range(4):
+            nc.sync.dma_start(out=g1s_hi[32 * q : 32 * q + 4, :].bitcast(I32),
+                                in_=g1s[32 * q + 4 : 32 * q + 8, :].bitcast(I32))
+        g1s_planes = [g1s, g1s_hi]
+        w2q = [quantize("w2q0", cast_w2(0, nc.vector.tensor_copy, "t1s"), PASS)]
+        w4_raw = [load_w4(0)]
+        g2s = pick("g2s", t2s, idx2, U8, "t1s")
+        w2q.append(quantize("w2q1", cast_w2(1, nc.scalar.copy, "g3w"), PASS))
+        w4_raw.append(load_w4(1))
+        g1w = [pick("g1w0", t1w[0], idx1, U32, "t2s")]
+        w1w = reorder("w1w", w1w_raw, 4, "t1w0")
+        w1s = reorder("w1s", w1s_raw, 2, "w1w_raw")
+
+        better = {}
+        for b in range(NB):
+            for jq in range(NJQ):
+                bank = psum.tile([P, PACK, JQ], F32, name="first", tag="first", bufs=6)
+                codes, scales = w2q[b]
+                for t in range(PACK):
+                    nc.tensor.matmul_mx(out=bank[:, t, :], lhsT=codes[:, cols(P * t)].bitcast(FP8X4),
+                                        lhsT_scale=scales[:, cols(P * t)], rhs=g2w[:, cols(JQ * jq)].bitcast(FP8X4),
+                                        rhs_scale=g2s[8:P, cols(JQ * jq)], start=True, stop=True)
+                soil = sb("soil%d%d" % (jq, b), [P, PASS], BF16)
+                nc.scalar.copy(out=as_jt(soil[:]), in_=interleaved(bank))
+                better[jq, b] = sb("better%d%d" % (jq, b), [P, PASS], BF16)
+                nc.vector.tensor_tensor(better[jq, b][:], soil[:], season[jq, b][:], ALU.max)
+            if b == 0:
+                g1w.append(pick("g1w1", t1w[1], idx1, U32, "soil10"))
+        base_sb = sb("base_sb", [P, N // P, S], F32, "t1w1")
+        nc.sync.dma_start(out=base_sb[:], in_=base.rearrange("(c p) j -> p c j", p=P))
+
+        def make_h(jq):
+            h = sb("h%d" % jq, [P, NB * PASS], BF16)
+            for b in range(NB):
+                bank = psum.tile([P, PACK, JQ], F32, name="first", tag="first", bufs=6)
+                for a in range(2):
+                    for t in range(PACK):
+                        c = H * a + PASS * b + P * t
+                        nc.tensor.matmul_mx(out=bank[:, t, :], lhsT=w1w[:, cols(2 * c, 2 * P)].bitcast(FP4X4),
+                                            lhsT_scale=w1s[:, cols(c)], rhs=g1w[a][:, cols(JQ * jq)].bitcast(FP8X4),
+                                            rhs_scale=g1s_planes[a][:, cols(JQ * jq)],
+                                            start=(a == 0 and t == 0), stop=(a == 1 and t == PACK - 1))
+                seed = sb("seed%d%d" % (jq, b), [P, PASS], BF16)
+                nc.scalar.copy(out=as_jt(seed[:]), in_=interleaved(bank))
+                nc.vector.tensor_tensor(h[:, cols(PASS * b, PASS)], seed[:], better[jq, b][:], ALU.min)
+            return h
+
+        def finish(jq, h):
+            codes, scales = quantize("hq%d" % jq, h, NB * JQ)
+            bank = psum.tile([P, N // P, JQ], F32, name="ybank", tag="ybank", bufs=2)
+            for c in range(N // P):
+                for b in range(NB):
+                    nc.tensor.matmul_mx(out=bank[:, c, :], lhsT=w4q[b][0][:, cols(P * c)].bitcast(FP8X4),
+                                        lhsT_scale=w4q[b][1][:, cols(P * c)],
+                                        rhs=codes[:, cols(JQ * b)].bitcast(FP8X4), rhs_scale=scales[:, cols(JQ * b)],
+                                        start=(b == 0), stop=(b == NB - 1))
+            res = sb("res%d" % jq, [P, N // P, JQ], F32)
+            nc.vector.tensor_tensor(res[:], bank[:], base_sb[:, :, cols(JQ * jq)], ALU.add)
+            nc.sync.dma_start(out=out.rearrange("(c p) j -> p c j", p=P)[:, :, cols(JQ * jq)], in_=res[:])
+
+        hs = [make_h(0), make_h(1)]
+        w4_bf0 = cast_w4(0, nc.scalar.copy, "seed10")
+        w4_bf1 = cast_w4(1, nc.vector.tensor_copy, "seed11")
+        w4q = [None, quantize("w4q1", w4_bf1, N)]
+        w4q[0] = quantize("w4q0", w4_bf0, N)
+        for jq in range(NJQ):
+            if jq + 2 < NJQ:
+                hs.append(make_h(jq + 2))
+            finish(jq, hs[jq])

@@ -51,52 +51,51 @@ def tile_list_maize_hybrid_placement_kernel(
         w2_raw = [sb("w2_raw%d" % b, [P, PACK, PASS], F32) for b in range(NB)]
         g1s_hi = sb("g1s_hi", [P, S], U8)
 
-        for plane in (t3s, w3s_raw, t1s, t2s, w1s_raw, g1s_hi):
+        for plane in (t3s, w3s_raw, t2s, t1s, w1s_raw):
             nc.vector.memset(plane[:].bitcast(I32), 0)
+        warm = sb("warm", [P, 2], F32)
+        nc.vector.memset(warm[:, 0:1], 0.0)
+        nc.scalar.copy(out=warm[:, 1:2], in_=warm[:, 0:1])
+        nc.gpsimd.memset(g1s_hi[:].bitcast(I32), 0)
 
-        def load_scale_rows(plane, first, src):
+        def load_scale_rows(queue, plane, first, src):
             for q in range(4):
-                nc.sync.dma_start(out=plane[32 * q + first : 32 * q + first + 4, :].bitcast(I32),
-                                  in_=src[4 * q : 4 * q + 4, :].bitcast(I32))
+                queue.dma_start(out=plane[32 * q + first : 32 * q + first + 4, :].bitcast(I32),
+                                in_=src[4 * q : 4 * q + 4, :].bitcast(I32))
 
-        def load_w2(b, j):
+        def load_w2(b, first, last):
             rows = w2.rearrange("(p j) c -> p j c", j=PACK)
-            nc.sync.dma_start(out=w2_raw[b][:, j : j + 2, :], in_=rows[:, j : j + 2, PASS * b : PASS * (b + 1)])
-
-        def load_halves(dst, src):
-            half = dst.shape[1] // 2
-            for first in (0, half):
-                nc.sync.dma_start(out=dst[:, first : first + half], in_=src[:, first : first + half])
+            nc.sync.dma_start(out=w2_raw[b][:, first:last, :], in_=rows[:, first:last, PASS * b : PASS * (b + 1)])
 
         def words(src):
             return src.rearrange("p t i -> p (t i)").bitcast(I32)
 
         nc.sync.dma_start(idx3[:], offs3)
-        load_halves(t3w[:].bitcast(I32), tab3_words[0].bitcast(I32))
-        load_halves(w3w_raw[:].bitcast(I32), words(w3_words[0]))
+        nc.sync.dma_start(out=t3w[:].bitcast(I32), in_=tab3_words[0].bitcast(I32))
+        nc.sync.dma_start(out=t2w[:].bitcast(I32), in_=words(tab2_words[0]))
         nc.sync.dma_start(idx2[:], offs2)
         nc.sync.dma_start(idx1[:], offs)
-        load_scale_rows(t3s, 0, tab3_scales[0])
-        nc.sync.dma_start(out=t2w[:].bitcast(I32), in_=words(tab2_words[0]))
-        load_scale_rows(w3s_raw, 0, w3_scales[0])
-        load_w2(0, 0)
-        load_w2(0, 2)
-        for q in range(4):
-            nc.sync.dma_start(out=t1s[32 * q : 32 * q + 8, :].bitcast(I32),
-                              in_=tab_scales[:, 4 * q : 4 * q + 4, :].bitcast(I32))
-        load_w2(1, 0)
-        load_scale_rows(t2s, 8, tab2_scales[0])
-        load_w2(1, 2)
-        load_halves(t1w[0][:].bitcast(I32), words(tab_words[0]))
+        load_w2(0, 0, 2)
+        load_w2(0, 2, 4)
+        load_scale_rows(nc.sync, t3s, 0, tab3_scales[0])
+        nc.sync.dma_start(out=w3w_raw[:].bitcast(I32), in_=words(w3_words[0]))
+        load_w2(1, 0, 2)
+        load_scale_rows(nc.sync, w3s_raw, 0, w3_scales[0])
+        load_w2(1, 2, 4)
+        nc.sync.dma_start(out=t1w[0][:].bitcast(I32), in_=words(tab_words[0]))
+        load_scale_rows(nc.sync, t2s, 8, tab2_scales[0])
         nc.sync.dma_start(out=w1w_raw[:].bitcast(I32).rearrange("p (a c) -> p a c", a=2),
                           in_=w1_words.bitcast(I32).rearrange("a p c -> p a c"))
         for q in range(4):
+            nc.sync.dma_start(out=t1s[32 * q : 32 * q + 8, :].bitcast(I32),
+                              in_=tab_scales[:, 4 * q : 4 * q + 4, :].bitcast(I32))
+        nc.sync.dma_start(out=t1w[1][:].bitcast(I32), in_=words(tab_words[1]))
+        for q in range(4):
             nc.sync.dma_start(out=w1s_raw[32 * q : 32 * q + 4, :].bitcast(I32).rearrange("r (a c) -> r a c", a=2),
                               in_=w1_scales[:, 4 * q : 4 * q + 4, :].bitcast(I32).rearrange("a r c -> r a c"))
-        nc.sync.dma_start(out=t1w[1][:].bitcast(I32), in_=words(tab_words[1]))
 
-        def load_w4(b):
-            raw = sb("w4_raw%d" % b, [P, PACK, N], F32, "w2_raw%d" % b)
+        def load_w4(b, tag):
+            raw = sb("w4_raw%d" % b, [P, PACK, N], F32, tag)
             rows = w4[PASS * b : PASS * (b + 1), :].rearrange("(g t i) n -> t g i n", t=PACK, i=8)
             for t in range(PACK):
                 nc.sync.dma_start(out=raw[:, t, :], in_=rows[t])
@@ -114,10 +113,10 @@ def tile_list_maize_hybrid_placement_kernel(
                 in_=raw[:].bitcast(I32).rearrange("p (u g t w) -> p u t g w", t=PACK, g=16, w=run))
             return done
 
-        def quantize(name, grouped, width):
-            codes = sb(name + "_codes", [P, width], U32)
+        def quantize(name, grouped, width, tag=None):
+            codes = sb(name + "_codes", [P, width], U32, tag)
             scales = sb(name + "_scales", [P, width], U8)
-            nc.vector.quantize_mx(out=codes[:].bitcast(FP8X4), scales=scales[:], in_=grouped[:])
+            nc.vector.quantize_mx(out=codes[:].bitcast(FP8X4), scales=scales[:], in_=grouped[:, :])
             return codes, scales
 
         def cast_w2(b, copy, tag=None):
@@ -128,10 +127,10 @@ def tile_list_maize_hybrid_placement_kernel(
                 copy(out=dst[:, t], in_=src[:, t])
             return grouped
 
-        def cast_w4(b, copy, tag):
-            grouped = sb("w4_bf%d" % b, [P, PACK * N], BF16, tag)
+        def cast_w4(b, first, count, copy):
+            grouped = sb("w4_bf%d%d" % (b, first), [P, PACK * P * count], BF16)
             copy(out=grouped[:].rearrange("p (u v t) -> p u t v", v=4, t=PACK),
-                 in_=w4_raw[b][:].rearrange("p t (u v) -> p u t v", v=4))
+                 in_=w4_raw[b][:, :, P * first : P * (first + count)].rearrange("p t (u v) -> p u t v", v=4))
             return grouped
 
         def cols(first, count=P):
@@ -143,91 +142,127 @@ def tile_list_maize_hybrid_placement_kernel(
         def as_jt(ap):
             return ap.rearrange("p (j t) -> p j t", t=PACK)
 
+        def first_bank():
+            return psum.tile([P, PACK, JQ], F32, name="bank", tag="bank", bufs=8)
+
+        def evacuate(rounded, bank):
+            nc.scalar.copy(out=as_jt(rounded), in_=interleaved(bank))
+
+        def season_sum(jq, b):
+            bank = first_bank()
+            for t in range(PACK):
+                c = PASS * b + P * t
+                nc.tensor.matmul_mx(out=bank[:, t, :], lhsT=w3w[:, cols(4 * c, 4 * P)].bitcast(FP8X4),
+                                    lhsT_scale=w3s[:, cols(c)], rhs=g3w[:, cols(JQ * jq)].bitcast(FP4X4),
+                                    rhs_scale=g3s[:, cols(JQ * jq)], start=True, stop=True)
+            evacuate(season[b][:, cols(PASS * jq, PASS)], bank)
+
+        def soil_sum(jq, b):
+            bank = first_bank()
+            codes, scales = w2q[b]
+            for t in range(PACK):
+                nc.tensor.matmul_mx(out=bank[:, t, :], lhsT=codes[:, cols(P * t)].bitcast(FP8X4),
+                                    lhsT_scale=scales[:, cols(P * t)], rhs=g2w[:, cols(JQ * jq)].bitcast(FP8X4),
+                                    rhs_scale=g2s[8:P, cols(JQ * jq)], start=True, stop=True)
+            evacuate(soil[b][:, cols(PASS * jq, PASS)], bank)
+
+        def seed_sum(jq, b):
+            bank = first_bank()
+            for a in range(2):
+                for t in range(PACK):
+                    c = H * a + PASS * b + P * t
+                    nc.tensor.matmul_mx(out=bank[:, t, :], lhsT=w1w[:, cols(2 * c, 2 * P)].bitcast(FP4X4),
+                                        lhsT_scale=w1s[:, cols(c)], rhs=g1w[a][:, cols(JQ * jq)].bitcast(FP8X4),
+                                        rhs_scale=g1s_planes[a][:, cols(JQ * jq)],
+                                        start=(a == 0 and t == 0), stop=(a == 1 and t == PACK - 1))
+            evacuate(seed[jq][:, cols(PASS * b, PASS)], bank)
+
+        def output_passes(bank, c, b, codes, scales):
+            for jq in range(NJQ):
+                h_codes, h_scales = hq[jq]
+                nc.tensor.matmul_mx(out=bank[:, jq, :], lhsT=codes.bitcast(FP8X4), lhsT_scale=scales,
+                                    rhs=h_codes[:, cols(JQ * b)].bitcast(FP8X4), rhs_scale=h_scales[:, cols(JQ * b)],
+                                    start=(b == 0 and jq == 0), stop=(b == NB - 1 and jq == NJQ - 1))
+
+        season = [sb("season%d" % b, [P, NJQ * PASS], BF16) for b in range(NB)]
+        soil = [sb("soil%d" % b, [P, NJQ * PASS], BF16) for b in range(NB)]
+        seed = [sb("seed%d" % jq, [P, NB * PASS], BF16) for jq in range(NJQ)]
+
         g3w = pick("g3w", t3w, idx3, U16)
+        g2w = pick("g2w", t2w, idx2, U32)
+        w2_bf0 = cast_w2(0, nc.scalar.copy)
         g3s = pick("g3s", t3s, idx3, U8)
         w3w = reorder("w3w", w3w_raw, 8)
         w3s = reorder("w3s", w3s_raw, 2)
-
-        season = {}
-        for jq in range(NJQ):
-            for b in range(NB):
-                bank = psum.tile([P, PACK, JQ], F32, name="first", tag="first", bufs=6)
-                for t in range(PACK):
-                    c = PASS * b + P * t
-                    nc.tensor.matmul_mx(out=bank[:, t, :], lhsT=w3w[:, cols(4 * c, 4 * P)].bitcast(FP8X4),
-                                        lhsT_scale=w3s[:, cols(c)], rhs=g3w[:, cols(JQ * jq)].bitcast(FP4X4),
-                                        rhs_scale=g3s[:, cols(JQ * jq)], start=True, stop=True)
-                season[jq, b] = sb("season%d%d" % (jq, b), [P, PASS], BF16)
-                nc.scalar.copy(out=as_jt(season[jq, b][:]), in_=interleaved(bank))
-
-        g2w = pick("g2w", t2w, idx2, U32, "w3s_raw")
-        g1s = pick("g1s", t1s, idx1, U8, "t2w")
-        for q in range(4):
-            nc.sync.dma_start(out=g1s_hi[32 * q : 32 * q + 4, :].bitcast(I32),
-                                in_=g1s[32 * q + 4 : 32 * q + 8, :].bitcast(I32))
-        g1s_planes = [g1s, g1s_hi]
-        w2q = [quantize("w2q0", cast_w2(0, nc.vector.tensor_copy, "t1s"), PASS)]
-        w4_raw = [load_w4(0)]
-        g2s = pick("g2s", t2s, idx2, U8, "t1s")
-        w2q.append(quantize("w2q1", cast_w2(1, nc.scalar.copy, "g3w"), PASS))
-        w4_raw.append(load_w4(1))
-        g1w = [pick("g1w0", t1w[0], idx1, U32, "t2s")]
-        w1w = reorder("w1w", w1w_raw, 4, "t1w0")
-        w1s = reorder("w1s", w1s_raw, 2, "w1w_raw")
-
-        better = {}
         for b in range(NB):
             for jq in range(NJQ):
-                bank = psum.tile([P, PACK, JQ], F32, name="first", tag="first", bufs=6)
-                codes, scales = w2q[b]
-                for t in range(PACK):
-                    nc.tensor.matmul_mx(out=bank[:, t, :], lhsT=codes[:, cols(P * t)].bitcast(FP8X4),
-                                        lhsT_scale=scales[:, cols(P * t)], rhs=g2w[:, cols(JQ * jq)].bitcast(FP8X4),
-                                        rhs_scale=g2s[8:P, cols(JQ * jq)], start=True, stop=True)
-                soil = sb("soil%d%d" % (jq, b), [P, PASS], BF16)
-                nc.scalar.copy(out=as_jt(soil[:]), in_=interleaved(bank))
-                better[jq, b] = sb("better%d%d" % (jq, b), [P, PASS], BF16)
-                nc.vector.tensor_tensor(better[jq, b][:], soil[:], season[jq, b][:], ALU.max)
-            if b == 0:
-                g1w.append(pick("g1w1", t1w[1], idx1, U32, "soil10"))
-        base_sb = sb("base_sb", [P, N // P, S], F32, "t1w1")
+                season_sum(jq, b)
+
+        w2q = [quantize("w2q0", w2_bf0, PASS, "w3s_raw")]
+        w2q.append(quantize("w2q1", cast_w2(1, nc.vector.tensor_copy), PASS))
+        g1w = [pick("g1w0", t1w[0], idx1, U32)]
+        g2s = pick("g2s", t2s, idx2, U8)
+        g1s = pick("g1s", t1s, idx1, U8)
+        for q in range(4):
+            nc.sync.dma_start(out=g1s_hi[32 * q : 32 * q + 4, :].bitcast(I32),
+                              in_=g1s[32 * q + 4 : 32 * q + 8, :].bitcast(I32))
+        g1s_planes = [g1s, g1s_hi]
+        w4_raw = [load_w4(0, "t1s")]
+        w1w = reorder("w1w", w1w_raw, 4)
+        w1s = reorder("w1s", w1s_raw, 2)
+        g1w.append(pick("g1w1", t1w[1], idx1, U32, "w1s_raw"))
+
+        better = sb("better", [P, NB, NJQ * PASS], BF16, "t1w1")
+        for b in range(NB):
+            for jq in range(NJQ):
+                soil_sum(jq, b)
+            nc.vector.tensor_tensor(better[:, b, :], soil[b][:], season[b][:], ALU.max)
+        w4_raw.append(load_w4(1, "soil0"))
+        base_sb = sb("base_sb", [P, N // P, S], F32, "soil1")
         nc.sync.dma_start(out=base_sb[:], in_=base.rearrange("(c p) j -> p c j", p=P))
 
-        def make_h(jq):
-            h = sb("h%d" % jq, [P, NB * PASS], BF16)
+        def make_h(jq, dst):
             for b in range(NB):
-                bank = psum.tile([P, PACK, JQ], F32, name="first", tag="first", bufs=6)
-                for a in range(2):
-                    for t in range(PACK):
-                        c = H * a + PASS * b + P * t
-                        nc.tensor.matmul_mx(out=bank[:, t, :], lhsT=w1w[:, cols(2 * c, 2 * P)].bitcast(FP4X4),
-                                            lhsT_scale=w1s[:, cols(c)], rhs=g1w[a][:, cols(JQ * jq)].bitcast(FP8X4),
-                                            rhs_scale=g1s_planes[a][:, cols(JQ * jq)],
-                                            start=(a == 0 and t == 0), stop=(a == 1 and t == PACK - 1))
-                seed = sb("seed%d%d" % (jq, b), [P, PASS], BF16)
-                nc.scalar.copy(out=as_jt(seed[:]), in_=interleaved(bank))
-                nc.vector.tensor_tensor(h[:, cols(PASS * b, PASS)], seed[:], better[jq, b][:], ALU.min)
-            return h
+                seed_sum(jq, b)
+            nc.vector.tensor_tensor(dst.rearrange("p (b c) -> p b c", b=NB),
+                                    seed[jq][:].rearrange("p (b c) -> p b c", b=NB),
+                                    better[:, :, cols(PASS * jq, PASS)], ALU.min)
 
-        def finish(jq, h):
-            codes, scales = quantize("hq%d" % jq, h, NB * JQ)
-            bank = psum.tile([P, N // P, JQ], F32, name="ybank", tag="ybank", bufs=2)
-            for c in range(N // P):
-                for b in range(NB):
-                    nc.tensor.matmul_mx(out=bank[:, c, :], lhsT=w4q[b][0][:, cols(P * c)].bitcast(FP8X4),
-                                        lhsT_scale=w4q[b][1][:, cols(P * c)],
-                                        rhs=codes[:, cols(JQ * b)].bitcast(FP8X4), rhs_scale=scales[:, cols(JQ * b)],
-                                        start=(b == 0), stop=(b == NB - 1))
-            res = sb("res%d" % jq, [P, N // P, JQ], F32)
-            nc.vector.tensor_tensor(res[:], bank[:], base_sb[:, :, cols(JQ * jq)], ALU.add)
-            nc.sync.dma_start(out=out.rearrange("(c p) j -> p c j", p=P)[:, :, cols(JQ * jq)], in_=res[:])
+        w4q = {}
 
-        hs = [make_h(0), make_h(1)]
-        w4_bf0 = cast_w4(0, nc.scalar.copy, "seed10")
-        w4_bf1 = cast_w4(1, nc.vector.tensor_copy, "seed11")
-        w4q = [None, quantize("w4q1", w4_bf1, N)]
-        w4q[0] = quantize("w4q0", w4_bf0, N)
-        for jq in range(NJQ):
-            if jq + 2 < NJQ:
-                hs.append(make_h(jq + 2))
-            finish(jq, hs[jq])
+        def quantize_w4(b, first, count, grouped):
+            codes, scales = quantize("w4q%d%d" % (b, first), grouped, P * count)
+            for n in range(count):
+                w4q[b, first + n] = (codes[:, cols(P * n)], scales[:, cols(P * n)])
+
+        h_first = sb("h_first", [P, H], BF16)
+        make_h(0, h_first[:])
+        w4_early = cast_w4(0, 0, 2, nc.vector.tensor_copy)
+        hq = [quantize("hq0", h_first, NB * JQ)]
+        quantize_w4(0, 0, 2, w4_early)
+        h_rest = sb("h_rest", [P, (NJQ - 1) * H], BF16, "w4_bf00")
+        for jq in range(1, NJQ):
+            make_h(jq, h_rest[:, cols(H * (jq - 1), H)])
+            if jq > 1:
+                hq.append(quantize("hq%d" % (jq - 1), h_rest[:, cols(H * (jq - 2), H)], NB * JQ))
+        hq.append(quantize("hq%d" % (NJQ - 1), h_rest[:, cols(H * (NJQ - 2), H)], NB * JQ))
+
+        def output_sum(c):
+            if c == 2:
+                quantize_w4(0, 2, 2, cast_w4(0, 2, 2, nc.scalar.copy))
+            quantize_w4(1, c, 1, cast_w4(1, c, 1, nc.scalar.copy))
+            bank = first_bank()
+            for b in range(NB):
+                output_passes(bank, c, b, *w4q[b, c])
+            return bank
+
+        def finish(c, bank):
+            res = sb("res%d" % c, [P, S], F32)
+            nc.vector.tensor_tensor(res[:], bank[:].rearrange("p q j -> p (q j)"), base_sb[:, c, :], ALU.add)
+            nc.sync.dma_start(out=out[cols(P * c), :], in_=res[:])
+
+        banks = [output_sum(0)]
+        for c in range(1, N // P):
+            banks.append(output_sum(c))
+            finish(c - 1, banks[c - 1])
+        finish(N // P - 1, banks[N // P - 1])

@@ -1,6 +1,7 @@
 from contextlib import ExitStack
 
 import concourse.mybir as mybir
+from concourse.masks import make_identity
 
 K, K2, H, N, T, T2, S = 1024, 512, 1024, 512, 2048, 1024, 512
 FLOPS = 2 * S * H * (K + K2 + K2 + N)
@@ -18,9 +19,11 @@ ALU = mybir.AluOpType
 P = 128
 PACK = 4
 PASS = 512
-JQ = 128
-NJQ = S // JQ
+NJ = S // P
 NB = H // PASS
+ROWS = 16
+TOP = 96
+AT_A, AT_B, AT_C, AT_D, AT_E = 1024, 16384, 32768, 49152, 69632
 
 
 def tile_list_maize_hybrid_placement_kernel(
@@ -30,239 +33,254 @@ def tile_list_maize_hybrid_placement_kernel(
     nc = tc.nc
     with ExitStack() as ctx:
         keep = ctx.enter_context(tc.tile_pool(name="keep", bufs=1))
+        shared = ctx.enter_context(tc.tile_pool(name="shared", bufs=1))
         psum = ctx.enter_context(tc.psum_pool(name="psum", bufs=1))
 
-        def sb(name, shape, dtype, tag=None):
-            return keep.tile(shape, dtype, name=name, tag=tag or name, align_bytes=64)
-
-        idx1 = sb("idx1", [P, S // 16], U16)
-        idx2 = sb("idx2", [P, S // 16], U16)
-        idx3 = sb("idx3", [P, S // 16], U16)
-        t1w = [sb("t1w%d" % a, [P, T], U32) for a in range(2)]
-        t2w = sb("t2w", [P, T2], U32)
-        t3w = sb("t3w", [P, T2], U16)
-        t1s = sb("t1s", [P, T], U8)
-        t2s = sb("t2s", [P, T2], U8)
-        t3s = sb("t3s", [P, T2], U8)
-        w1w_raw = sb("w1w_raw", [P, 2 * 2 * H], U8)
-        w3w_raw = sb("w3w_raw", [P, 4 * H], U8)
-        w1s_raw = sb("w1s_raw", [P, 2 * H], U8)
-        w3s_raw = sb("w3s_raw", [P, H], U8)
-        w2_raw = [sb("w2_raw%d" % b, [P, PACK, PASS], F32) for b in range(NB)]
-        g1s_hi = sb("g1s_hi", [P, S], U8)
-
-        for plane in (t3s, w3s_raw, t2s, t1s, w1s_raw):
-            nc.vector.memset(plane[:].bitcast(I32), 0)
-        warm = sb("warm", [P, 2], F32)
-        nc.vector.memset(warm[:, 0:1], 0.0)
-        nc.scalar.copy(out=warm[:, 1:2], in_=warm[:, 0:1])
-        nc.gpsimd.memset(g1s_hi[:].bitcast(I32), 0)
-
-        def load_scale_rows(queue, plane, first, src):
-            for q in range(4):
-                queue.dma_start(out=plane[32 * q + first : 32 * q + first + 4, :].bitcast(I32),
-                                in_=src[4 * q : 4 * q + 4, :].bitcast(I32))
-
-        def load_w2(b, first, last):
-            rows = w2.rearrange("(p j) c -> p j c", j=PACK)
-            nc.sync.dma_start(out=w2_raw[b][:, first:last, :], in_=rows[:, first:last, PASS * b : PASS * (b + 1)])
-
-        def words(src):
-            return src.rearrange("p t i -> p (t i)").bitcast(I32)
-
-        nc.sync.dma_start(idx3[:], offs3)
-        nc.sync.dma_start(out=t3w[:].bitcast(I32), in_=tab3_words[0].bitcast(I32))
-        nc.sync.dma_start(out=t2w[:].bitcast(I32), in_=words(tab2_words[0]))
-        nc.sync.dma_start(idx2[:], offs2)
-        nc.sync.dma_start(idx1[:], offs)
-        load_w2(0, 0, 2)
-        load_w2(0, 2, 4)
-        load_scale_rows(nc.sync, t3s, 0, tab3_scales[0])
-        nc.sync.dma_start(out=w3w_raw[:].bitcast(I32), in_=words(w3_words[0]))
-        load_w2(1, 0, 2)
-        load_scale_rows(nc.sync, w3s_raw, 0, w3_scales[0])
-        load_w2(1, 2, 4)
-        nc.sync.dma_start(out=t1w[0][:].bitcast(I32), in_=words(tab_words[0]))
-        load_scale_rows(nc.sync, t2s, 8, tab2_scales[0])
-        nc.sync.dma_start(out=w1w_raw[:].bitcast(I32).rearrange("p (a c) -> p a c", a=2),
-                          in_=w1_words.bitcast(I32).rearrange("a p c -> p a c"))
-        for q in range(4):
-            nc.sync.dma_start(out=t1s[32 * q : 32 * q + 8, :].bitcast(I32),
-                              in_=tab_scales[:, 4 * q : 4 * q + 4, :].bitcast(I32))
-        nc.sync.dma_start(out=t1w[1][:].bitcast(I32), in_=words(tab_words[1]))
-        for q in range(4):
-            nc.sync.dma_start(out=w1s_raw[32 * q : 32 * q + 4, :].bitcast(I32).rearrange("r (a c) -> r a c", a=2),
-                              in_=w1_scales[:, 4 * q : 4 * q + 4, :].bitcast(I32).rearrange("a r c -> r a c"))
-
-        def load_w4(b, tag):
-            raw = sb("w4_raw%d" % b, [P, PACK, N], F32, tag)
-            rows = w4[PASS * b : PASS * (b + 1), :].rearrange("(g t i) n -> t g i n", t=PACK, i=8)
-            for t in range(PACK):
-                nc.sync.dma_start(out=raw[:, t, :], in_=rows[t])
-            return raw
-
-        def pick(name, window, idx, dtype, tag=None):
-            got = sb(name, [P, S], dtype, tag)
-            nc.vector.tensor_copy(got[:], window[:].indirect(idx[:]))
-            return got
-
-        def reorder(name, raw, run, tag=None):
-            done = sb(name, list(raw.shape), U8, tag)
-            nc.vector.tensor_copy(
-                out=done[:].bitcast(I32).rearrange("p (u t g w) -> p u t g w", t=PACK, g=16, w=run),
-                in_=raw[:].bitcast(I32).rearrange("p (u g t w) -> p u t g w", t=PACK, g=16, w=run))
-            return done
-
-        def quantize(name, grouped, width, tag=None):
-            codes = sb(name + "_codes", [P, width], U32, tag)
-            scales = sb(name + "_scales", [P, width], U8)
-            nc.vector.quantize_mx(out=codes[:].bitcast(FP8X4), scales=scales[:], in_=grouped[:, :])
-            return codes, scales
-
-        def cast_w2(b, copy, tag=None):
-            grouped = sb("w2_bf%d" % b, [P, PACK * PASS], BF16, tag)
-            dst = grouped[:].rearrange("p (t g u v j) -> p t g u j v", t=PACK, g=16, u=2, v=4)
-            src = w2_raw[b][:].rearrange("p j (g t u v) -> p t g u j v", t=PACK, u=2, v=4)
-            for t in range(PACK):
-                copy(out=dst[:, t], in_=src[:, t])
-            return grouped
-
-        def cast_w4(b, first, count, copy):
-            grouped = sb("w4_bf%d%d" % (b, first), [P, PACK * P * count], BF16)
-            copy(out=grouped[:].rearrange("p (u v t) -> p u t v", v=4, t=PACK),
-                 in_=w4_raw[b][:, :, P * first : P * (first + count)].rearrange("p t (u v) -> p u t v", v=4))
-            return grouped
+        def sb(name, shape, dtype, offset=None):
+            if offset is None:
+                return keep.tile(shape, dtype, name=name, align_bytes=64)
+            return shared.tile(shape, dtype, name=name, align_bytes=64, offset=offset)
 
         def cols(first, count=P):
             return slice(first, first + count)
 
-        def interleaved(bank):
-            return bank[:].rearrange("p t j -> p j t")
+        def words(src):
+            return src.rearrange("p t i -> p (t i)").bitcast(I32)
 
-        def as_jt(ap):
-            return ap.rearrange("p (j t) -> p j t", t=PACK)
+        def load_float(name, rows, offset=None):
+            raw = sb(name, [P, PACK, PASS], F32, offset)
+            nc.sync.dma_start(out=raw[:], in_=rows.rearrange("(p i) c -> p i c", i=PACK))
+            return raw
 
-        def first_bank():
-            return psum.tile([P, PACK, JQ], F32, name="bank", tag="bank", bufs=8)
+        def load_words(name, src, width, dtype, offset=None):
+            raw = sb(name, [P, width], dtype, offset)
+            nc.sync.dma_start(out=raw[:].bitcast(I32), in_=src)
+            return raw
+
+        def load_list(name, src):
+            idx = sb(name, [P, S // 16], U16)
+            nc.sync.dma_start(idx[:], src)
+            return idx
+
+        def load_rows(tile, first, src):
+            passes, width = src.shape[0], src.shape[2]
+            nc.sync.dma_start(out=tile[P - passes * ROWS : P, cols(first, width)].bitcast(I32),
+                              in_=src.bitcast(I32).rearrange("a q c -> q a c"))
+
+        def pick(got, window, idx):
+            nc.vector.tensor_copy(got, window[:].indirect(idx[:]))
+
+        def move(dst, src):
+            nc.vector.tensor_copy(out=dst.bitcast(I32), in_=src.bitcast(I32))
+
+        def quantize(codes, scales, grouped):
+            nc.vector.quantize_mx(out=codes.bitcast(FP8X4), scales=scales, in_=grouped)
+
+        def round_rows(copy, grouped, raw, first, count):
+            copy(out=grouped[:, cols(PACK * first, PACK * count)].rearrange("p (u v i) -> p u i v", v=4, i=PACK),
+                 in_=raw[:, :, cols(first, count)].rearrange("p i (u v) -> p u i v", v=4))
+
+        def new_bank():
+            return psum.tile([P, PASS], F32, name="bank", tag="bank", bufs=8)
+
+        def paired(bank):
+            return bank[:].rearrange("j (p u e) -> j u p e", u=2, e=2)
+
+        def as_pairs(ap):
+            return ap.rearrange("j (u p e) -> j u p e", u=2, e=2)
 
         def evacuate(rounded, bank):
-            nc.scalar.copy(out=as_jt(rounded), in_=interleaved(bank))
+            nc.scalar.copy(out=as_pairs(rounded), in_=paired(bank))
 
-        def season_sum(jq, b):
-            bank = first_bank()
-            for t in range(PACK):
-                c = PASS * b + P * t
-                nc.tensor.matmul_mx(out=bank[:, t, :], lhsT=w3w[:, cols(4 * c, 4 * P)].bitcast(FP8X4),
-                                    lhsT_scale=w3s[:, cols(c)], rhs=g3w[:, cols(JQ * jq)].bitcast(FP4X4),
-                                    rhs_scale=g3s[:, cols(JQ * jq)], start=True, stop=True)
-            evacuate(season[b][:, cols(PASS * jq, PASS)], bank)
+        def combine(dst, bank, other, op):
+            nc.vector.tensor_tensor(as_pairs(dst), paired(bank), as_pairs(other), op)
 
-        def soil_sum(jq, b):
-            bank = first_bank()
-            codes, scales = w2q[b]
-            for t in range(PACK):
-                nc.tensor.matmul_mx(out=bank[:, t, :], lhsT=codes[:, cols(P * t)].bitcast(FP8X4),
-                                    lhsT_scale=scales[:, cols(P * t)], rhs=g2w[:, cols(JQ * jq)].bitcast(FP8X4),
-                                    rhs_scale=g2s[8:P, cols(JQ * jq)], start=True, stop=True)
-            evacuate(soil[b][:, cols(PASS * jq, PASS)], bank)
+        t3s = sb("t3s", [P, T2], U8)
+        t2s = sb("t2s", [P, T2], U8)
+        t1s = sb("t1s", [P, T], U8)
+        plane1 = sb("plane1", [P, 2 * S + H], U8)
+        plane2 = sb("plane2", [P, 2, S + H], U8)
+        stage1 = sb("stage1", [P, 2 * S + H], U8)
+        stage2 = sb("stage2", [P, S + H], U8)
+        nc.vector.memset(t3s[0 : P - ROWS, :].bitcast(I32), 0)
+        nc.vector.memset(t2s[0 : P - ROWS, :].bitcast(I32), 0)
+        nc.vector.memset(t1s[0:TOP, :].bitcast(I32), 0)
+        warm = sb("warm", [P, 2], F32)
+        nc.vector.memset(warm[:, 0:1], 0.0)
+        nc.scalar.copy(out=warm[:, 1:2], in_=warm[:, 0:1])
+        nc.gpsimd.memset(plane1[:].bitcast(I32), 0)
+        nc.gpsimd.memset(plane2[:].bitcast(I32), 0)
+        identity = sb("identity", [P, P], F32)
+        make_identity(nc, identity[:])
 
-        def seed_sum(jq, b):
-            bank = first_bank()
-            for a in range(2):
-                for t in range(PACK):
-                    c = H * a + PASS * b + P * t
-                    nc.tensor.matmul_mx(out=bank[:, t, :], lhsT=w1w[:, cols(2 * c, 2 * P)].bitcast(FP4X4),
-                                        lhsT_scale=w1s[:, cols(c)], rhs=g1w[a][:, cols(JQ * jq)].bitcast(FP8X4),
-                                        rhs_scale=g1s_planes[a][:, cols(JQ * jq)],
-                                        start=(a == 0 and t == 0), stop=(a == 1 and t == PACK - 1))
-            evacuate(seed[jq][:, cols(PASS * b, PASS)], bank)
+        idx3 = load_list("idx3", offs3)
+        load_rows(t3s, 0, tab3_scales)
+        idx2 = load_list("idx2", offs2)
+        load_rows(t2s, 0, tab2_scales)
+        load_rows(stage1, 2 * S, w3_scales)
+        w2_raw = [load_float("w2_raw0", w2[:, cols(0, PASS)], AT_C)]
+        t3w = load_words("t3w", tab3_words[0].bitcast(I32), T2, U16, AT_B)
+        idx1 = load_list("idx1", offs)
+        load_rows(stage2, S, w1_scales)
+        w3w = load_words("w3w", words(w3_words[0]), 4 * H, U8)
+        t2w = load_words("t2w", words(tab2_words[0]), T2, U32, AT_E)
+        load_rows(t1s, 0, tab_scales)
 
-        def output_passes(bank, c, b, codes, scales):
-            for jq in range(NJQ):
-                h_codes, h_scales = hq[jq]
-                nc.tensor.matmul_mx(out=bank[:, jq, :], lhsT=codes.bitcast(FP8X4), lhsT_scale=scales,
-                                    rhs=h_codes[:, cols(JQ * b)].bitcast(FP8X4), rhs_scale=h_scales[:, cols(JQ * b)],
-                                    start=(b == 0 and jq == 0), stop=(b == NB - 1 and jq == NJQ - 1))
-
-        season = [sb("season%d" % b, [P, NJQ * PASS], BF16) for b in range(NB)]
-        soil = [sb("soil%d" % b, [P, NJQ * PASS], BF16) for b in range(NB)]
-        seed = [sb("seed%d" % jq, [P, NB * PASS], BF16) for jq in range(NJQ)]
-
-        g3w = pick("g3w", t3w, idx3, U16)
-        g2w = pick("g2w", t2w, idx2, U32)
-        w2_bf0 = cast_w2(0, nc.scalar.copy)
-        g3s = pick("g3s", t3s, idx3, U8)
-        w3w = reorder("w3w", w3w_raw, 8)
-        w3s = reorder("w3s", w3s_raw, 2)
-        for b in range(NB):
-            for jq in range(NJQ):
-                season_sum(jq, b)
-
-        w2q = [quantize("w2q0", w2_bf0, PASS, "w3s_raw")]
-        w2q.append(quantize("w2q1", cast_w2(1, nc.vector.tensor_copy), PASS))
-        g1w = [pick("g1w0", t1w[0], idx1, U32)]
-        g2s = pick("g2s", t2s, idx2, U8)
-        g1s = pick("g1s", t1s, idx1, U8)
+        picked1 = sb("picked1", [P, 2 * S], U8, AT_A)
+        pick(picked1[:, cols(0, S)], t3s, idx3)
+        pick(picked1[:, cols(S, S)], t2s, idx2)
+        move(stage1[TOP:P, cols(0, 2 * S)], picked1[TOP:P, :])
         for q in range(4):
-            nc.sync.dma_start(out=g1s_hi[32 * q : 32 * q + 4, :].bitcast(I32),
-                              in_=g1s[32 * q + 4 : 32 * q + 8, :].bitcast(I32))
-        g1s_planes = [g1s, g1s_hi]
-        w4_raw = [load_w4(0, "t1s")]
-        w1w = reorder("w1w", w1w_raw, 4)
-        w1s = reorder("w1s", w1s_raw, 2)
-        g1w.append(pick("g1w1", t1w[1], idx1, U32, "w1s_raw"))
+            nc.sync.dma_start(out=plane1[cols(32 * q, 4), :].bitcast(I32),
+                              in_=stage1[cols(P - ROWS + 4 * q, 4), :].bitcast(I32))
+        g3s, g2s, w3s = plane1[:, cols(0, S)], plane1[:, cols(S, S)], plane1[:, cols(2 * S, H)]
+        w2_raw.append(load_float("w2_raw1", w2[:, cols(PASS, PASS)], AT_A + 512))
 
-        better = sb("better", [P, NB, NJQ * PASS], BF16, "t1w1")
-        for b in range(NB):
-            for jq in range(NJQ):
-                soil_sum(jq, b)
-            nc.vector.tensor_tensor(better[:, b, :], soil[b][:], season[b][:], ALU.max)
-        w4_raw.append(load_w4(1, "soil0"))
-        base_sb = sb("base_sb", [P, N // P, S], F32, "soil1")
-        nc.sync.dma_start(out=base_sb[:], in_=base.rearrange("(c p) j -> p c j", p=P))
+        g3w = sb("g3w", [P, S], U16, AT_A - 512)
+        pick(g3w[:], t3w, idx3)
+        t1w = [load_words("t1w0", words(tab_words[0]), T, U32, AT_B + 1024)]
 
-        def make_h(jq, dst):
-            for b in range(NB):
-                seed_sum(jq, b)
-            nc.vector.tensor_tensor(dst.rearrange("p (b c) -> p b c", b=NB),
-                                    seed[jq][:].rearrange("p (b c) -> p b c", b=NB),
-                                    better[:, :, cols(PASS * jq, PASS)], ALU.min)
+        w2_bf = [sb("w2_bf0", [P, PACK * PASS], BF16, AT_D), sb("w2_bf1", [P, PACK * PASS], BF16)]
+        w2_scales = sb("w2_scales", [P, H], U8)
+        w2_codes = [sb("w2_codes0", [P, PASS], U32)]
+        round_rows(nc.scalar.copy, w2_bf[0], w2_raw[0], 0, PASS)
+        w1w = sb("w1w", [P, 2, 2 * H], U8, AT_C)
+        nc.sync.dma_start(out=w1w[:].bitcast(I32), in_=w1_words.bitcast(I32).rearrange("a p c -> p a c"))
+        quantize(w2_codes[0][:], w2_scales[:, cols(0, PASS)], w2_bf[0][:])
 
-        w4q = {}
+        picked2 = sb("picked2", [P, S], U8, AT_D + 3584)
+        pick(picked2[:], t1s, idx1)
+        move(stage2[TOP:P, cols(0, S)], picked2[TOP:P, :])
+        for q in range(4):
+            nc.sync.dma_start(out=plane2[cols(32 * q, 4), :, :].bitcast(I32),
+                              in_=stage2[cols(TOP + 8 * q, 8), :].bitcast(I32))
+        t1w.append(load_words("t1w1", words(tab_words[1]), T, U32, AT_D + 3840))
+        g2w = sb("g2w", [P, S], U32, AT_D + 1792)
+        pick(g2w[:], t2w, idx2)
+        w4_raw = [load_float("w4_raw0", w4[cols(PASS, PASS), :], AT_E)]
 
-        def quantize_w4(b, first, count, grouped):
-            codes, scales = quantize("w4q%d%d" % (b, first), grouped, P * count)
-            for n in range(count):
-                w4q[b, first + n] = (codes[:, cols(P * n)], scales[:, cols(P * n)])
-
-        h_first = sb("h_first", [P, H], BF16)
-        make_h(0, h_first[:])
-        w4_early = cast_w4(0, 0, 2, nc.vector.tensor_copy)
-        hq = [quantize("hq0", h_first, NB * JQ)]
-        quantize_w4(0, 0, 2, w4_early)
-        h_rest = sb("h_rest", [P, (NJQ - 1) * H], BF16, "w4_bf00")
-        for jq in range(1, NJQ):
-            make_h(jq, h_rest[:, cols(H * (jq - 1), H)])
-            if jq > 1:
-                hq.append(quantize("hq%d" % (jq - 1), h_rest[:, cols(H * (jq - 2), H)], NB * JQ))
-        hq.append(quantize("hq%d" % (NJQ - 1), h_rest[:, cols(H * (NJQ - 2), H)], NB * JQ))
-
-        def output_sum(c):
-            if c == 2:
-                quantize_w4(0, 2, 2, cast_w4(0, 2, 2, nc.scalar.copy))
-            quantize_w4(1, c, 1, cast_w4(1, c, 1, nc.scalar.copy))
-            bank = first_bank()
-            for b in range(NB):
-                output_passes(bank, c, b, *w4q[b, c])
+        def season_sum(jt, b):
+            bank = new_bank()
+            nc.tensor.matmul_mx(out=bank[:], lhsT=g3w[:, cols(P * jt)].bitcast(FP4X4), lhsT_scale=g3s[:, cols(P * jt)],
+                                rhs=w3w[:, cols(4 * PASS * b, 4 * PASS)].bitcast(FP8X4),
+                                rhs_scale=w3s[:, cols(PASS * b, PASS)], start=True, stop=True)
             return bank
 
-        def finish(c, bank):
+        def soil_sum(jt, b):
+            bank = new_bank()
+            nc.tensor.matmul_mx(out=bank[:], lhsT=g2w[:, cols(P * jt)].bitcast(FP8X4), lhsT_scale=g2s[:, cols(P * jt)],
+                                rhs=w2_codes[b][:].bitcast(FP8X4), rhs_scale=w2_scales[:, cols(PASS * b, PASS)],
+                                start=True, stop=True)
+            return bank
+
+        def seed_pass(bank, a, jt, b):
+            nc.tensor.matmul_mx(out=bank[:], lhsT=g1w[a][:, cols(P * jt)].bitcast(FP8X4),
+                                lhsT_scale=plane2[:, a, cols(P * jt)],
+                                rhs=w1w[:, a, cols(2 * PASS * b, 2 * PASS)].bitcast(FP4X4),
+                                rhs_scale=plane2[:, a, cols(S + PASS * b, PASS)], start=(a == 0), stop=(a == 1))
+
+        def strip(tile, jt, count=1):
+            return tile[:, cols(PASS * jt, PASS * count)]
+
+        season = [sb("season0", [P, NJ * PASS], BF16)]
+        for jt in range(NJ):
+            evacuate(strip(season[0], jt), season_sum(jt, 0))
+        better0 = sb("better0", [P, NJ * PASS], BF16)
+        for jt in range(NJ):
+            combine(strip(better0, jt), soil_sum(jt, 0), strip(season[0], jt), ALU.max)
+        round_rows(nc.scalar.copy, w2_bf[1], w2_raw[1], 0, PASS)
+        season.append(sb("season1", [P, NJ * PASS], BF16, AT_A + 512))
+        for jt in range(NJ):
+            evacuate(strip(season[1], jt), season_sum(jt, 1))
+
+        g1w = [sb("g1w0", [P, S], U32)]
+        pick(g1w[0][:], t1w[0], idx1)
+        w4_raw.append(load_float("w4_raw1", w4[cols(0, PASS), :], AT_B + 3072))
+        w2_codes.append(sb("w2_codes1", [P, PASS], U32, AT_B + 1024))
+        quantize(w2_codes[1][:], w2_scales[:, cols(PASS, PASS)], w2_bf[1][:])
+
+        better1 = [sb("better10", [P, 2 * PASS], BF16)]
+        soil_banks = [soil_sum(jt, 1) for jt in range(NJ)]
+        for jt in range(2):
+            combine(strip(better1[0], jt), soil_banks[jt], strip(season[1], jt), ALU.max)
+        g1w.append(sb("g1w1", [P, S], U32))
+        pick(g1w[1][:], t1w[1], idx1)
+        base_sb = sb("base_sb", [P, N // P, S], F32, AT_D + 3840 + 4 * PASS)
+        nc.sync.dma_start(out=base_sb[:], in_=base.rearrange("(c p) j -> p c j", p=P))
+        better1.append(sb("better11", [P, 2 * PASS], BF16, AT_D + 3840))
+        for jt in range(2):
+            combine(strip(better1[1], jt), soil_banks[2 + jt], strip(season[1], 2 + jt), ALU.max)
+
+        seed_banks = {}
+        for b in (1, 0):
+            for jt in range(NJ):
+                seed_banks[b, jt] = new_bank()
+                seed_pass(seed_banks[b, jt], 0, jt, b)
+            for jt in range(NJ):
+                seed_pass(seed_banks[b, jt], 1, jt, b)
+
+        h_rows = [sb("h_rows%d" % b, [P, NJ * PASS], BF16) for b in range(NB)]
+        h = [sb("h%d" % b, [P, PACK * S], BF16) for b in range(NB)]
+        h_codes = sb("h_codes", [P, NB, S], U32)
+        h_scales = sb("h_scales", [P, NB, S], U8)
+        w4_bf = [sb("w4_bf%d" % b, [P, PACK * N], BF16) for b in range(NB)]
+        w4_codes = sb("w4_codes", [P, NB, N], U32)
+        w4_scales = sb("w4_scales", [P, NB, N], U8)
+
+        def turn(b, pair):
+            bank = new_bank()
+            for slot in range(4):
+                nc.tensor.transpose(bank[:, cols(P * slot)],
+                                    h_rows[b][:].bitcast(F32)[:, cols(PASS * pair + P * slot)], identity[:])
+            nc.scalar.copy(out=h[b][:].bitcast(F32)[:, cols(PASS * pair, PASS)].rearrange("p (a j u) -> p a j u", a=2, u=2),
+                           in_=bank[:].rearrange("p (a u j) -> p a j u", a=2, u=2))
+
+        def quantize_w4(b, first, count):
+            quantize(w4_codes[:, b, cols(P * first, P * count)], w4_scales[:, b, cols(P * first, P * count)],
+                     w4_bf[b][:, cols(PACK * P * first, PACK * P * count)])
+
+        def output_pass(c, b):
+            nc.tensor.matmul_mx(out=banks[c][:], lhsT=w4_codes[:, b, cols(P * c)].bitcast(FP8X4),
+                                lhsT_scale=w4_scales[:, b, cols(P * c)], rhs=h_codes[:, b, :].bitcast(FP8X4),
+                                rhs_scale=h_scales[:, b, :], start=(b == 1), stop=(b == 0))
+
+        seed1 = sb("seed1", [P, NJ * PASS], BF16)
+        for jt in range(NJ):
+            evacuate(strip(seed1, jt), seed_banks[1, jt])
+        for pair in range(2):
+            nc.vector.tensor_tensor(strip(h_rows[1], 2 * pair, 2), strip(seed1, 2 * pair, 2), better1[pair][:], ALU.min)
+            combine(strip(h_rows[0], pair), seed_banks[0, pair], strip(better0, pair), ALU.min)
+        round_rows(nc.scalar.copy, w4_bf[1], w4_raw[0], 0, 2 * P)
+        for pair in range(2):
+            turn(1, pair)
+        for jt in range(2, NJ):
+            combine(strip(h_rows[0], jt), seed_banks[0, jt], strip(better0, jt), ALU.min)
+        quantize(h_codes[:, 1, :], h_scales[:, 1, :], h[1][:])
+        for pair in range(2):
+            turn(0, pair)
+        round_rows(nc.scalar.copy, w4_bf[1], w4_raw[0], 2 * P, 2 * P)
+        banks = [new_bank() for c in range(N // P)]
+        quantize_w4(1, 0, 2)
+        output_pass(0, 1)
+        output_pass(1, 1)
+        round_rows(nc.vector.tensor_copy, w4_bf[0], w4_raw[1], 0, 2 * P)
+        quantize(h_codes[:, 0, :], h_scales[:, 0, :], h[0][:])
+        quantize_w4(0, 0, 2)
+        output_pass(0, 0)
+        output_pass(1, 0)
+        quantize_w4(1, 2, 2)
+        output_pass(2, 1)
+        output_pass(3, 1)
+
+        def finish(c):
             res = sb("res%d" % c, [P, S], F32)
-            nc.vector.tensor_tensor(res[:], bank[:].rearrange("p q j -> p (q j)"), base_sb[:, c, :], ALU.add)
+            nc.vector.tensor_tensor(res[:], banks[c][:], base_sb[:, c, :], ALU.add)
             nc.sync.dma_start(out=out[cols(P * c), :], in_=res[:])
 
-        banks = [output_sum(0)]
-        for c in range(1, N // P):
-            banks.append(output_sum(c))
-            finish(c - 1, banks[c - 1])
-        finish(N // P - 1, banks[N // P - 1])
+        for c in range(2, N // P):
+            round_rows(nc.scalar.copy, w4_bf[0], w4_raw[1], P * c, P)
+            finish(c - 2)
+            quantize_w4(0, c, 1)
+            output_pass(c, 0)
+        for c in range(2, N // P):
+            finish(c)

@@ -23,7 +23,7 @@ NJ = S // P
 NB = H // PASS
 ROWS = 16
 TOP = 96
-AT_A, AT_B, AT_C, AT_D, AT_E = 1024, 16384, 32768, 49152, 69632
+AT_A, AT_B, AT_C, AT_D, AT_E, AT_F = 1024, 18432, 32768, 49152, 69632, 81920
 
 
 def tile_list_maize_hybrid_placement_kernel(
@@ -76,12 +76,20 @@ def tile_list_maize_hybrid_placement_kernel(
         def quantize(codes, scales, grouped):
             nc.vector.quantize_mx(out=codes.bitcast(FP8X4), scales=scales, in_=grouped)
 
-        def round_rows(copy, grouped, raw, first, count):
-            copy(out=grouped[:, cols(PACK * first, PACK * count)].rearrange("p (u v i) -> p u i v", v=4, i=PACK),
-                 in_=raw[:, :, cols(first, count)].rearrange("p i (u v) -> p u i v", v=4))
+        def round_rows(grouped, raw, first=0, count=PASS):
+            nc.scalar.copy(
+                out=grouped[:, cols(PACK * first, PACK * count)].rearrange("p (u v i) -> p u i v", v=4, i=PACK),
+                in_=raw[:, :, cols(first, count)].rearrange("p i (u v) -> p u i v", v=4))
 
-        def new_bank():
-            return psum.tile([P, PASS], F32, name="bank", tag="bank", bufs=8)
+        def round_on_gpsimd(grouped, raw, count=PASS):
+            for first in range(0, count, P):
+                nc.gpsimd.tensor_scalar(
+                    out=grouped[:, cols(PACK * first, PACK * P)].rearrange("p (c i) -> p c i", i=PACK),
+                    in0=raw[:, :, cols(first)].rearrange("p i c -> p c i"),
+                    scalar1=1.0, scalar2=0.0, op0=ALU.mult, op1=ALU.add)
+
+        def new_bank(side):
+            return psum.tile([P, PASS], F32, name=side, tag=side, bufs=4)
 
         def paired(bank):
             return bank[:].rearrange("j (p u e) -> j u p e", u=2, e=2)
@@ -97,7 +105,7 @@ def tile_list_maize_hybrid_placement_kernel(
 
         t3s = sb("t3s", [P, T2], U8)
         t2s = sb("t2s", [P, T2], U8)
-        t1s = sb("t1s", [P, T], U8)
+        t1s = sb("t1s", [P, T], U8, AT_D)
         plane1 = sb("plane1", [P, 2 * S + H], U8)
         plane2 = sb("plane2", [P, 2, S + H], U8)
         stage1 = sb("stage1", [P, 2 * S + H], U8)
@@ -122,9 +130,9 @@ def tile_list_maize_hybrid_placement_kernel(
         t3w = load_words("t3w", tab3_words[0].bitcast(I32), T2, U16, AT_B)
         idx1 = load_list("idx1", offs)
         load_rows(stage2, S, w1_scales)
+        load_rows(t1s, 0, tab_scales)
         w3w = load_words("w3w", words(w3_words[0]), 4 * H, U8)
         t2w = load_words("t2w", words(tab2_words[0]), T2, U32, AT_E)
-        load_rows(t1s, 0, tab_scales)
 
         picked1 = sb("picked1", [P, 2 * S], U8, AT_A)
         pick(picked1[:, cols(0, S)], t3s, idx3)
@@ -140,34 +148,36 @@ def tile_list_maize_hybrid_placement_kernel(
         pick(g3w[:], t3w, idx3)
         t1w = [load_words("t1w0", words(tab_words[0]), T, U32, AT_B + 1024)]
 
-        w2_bf = [sb("w2_bf0", [P, PACK * PASS], BF16, AT_D), sb("w2_bf1", [P, PACK * PASS], BF16)]
+        w2_bf = [sb("w2_bf0", [P, PACK * PASS], BF16)]
         w2_scales = sb("w2_scales", [P, H], U8)
-        w2_codes = [sb("w2_codes0", [P, PASS], U32)]
-        round_rows(nc.scalar.copy, w2_bf[0], w2_raw[0], 0, PASS)
+        round_rows(w2_bf[0], w2_raw[0])
         w1w = sb("w1w", [P, 2, 2 * H], U8, AT_C)
         nc.sync.dma_start(out=w1w[:].bitcast(I32), in_=w1_words.bitcast(I32).rearrange("a p c -> p a c"))
-        quantize(w2_codes[0][:], w2_scales[:, cols(0, PASS)], w2_bf[0][:])
 
-        picked2 = sb("picked2", [P, S], U8, AT_D + 3584)
+        picked2 = sb("picked2", [P, S], U8, AT_B + 256)
         pick(picked2[:], t1s, idx1)
         move(stage2[TOP:P, cols(0, S)], picked2[TOP:P, :])
         for q in range(4):
             nc.sync.dma_start(out=plane2[cols(32 * q, 4), :, :].bitcast(I32),
                               in_=stage2[cols(TOP + 8 * q, 8), :].bitcast(I32))
-        t1w.append(load_words("t1w1", words(tab_words[1]), T, U32, AT_D + 3840))
-        g2w = sb("g2w", [P, S], U32, AT_D + 1792)
+        t1w.append(load_words("t1w1", words(tab_words[1]), T, U32, AT_B - 7424))
+        w2_codes = [sb("w2_codes0", [P, PASS], U32, AT_D), sb("w2_codes1", [P, PASS], U32)]
+        quantize(w2_codes[0][:], w2_scales[:, cols(0, PASS)], w2_bf[0][:])
+        g2w = sb("g2w", [P, S], U32)
         pick(g2w[:], t2w, idx2)
-        w4_raw = [load_float("w4_raw0", w4[cols(PASS, PASS), :], AT_E)]
+        w4_raw = [load_float("w4_raw0", w4[cols(0, PASS), :], AT_E + 2048)]
+        w2_bf.append(sb("w2_bf1", [P, PACK * PASS], BF16, AT_E - 2048))
+        round_on_gpsimd(w2_bf[1], w2_raw[1], 3 * P)
 
         def season_sum(jt, b):
-            bank = new_bank()
+            bank = new_bank("low")
             nc.tensor.matmul_mx(out=bank[:], lhsT=g3w[:, cols(P * jt)].bitcast(FP4X4), lhsT_scale=g3s[:, cols(P * jt)],
                                 rhs=w3w[:, cols(4 * PASS * b, 4 * PASS)].bitcast(FP8X4),
                                 rhs_scale=w3s[:, cols(PASS * b, PASS)], start=True, stop=True)
             return bank
 
         def soil_sum(jt, b):
-            bank = new_bank()
+            bank = new_bank("high")
             nc.tensor.matmul_mx(out=bank[:], lhsT=g2w[:, cols(P * jt)].bitcast(FP8X4), lhsT_scale=g2s[:, cols(P * jt)],
                                 rhs=w2_codes[b][:].bitcast(FP8X4), rhs_scale=w2_scales[:, cols(PASS * b, PASS)],
                                 start=True, stop=True)
@@ -185,102 +195,101 @@ def tile_list_maize_hybrid_placement_kernel(
         season = [sb("season0", [P, NJ * PASS], BF16)]
         for jt in range(NJ):
             evacuate(strip(season[0], jt), season_sum(jt, 0))
-        better0 = sb("better0", [P, NJ * PASS], BF16)
+        better0 = sb("better0", [P, NJ * PASS], BF16, AT_F + 4096)
         for jt in range(NJ):
             combine(strip(better0, jt), soil_sum(jt, 0), strip(season[0], jt), ALU.max)
-        round_rows(nc.scalar.copy, w2_bf[1], w2_raw[1], 0, PASS)
-        season.append(sb("season1", [P, NJ * PASS], BF16, AT_A + 512))
+        season.append(sb("season1", [P, NJ * PASS], BF16))
         for jt in range(NJ):
             evacuate(strip(season[1], jt), season_sum(jt, 1))
-
-        g1w = [sb("g1w0", [P, S], U32)]
-        pick(g1w[0][:], t1w[0], idx1)
-        w4_raw.append(load_float("w4_raw1", w4[cols(0, PASS), :], AT_B + 3072))
-        w2_codes.append(sb("w2_codes1", [P, PASS], U32, AT_B + 1024))
+        round_rows(w2_bf[1], w2_raw[1], 3 * P, P)
         quantize(w2_codes[1][:], w2_scales[:, cols(PASS, PASS)], w2_bf[1][:])
 
-        better1 = [sb("better10", [P, 2 * PASS], BF16)]
-        soil_banks = [soil_sum(jt, 1) for jt in range(NJ)]
-        for jt in range(2):
-            combine(strip(better1[0], jt), soil_banks[jt], strip(season[1], jt), ALU.max)
+        g1w = [sb("g1w0", [P, S], U32, AT_E - 2048)]
+        pick(g1w[0][:], t1w[0], idx1)
+        w4_raw.append(load_float("w4_raw1", w4[cols(PASS, PASS), :], AT_B + 3072))
+        soil1 = sb("soil1", [P, NJ * PASS], BF16)
+        for jt in range(NJ):
+            evacuate(strip(soil1, jt), soil_sum(jt, 1))
+        better1 = [sb("better10", [P, 2 * PASS], BF16, AT_B + 1024)]
+        nc.vector.tensor_tensor(better1[0][:], strip(soil1, 0, 2), strip(season[1], 0, 2), ALU.max)
         g1w.append(sb("g1w1", [P, S], U32))
         pick(g1w[1][:], t1w[1], idx1)
-        base_sb = sb("base_sb", [P, N // P, S], F32, AT_D + 3840 + 4 * PASS)
+        base_sb = sb("base_sb", [P, N // P, S], F32, AT_B - 13568)
         nc.sync.dma_start(out=base_sb[:], in_=base.rearrange("(c p) j -> p c j", p=P))
-        better1.append(sb("better11", [P, 2 * PASS], BF16, AT_D + 3840))
-        for jt in range(2):
-            combine(strip(better1[1], jt), soil_banks[2 + jt], strip(season[1], 2 + jt), ALU.max)
+        better1.append(sb("better11", [P, 2 * PASS], BF16, AT_B - 5376))
+        nc.vector.tensor_tensor(better1[1][:], strip(soil1, 2, 2), strip(season[1], 2, 2), ALU.max)
 
         seed_banks = {}
-        for b in (1, 0):
-            for jt in range(NJ):
-                seed_banks[b, jt] = new_bank()
-                seed_pass(seed_banks[b, jt], 0, jt, b)
-            for jt in range(NJ):
-                seed_pass(seed_banks[b, jt], 1, jt, b)
+        for b, jt in [(0, jt) for jt in range(NJ)] + [(1, 0), (1, 1)]:
+            seed_banks[b, jt] = new_bank("high" if b else "low")
+            seed_pass(seed_banks[b, jt], 0, jt, b)
+        for b, jt in [(0, 0), (1, 0), (0, 1), (1, 1), (0, 2), (0, 3)]:
+            seed_pass(seed_banks[b, jt], 1, jt, b)
 
-        h_rows = [sb("h_rows%d" % b, [P, NJ * PASS], BF16) for b in range(NB)]
+        h_rows = [sb("h_rows%d" % b, [P, NJ * PASS], BF16, AT_F + 4096 * b) for b in range(NB)]
         h = [sb("h%d" % b, [P, PACK * S], BF16) for b in range(NB)]
         h_codes = sb("h_codes", [P, NB, S], U32)
-        h_scales = sb("h_scales", [P, NB, S], U8)
-        w4_bf = [sb("w4_bf%d" % b, [P, PACK * N], BF16) for b in range(NB)]
         w4_codes = sb("w4_codes", [P, NB, N], U32)
-        w4_scales = sb("w4_scales", [P, NB, N], U8)
 
         def turn(b, pair):
-            bank = new_bank()
+            bank = new_bank("high")
             for slot in range(4):
                 nc.tensor.transpose(bank[:, cols(P * slot)],
                                     h_rows[b][:].bitcast(F32)[:, cols(PASS * pair + P * slot)], identity[:])
             nc.scalar.copy(out=h[b][:].bitcast(F32)[:, cols(PASS * pair, PASS)].rearrange("p (a j u) -> p a j u", a=2, u=2),
                            in_=bank[:].rearrange("p (a u j) -> p a j u", a=2, u=2))
 
-        def quantize_w4(b, first, count):
-            quantize(w4_codes[:, b, cols(P * first, P * count)], w4_scales[:, b, cols(P * first, P * count)],
-                     w4_bf[b][:, cols(PACK * P * first, PACK * P * count)])
+        def quantize_w4(b, first, count, grouped):
+            quantize(w4_codes[:, b, cols(P * first, P * count)], w4_scales[:, b, cols(P * first, P * count)], grouped[:])
+
+        def round_w4_tile(c, offset):
+            grouped = sb("w4_bf1%d" % c, [P, PACK * P], BF16, offset)
+            nc.scalar.copy(out=grouped[:].rearrange("p (u v i) -> p u i v", v=4, i=PACK),
+                           in_=w4_raw[1][:, :, cols(P * c)].rearrange("p i (u v) -> p u i v", v=4))
+            return grouped
 
         def output_pass(c, b):
             nc.tensor.matmul_mx(out=banks[c][:], lhsT=w4_codes[:, b, cols(P * c)].bitcast(FP8X4),
                                 lhsT_scale=w4_scales[:, b, cols(P * c)], rhs=h_codes[:, b, :].bitcast(FP8X4),
-                                rhs_scale=h_scales[:, b, :], start=(b == 1), stop=(b == 0))
+                                rhs_scale=h_scales[:, b, :], start=(b == 0), stop=(b == 1))
 
-        seed1 = sb("seed1", [P, NJ * PASS], BF16)
+        w4_bf0 = sb("w4_bf0", [P, PACK * N], BF16, AT_B - 3328)
+        round_on_gpsimd(w4_bf0, w4_raw[0])
         for jt in range(NJ):
-            evacuate(strip(seed1, jt), seed_banks[1, jt])
-        for pair in range(2):
-            nc.vector.tensor_tensor(strip(h_rows[1], 2 * pair, 2), strip(seed1, 2 * pair, 2), better1[pair][:], ALU.min)
-            combine(strip(h_rows[0], pair), seed_banks[0, pair], strip(better0, pair), ALU.min)
-        round_rows(nc.scalar.copy, w4_bf[1], w4_raw[0], 0, 2 * P)
-        for pair in range(2):
-            turn(1, pair)
-        for jt in range(2, NJ):
             combine(strip(h_rows[0], jt), seed_banks[0, jt], strip(better0, jt), ALU.min)
-        quantize(h_codes[:, 1, :], h_scales[:, 1, :], h[1][:])
+        seed1 = [sb("seed1%d" % pair, [P, 2 * PASS], BF16, AT_F + 12288 + 2048 * pair) for pair in range(2)]
+        for jt in range(NJ):
+            if jt > 1:
+                seed_banks[1, jt] = new_bank("low")
+                for a in range(2):
+                    seed_pass(seed_banks[1, jt], a, jt, 1)
+            evacuate(strip(seed1[jt // 2], jt % 2), seed_banks[1, jt])
         for pair in range(2):
             turn(0, pair)
-        round_rows(nc.scalar.copy, w4_bf[1], w4_raw[0], 2 * P, 2 * P)
-        banks = [new_bank() for c in range(N // P)]
-        quantize_w4(1, 0, 2)
-        output_pass(0, 1)
-        output_pass(1, 1)
-        round_rows(nc.vector.tensor_copy, w4_bf[0], w4_raw[1], 0, 2 * P)
+        w4_bf1 = [round_w4_tile(0, AT_F)]
+        for pair in range(2):
+            nc.vector.tensor_tensor(strip(h_rows[1], 2 * pair, 2), seed1[pair][:], better1[pair][:], ALU.min)
+        for pair in range(2):
+            turn(1, pair)
+        h_scales = sb("h_scales", [P, NB, S], U8, AT_F + 12288)
+        w4_scales = sb("w4_scales", [P, NB, N], U8, AT_F + 14336)
         quantize(h_codes[:, 0, :], h_scales[:, 0, :], h[0][:])
-        quantize_w4(0, 0, 2)
-        output_pass(0, 0)
-        output_pass(1, 0)
-        quantize_w4(1, 2, 2)
-        output_pass(2, 1)
-        output_pass(3, 1)
+        quantize_w4(0, 0, 4, w4_bf0)
+        banks = [new_bank("low") for c in range(N // P)]
+        for c in range(N // P):
+            output_pass(c, 0)
+        quantize_w4(1, 0, 1, w4_bf1[0])
+        quantize(h_codes[:, 1, :], h_scales[:, 1, :], h[1][:])
 
         def finish(c):
             res = sb("res%d" % c, [P, S], F32)
             nc.vector.tensor_tensor(res[:], banks[c][:], base_sb[:, c, :], ALU.add)
             nc.sync.dma_start(out=out[cols(P * c), :], in_=res[:])
 
-        for c in range(2, N // P):
-            round_rows(nc.scalar.copy, w4_bf[0], w4_raw[1], P * c, P)
-            finish(c - 2)
-            quantize_w4(0, c, 1)
-            output_pass(c, 0)
-        for c in range(2, N // P):
-            finish(c)
+        for c in range(N // P):
+            if c > 0:
+                quantize_w4(1, c, 1, round_w4_tile(c, AT_F + 4096 + 1024 * c))
+            output_pass(c, 1)
+            if c > 0:
+                finish(c - 1)
+        finish(N // P - 1)

@@ -113,9 +113,6 @@ def tile_list_maize_hybrid_placement_kernel(
         nc.vector.memset(t3s[0 : P - ROWS, :].bitcast(I32), 0)
         nc.vector.memset(t2s[0 : P - ROWS, :].bitcast(I32), 0)
         nc.vector.memset(t1s[0:TOP, :].bitcast(I32), 0)
-        warm = sb("warm", [P, 2], F32)
-        nc.vector.memset(warm[:, 0:1], 0.0)
-        nc.scalar.copy(out=warm[:, 1:2], in_=warm[:, 0:1])
         nc.gpsimd.memset(plane1[:].bitcast(I32), 0)
         nc.gpsimd.memset(plane2[:].bitcast(I32), 0)
         identity = sb("identity", [P, P], F32)
@@ -148,11 +145,10 @@ def tile_list_maize_hybrid_placement_kernel(
         pick(g3w[:], t3w, idx3)
         t1w = [load_words("t1w0", words(tab_words[0]), T, U32, AT_B + 1024)]
 
-        w2_bf = [sb("w2_bf0", [P, PACK * PASS], BF16)]
+        w2_bf = [sb("w2_bf0", [P, PACK * PASS], BF16, AT_D + 4096)]
         w2_scales = sb("w2_scales", [P, H], U8)
         round_rows(w2_bf[0], w2_raw[0])
-        w1w = sb("w1w", [P, 2, 2 * H], U8, AT_C)
-        nc.sync.dma_start(out=w1w[:].bitcast(I32), in_=w1_words.bitcast(I32).rearrange("a p c -> p a c"))
+        w1w = [load_words("w1w0", w1_words[0].bitcast(I32), 2 * H, U8, AT_C)]
 
         picked2 = sb("picked2", [P, S], U8, AT_B + 256)
         pick(picked2[:], t1s, idx1)
@@ -163,11 +159,12 @@ def tile_list_maize_hybrid_placement_kernel(
         t1w.append(load_words("t1w1", words(tab_words[1]), T, U32, AT_B - 7424))
         w2_codes = [sb("w2_codes0", [P, PASS], U32, AT_D), sb("w2_codes1", [P, PASS], U32)]
         quantize(w2_codes[0][:], w2_scales[:, cols(0, PASS)], w2_bf[0][:])
+        w1w.append(load_words("w1w1", w1_words[1].bitcast(I32), 2 * H, U8, AT_D + 4096))
         g2w = sb("g2w", [P, S], U32)
         pick(g2w[:], t2w, idx2)
         w4_raw = [load_float("w4_raw0", w4[cols(0, PASS), :], AT_E + 2048)]
         w2_bf.append(sb("w2_bf1", [P, PACK * PASS], BF16, AT_E - 2048))
-        round_on_gpsimd(w2_bf[1], w2_raw[1], 3 * P)
+        round_on_gpsimd(w2_bf[1], w2_raw[1], 2 * P)
 
         def season_sum(jt, b):
             bank = new_bank("low")
@@ -186,7 +183,7 @@ def tile_list_maize_hybrid_placement_kernel(
         def seed_pass(bank, a, jt, b):
             nc.tensor.matmul_mx(out=bank[:], lhsT=g1w[a][:, cols(P * jt)].bitcast(FP8X4),
                                 lhsT_scale=plane2[:, a, cols(P * jt)],
-                                rhs=w1w[:, a, cols(2 * PASS * b, 2 * PASS)].bitcast(FP4X4),
+                                rhs=w1w[a][:, cols(2 * PASS * b, 2 * PASS)].bitcast(FP4X4),
                                 rhs_scale=plane2[:, a, cols(S + PASS * b, PASS)], start=(a == 0), stop=(a == 1))
 
         def strip(tile, jt, count=1):
@@ -201,23 +198,23 @@ def tile_list_maize_hybrid_placement_kernel(
         season.append(sb("season1", [P, NJ * PASS], BF16))
         for jt in range(NJ):
             evacuate(strip(season[1], jt), season_sum(jt, 1))
-        round_rows(w2_bf[1], w2_raw[1], 3 * P, P)
+        round_rows(w2_bf[1], w2_raw[1], 2 * P, 2 * P)
         quantize(w2_codes[1][:], w2_scales[:, cols(PASS, PASS)], w2_bf[1][:])
 
         g1w = [sb("g1w0", [P, S], U32, AT_E - 2048)]
         pick(g1w[0][:], t1w[0], idx1)
-        w4_raw.append(load_float("w4_raw1", w4[cols(PASS, PASS), :], AT_B + 3072))
+        w4_raw.append(load_float("w4_raw1", w4[cols(PASS, PASS), :], AT_B + 1024))
         soil1 = sb("soil1", [P, NJ * PASS], BF16)
         for jt in range(NJ):
             evacuate(strip(soil1, jt), soil_sum(jt, 1))
-        better1 = [sb("better10", [P, 2 * PASS], BF16, AT_B + 1024)]
-        nc.vector.tensor_tensor(better1[0][:], strip(soil1, 0, 2), strip(season[1], 0, 2), ALU.max)
         g1w.append(sb("g1w1", [P, S], U32))
         pick(g1w[1][:], t1w[1], idx1)
-        base_sb = sb("base_sb", [P, N // P, S], F32, AT_B - 13568)
+        base_sb = sb("base_sb", [P, N // P, S], F32, AT_B - 15552)
         nc.sync.dma_start(out=base_sb[:], in_=base.rearrange("(c p) j -> p c j", p=P))
-        better1.append(sb("better11", [P, 2 * PASS], BF16, AT_B - 5376))
-        nc.vector.tensor_tensor(better1[1][:], strip(soil1, 2, 2), strip(season[1], 2, 2), ALU.max)
+        better1 = []
+        for pair in range(2):
+            better1.append(sb("better1%d" % pair, [P, 2 * PASS], BF16, AT_B - 7360 + 2048 * pair))
+            nc.vector.tensor_tensor(better1[pair][:], strip(soil1, 2 * pair, 2), strip(season[1], 2 * pair, 2), ALU.max)
 
         seed_banks = {}
         for b, jt in [(0, jt) for jt in range(NJ)] + [(1, 0), (1, 1)]:
@@ -253,7 +250,7 @@ def tile_list_maize_hybrid_placement_kernel(
                                 lhsT_scale=w4_scales[:, b, cols(P * c)], rhs=h_codes[:, b, :].bitcast(FP8X4),
                                 rhs_scale=h_scales[:, b, :], start=(b == 0), stop=(b == 1))
 
-        w4_bf0 = sb("w4_bf0", [P, PACK * N], BF16, AT_B - 3328)
+        w4_bf0 = sb("w4_bf0", [P, PACK * N], BF16, AT_B - 3264)
         round_on_gpsimd(w4_bf0, w4_raw[0])
         for jt in range(NJ):
             combine(strip(h_rows[0], jt), seed_banks[0, jt], strip(better0, jt), ALU.min)

@@ -164,7 +164,7 @@ def tile_list_maize_hybrid_placement_kernel(
         pick(g2w[:], t2w, idx2)
         w4_raw = [load_float("w4_raw0", w4[cols(0, PASS), :], AT_E + 2048)]
         w2_bf.append(sb("w2_bf1", [P, PACK * PASS], BF16, AT_E - 2048))
-        round_on_gpsimd(w2_bf[1], w2_raw[1], 2 * P)
+        round_on_gpsimd(w2_bf[1], w2_raw[1], 3 * P)
 
         def season_sum(jt, b):
             bank = new_bank("low")
@@ -198,13 +198,13 @@ def tile_list_maize_hybrid_placement_kernel(
         season.append(sb("season1", [P, NJ * PASS], BF16))
         for jt in range(NJ):
             evacuate(strip(season[1], jt), season_sum(jt, 1))
-        round_rows(w2_bf[1], w2_raw[1], 2 * P, 2 * P)
+        round_rows(w2_bf[1], w2_raw[1], 3 * P, P)
         quantize(w2_codes[1][:], w2_scales[:, cols(PASS, PASS)], w2_bf[1][:])
 
         g1w = [sb("g1w0", [P, S], U32, AT_E - 2048)]
         pick(g1w[0][:], t1w[0], idx1)
         w4_raw.append(load_float("w4_raw1", w4[cols(PASS, PASS), :], AT_B + 1024))
-        soil1 = sb("soil1", [P, NJ * PASS], BF16)
+        soil1 = sb("soil1", [P, NJ * PASS], BF16, AT_D + 8192)
         for jt in range(NJ):
             evacuate(strip(soil1, jt), soil_sum(jt, 1))
         g1w.append(sb("g1w1", [P, S], U32))
@@ -237,7 +237,7 @@ def tile_list_maize_hybrid_placement_kernel(
                            in_=bank[:].rearrange("p (a u j) -> p a j u", a=2, u=2))
 
         def quantize_w4(b, first, count, grouped):
-            quantize(w4_codes[:, b, cols(P * first, P * count)], w4_scales[:, b, cols(P * first, P * count)], grouped[:])
+            quantize(w4_codes[:, b, cols(P * first, P * count)], w4_scales[:, b, cols(P * first, P * count)], grouped[:, :])
 
         def round_w4_tile(c, offset):
             grouped = sb("w4_bf1%d" % c, [P, PACK * P], BF16, offset)
@@ -250,8 +250,8 @@ def tile_list_maize_hybrid_placement_kernel(
                                 lhsT_scale=w4_scales[:, b, cols(P * c)], rhs=h_codes[:, b, :].bitcast(FP8X4),
                                 rhs_scale=h_scales[:, b, :], start=(b == 0), stop=(b == 1))
 
-        w4_bf0 = sb("w4_bf0", [P, PACK * N], BF16, AT_B - 3264)
-        round_on_gpsimd(w4_bf0, w4_raw[0])
+        w4_bf0 = sb("w4_bf0", [P, PACK * 3 * P], BF16, AT_D + 8192)
+        round_on_gpsimd(w4_bf0, w4_raw[0], 3 * P)
         for jt in range(NJ):
             combine(strip(h_rows[0], jt), seed_banks[0, jt], strip(better0, jt), ALU.min)
         seed1 = [sb("seed1%d" % pair, [P, 2 * PASS], BF16, AT_F + 12288 + 2048 * pair) for pair in range(2)]
@@ -271,7 +271,12 @@ def tile_list_maize_hybrid_placement_kernel(
         h_scales = sb("h_scales", [P, NB, S], U8, AT_F + 12288)
         w4_scales = sb("w4_scales", [P, NB, N], U8, AT_F + 14336)
         quantize(h_codes[:, 0, :], h_scales[:, 0, :], h[0][:])
-        quantize_w4(0, 0, 4, w4_bf0)
+        w4_last = sb("w4_last", [P, PACK * P], BF16, AT_F + 15360)
+        nc.vector.tensor_copy(out=w4_last[:].rearrange("p (u v i) -> p u i v", v=4, i=PACK),
+                              in_=w4_raw[0][:, :, cols(3 * P)].rearrange("p i (u v) -> p u i v", v=4))
+        quantize_w4(0, 0, 2, w4_bf0[:, cols(0, 2 * PACK * P)])
+        quantize_w4(0, 2, 1, w4_bf0[:, cols(2 * PACK * P, PACK * P)])
+        quantize_w4(0, 3, 1, w4_last)
         banks = [new_bank("low") for c in range(N // P)]
         for c in range(N // P):
             output_pass(c, 0)

@@ -23,7 +23,7 @@ NJ = S // P
 NB = H // PASS
 ROWS = 16
 TOP = 96
-AT_A, AT_B, AT_C, AT_D, AT_E, AT_F = 1024, 18432, 32768, 49152, 69632, 81920
+AT_A, AT_B, AT_C, AT_D, AT_E, AT_F = 1024, 18432, 32768, 49152, 86016, 98304
 
 
 def tile_list_maize_hybrid_placement_kernel(
@@ -123,7 +123,7 @@ def tile_list_maize_hybrid_placement_kernel(
         idx2 = load_list("idx2", offs2)
         load_rows(t2s, 0, tab2_scales)
         load_rows(stage1, 2 * S, w3_scales)
-        w2_raw = [load_float("w2_raw0", w2[:, cols(0, PASS)], AT_C)]
+        w2_raw = [load_float("w2_raw0", w2[:, cols(0, PASS)])]
         t3w = load_words("t3w", tab3_words[0].bitcast(I32), T2, U16, AT_B)
         idx1 = load_list("idx1", offs)
         load_rows(stage2, S, w1_scales)
@@ -135,9 +135,8 @@ def tile_list_maize_hybrid_placement_kernel(
         pick(picked1[:, cols(0, S)], t3s, idx3)
         pick(picked1[:, cols(S, S)], t2s, idx2)
         move(stage1[TOP:P, cols(0, 2 * S)], picked1[TOP:P, :])
-        for q in range(4):
-            nc.sync.dma_start(out=plane1[cols(32 * q, 4), :].bitcast(I32),
-                              in_=stage1[cols(P - ROWS + 4 * q, 4), :].bitcast(I32))
+        for r in range(4):
+            nc.sync.dma_start(out=plane1[r:P:32, :].bitcast(I32), in_=stage1[P - ROWS + r : P : 4, :].bitcast(I32))
         g3s, g2s, w3s = plane1[:, cols(0, S)], plane1[:, cols(S, S)], plane1[:, cols(2 * S, H)]
         w2_raw.append(load_float("w2_raw1", w2[:, cols(PASS, PASS)], AT_A + 512))
 
@@ -145,25 +144,23 @@ def tile_list_maize_hybrid_placement_kernel(
         pick(g3w[:], t3w, idx3)
         t1w = [load_words("t1w0", words(tab_words[0]), T, U32, AT_B + 1024)]
 
-        w2_bf = [sb("w2_bf0", [P, PACK * PASS], BF16, AT_D + 4096)]
+        w2_bf = [sb("w2_bf0", [P, PACK * PASS], BF16)]
         w2_scales = sb("w2_scales", [P, H], U8)
         round_rows(w2_bf[0], w2_raw[0])
-        w1w = [load_words("w1w0", w1_words[0].bitcast(I32), 2 * H, U8, AT_C)]
 
         picked2 = sb("picked2", [P, S], U8, AT_B + 256)
         pick(picked2[:], t1s, idx1)
+        w2_codes = [sb("w2_codes0", [P, PASS], U32, AT_D), sb("w2_codes1", [P, PASS], U32)]
+        quantize(w2_codes[0][:], w2_scales[:, cols(0, PASS)], w2_bf[0][:])
         move(stage2[TOP:P, cols(0, S)], picked2[TOP:P, :])
         for q in range(4):
             nc.sync.dma_start(out=plane2[cols(32 * q, 4), :, :].bitcast(I32),
                               in_=stage2[cols(TOP + 8 * q, 8), :].bitcast(I32))
         t1w.append(load_words("t1w1", words(tab_words[1]), T, U32, AT_B - 7424))
-        w2_codes = [sb("w2_codes0", [P, PASS], U32, AT_D), sb("w2_codes1", [P, PASS], U32)]
-        quantize(w2_codes[0][:], w2_scales[:, cols(0, PASS)], w2_bf[0][:])
-        w1w.append(load_words("w1w1", w1_words[1].bitcast(I32), 2 * H, U8, AT_D + 4096))
         g2w = sb("g2w", [P, S], U32)
         pick(g2w[:], t2w, idx2)
-        w4_raw = [load_float("w4_raw0", w4[cols(0, PASS), :], AT_E + 2048)]
-        w2_bf.append(sb("w2_bf1", [P, PACK * PASS], BF16, AT_E - 2048))
+        w1w = [load_words("w1w%d" % a, w1_words[a].bitcast(I32), 2 * H, U8, AT_E + 64 + 2 * H * a) for a in range(2)]
+        w2_bf.append(sb("w2_bf1", [P, PACK * PASS], BF16, AT_E - 4032))
         round_on_gpsimd(w2_bf[1], w2_raw[1], 3 * P)
 
         def season_sum(jt, b):
@@ -189,19 +186,20 @@ def tile_list_maize_hybrid_placement_kernel(
         def strip(tile, jt, count=1):
             return tile[:, cols(PASS * jt, PASS * count)]
 
-        season = [sb("season0", [P, NJ * PASS], BF16)]
+        season = [sb("season0", [P, NJ * PASS], BF16, AT_C)]
         for jt in range(NJ):
             evacuate(strip(season[0], jt), season_sum(jt, 0))
         better0 = sb("better0", [P, NJ * PASS], BF16, AT_F + 4096)
         for jt in range(NJ):
             combine(strip(better0, jt), soil_sum(jt, 0), strip(season[0], jt), ALU.max)
+        w4_raw = [load_float("w4_raw0", w4[cols(0, PASS), :], AT_C)]
         season.append(sb("season1", [P, NJ * PASS], BF16))
         for jt in range(NJ):
             evacuate(strip(season[1], jt), season_sum(jt, 1))
         round_rows(w2_bf[1], w2_raw[1], 3 * P, P)
         quantize(w2_codes[1][:], w2_scales[:, cols(PASS, PASS)], w2_bf[1][:])
 
-        g1w = [sb("g1w0", [P, S], U32, AT_E - 2048)]
+        g1w = [sb("g1w0", [P, S], U32, AT_E - 4032)]
         pick(g1w[0][:], t1w[0], idx1)
         w4_raw.append(load_float("w4_raw1", w4[cols(PASS, PASS), :], AT_B + 1024))
         soil1 = sb("soil1", [P, NJ * PASS], BF16, AT_D + 8192)
@@ -239,10 +237,10 @@ def tile_list_maize_hybrid_placement_kernel(
         def quantize_w4(b, first, count, grouped):
             quantize(w4_codes[:, b, cols(P * first, P * count)], w4_scales[:, b, cols(P * first, P * count)], grouped[:, :])
 
-        def round_w4_tile(c, offset):
-            grouped = sb("w4_bf1%d" % c, [P, PACK * P], BF16, offset)
+        def round_w4_tile(b, c, offset):
+            grouped = sb("w4_bf%d%d" % (b, c), [P, PACK * P], BF16, offset)
             nc.scalar.copy(out=grouped[:].rearrange("p (u v i) -> p u i v", v=4, i=PACK),
-                           in_=w4_raw[1][:, :, cols(P * c)].rearrange("p i (u v) -> p u i v", v=4))
+                           in_=w4_raw[b][:, :, cols(P * c)].rearrange("p i (u v) -> p u i v", v=4))
             return grouped
 
         def output_pass(c, b):
@@ -250,8 +248,8 @@ def tile_list_maize_hybrid_placement_kernel(
                                 lhsT_scale=w4_scales[:, b, cols(P * c)], rhs=h_codes[:, b, :].bitcast(FP8X4),
                                 rhs_scale=h_scales[:, b, :], start=(b == 0), stop=(b == 1))
 
-        w4_bf0 = sb("w4_bf0", [P, PACK * 3 * P], BF16, AT_D + 8192)
-        round_on_gpsimd(w4_bf0, w4_raw[0], 3 * P)
+        w4_bf0 = sb("w4_bf0", [P, PACK * 2 * P], BF16, AT_D + 8192)
+        round_on_gpsimd(w4_bf0, w4_raw[0], 2 * P)
         for jt in range(NJ):
             combine(strip(h_rows[0], jt), seed_banks[0, jt], strip(better0, jt), ALU.min)
         seed1 = [sb("seed1%d" % pair, [P, 2 * PASS], BF16, AT_F + 12288 + 2048 * pair) for pair in range(2)]
@@ -263,7 +261,7 @@ def tile_list_maize_hybrid_placement_kernel(
             evacuate(strip(seed1[jt // 2], jt % 2), seed_banks[1, jt])
         for pair in range(2):
             turn(0, pair)
-        w4_bf1 = [round_w4_tile(0, AT_F)]
+        w4_third = round_w4_tile(0, 2, AT_F)
         for pair in range(2):
             nc.vector.tensor_tensor(strip(h_rows[1], 2 * pair, 2), seed1[pair][:], better1[pair][:], ALU.min)
         for pair in range(2):
@@ -274,13 +272,12 @@ def tile_list_maize_hybrid_placement_kernel(
         w4_last = sb("w4_last", [P, PACK * P], BF16, AT_F + 15360)
         nc.vector.tensor_copy(out=w4_last[:].rearrange("p (u v i) -> p u i v", v=4, i=PACK),
                               in_=w4_raw[0][:, :, cols(3 * P)].rearrange("p i (u v) -> p u i v", v=4))
-        quantize_w4(0, 0, 2, w4_bf0[:, cols(0, 2 * PACK * P)])
-        quantize_w4(0, 2, 1, w4_bf0[:, cols(2 * PACK * P, PACK * P)])
+        quantize_w4(0, 0, 2, w4_bf0)
+        quantize_w4(0, 2, 1, w4_third)
         quantize_w4(0, 3, 1, w4_last)
         banks = [new_bank("low") for c in range(N // P)]
         for c in range(N // P):
             output_pass(c, 0)
-        quantize_w4(1, 0, 1, w4_bf1[0])
         quantize(h_codes[:, 1, :], h_scales[:, 1, :], h[1][:])
 
         def finish(c):
@@ -289,8 +286,7 @@ def tile_list_maize_hybrid_placement_kernel(
             nc.sync.dma_start(out=out[cols(P * c), :], in_=res[:])
 
         for c in range(N // P):
-            if c > 0:
-                quantize_w4(1, c, 1, round_w4_tile(c, AT_F + 4096 + 1024 * c))
+            quantize_w4(1, c, 1, round_w4_tile(1, c, AT_F + 4096 + 1024 * c))
             output_pass(c, 1)
             if c > 0:
                 finish(c - 1)

@@ -15,15 +15,17 @@ U8 = mybir.dt.uint8
 FP8X4 = mybir.dt.float8_e4m3fn_x4
 FP4X4 = mybir.dt.float4_e2m1fn_x4
 ALU = mybir.AluOpType
+BYTES_OF = {F32: 4, BF16: 2, U32: 4, U16: 2, U8: 1}
 
 P = 128
 PACK = 4
 PASS = 512
 NJ = S // P
-NB = H // PASS
 ROWS = 16
 TOP = 96
-AT_A, AT_B, AT_C, AT_D, AT_E, AT_F = 1024, 18432, 32768, 49152, 86016, 98304
+BANK = 2048
+LAP = 64
+KIB = 1024
 
 
 def tile_list_maize_hybrid_placement_kernel(
@@ -35,11 +37,27 @@ def tile_list_maize_hybrid_placement_kernel(
         keep = ctx.enter_context(tc.tile_pool(name="keep", bufs=1))
         shared = ctx.enter_context(tc.tile_pool(name="shared", bufs=1))
         psum = ctx.enter_context(tc.psum_pool(name="psum", bufs=1))
+        span = {}
+        banks_made = []
 
-        def sb(name, shape, dtype, offset=None):
-            if offset is None:
+        def sb(name, shape, dtype, at=None, on=None, above=None, below=None):
+            size = BYTES_OF[dtype]
+            for extent in shape[1:]:
+                size = size * extent
+            if on is not None:
+                at = span[on[0]][0] + on[1]
+            if above is not None:
+                at = span[above][1] - LAP
+            if below is not None:
+                at = span[below][0] + LAP - size
+            if at is None:
                 return keep.tile(shape, dtype, name=name, align_bytes=64)
-            return shared.tile(shape, dtype, name=name, align_bytes=64, offset=offset)
+            span[name] = (at, at + size)
+            return shared.tile(shape, dtype, name=name, align_bytes=64, offset=at)
+
+        def bank_at(number):
+            banks_made.append(number)
+            return psum.tile([P, PASS], F32, name="bank%d" % len(banks_made), offset=BANK * number)
 
         def cols(first, count=P):
             return slice(first, first + count)
@@ -47,13 +65,13 @@ def tile_list_maize_hybrid_placement_kernel(
         def words(src):
             return src.rearrange("p t i -> p (t i)").bitcast(I32)
 
-        def load_float(name, rows, offset=None):
-            raw = sb(name, [P, PACK, PASS], F32, offset)
+        def load_float(name, rows, **place):
+            raw = sb(name, [P, PACK, PASS], F32, **place)
             nc.sync.dma_start(out=raw[:], in_=rows.rearrange("(p i) c -> p i c", i=PACK))
             return raw
 
-        def load_words(name, src, width, dtype, offset=None):
-            raw = sb(name, [P, width], dtype, offset)
+        def load_words(name, src, width, dtype, **place):
+            raw = sb(name, [P, width], dtype, **place)
             nc.sync.dma_start(out=raw[:].bitcast(I32), in_=src)
             return raw
 
@@ -76,20 +94,13 @@ def tile_list_maize_hybrid_placement_kernel(
         def quantize(codes, scales, grouped):
             nc.vector.quantize_mx(out=codes.bitcast(FP8X4), scales=scales, in_=grouped)
 
-        def round_rows(grouped, raw, first=0, count=PASS):
-            nc.scalar.copy(
-                out=grouped[:, cols(PACK * first, PACK * count)].rearrange("p (u v i) -> p u i v", v=4, i=PACK),
-                in_=raw[:, :, cols(first, count)].rearrange("p i (u v) -> p u i v", v=4))
+        def round_on_scalar(grouped, raw):
+            nc.scalar.copy(out=grouped.rearrange("p (u v i) -> p u i v", v=4, i=PACK),
+                           in_=raw.rearrange("p i (u v) -> p u i v", v=4))
 
-        def round_on_gpsimd(grouped, raw, count=PASS):
-            for first in range(0, count, P):
-                nc.gpsimd.tensor_scalar(
-                    out=grouped[:, cols(PACK * first, PACK * P)].rearrange("p (c i) -> p c i", i=PACK),
-                    in0=raw[:, :, cols(first)].rearrange("p i c -> p c i"),
-                    scalar1=1.0, scalar2=0.0, op0=ALU.mult, op1=ALU.add)
-
-        def new_bank(side):
-            return psum.tile([P, PASS], F32, name=side, tag=side, bufs=4)
+        def round_on_gpsimd(grouped, raw):
+            nc.gpsimd.tensor_scalar(out=grouped.rearrange("p (c i) -> p c i", i=PACK), in0=raw.rearrange("p i c -> p c i"),
+                                    scalar1=1.0, scalar2=0.0, op0=ALU.mult, op1=ALU.add)
 
         def paired(bank):
             return bank[:].rearrange("j (p u e) -> j u p e", u=2, e=2)
@@ -97,15 +108,35 @@ def tile_list_maize_hybrid_placement_kernel(
         def as_pairs(ap):
             return ap.rearrange("j (u p e) -> j u p e", u=2, e=2)
 
+        def strip(tile, jt, count=1):
+            return tile[:, cols(PASS * jt, PASS * count)]
+
         def evacuate(rounded, bank):
             nc.scalar.copy(out=as_pairs(rounded), in_=paired(bank))
 
         def combine(dst, bank, other, op):
             nc.vector.tensor_tensor(as_pairs(dst), paired(bank), as_pairs(other), op)
 
+        def turn(rows, pair, number):
+            bank = bank_at(number)
+            for u in range(2):
+                for a in range(2):
+                    nc.tensor.transpose(bank[:, cols(P * (2 * u + a))],
+                                        rows[:].bitcast(F32)[:, cols(P * (4 * pair + 2 * a + u))], identity[:])
+            return bank
+
+        def copy_turned(dst, bank):
+            nc.scalar.copy(out=dst.bitcast(F32).rearrange("p (x u) -> p x u", u=2),
+                           in_=bank[:].rearrange("p (u x) -> p x u", u=2))
+
+        def combine_turned(dst, bank, other, op):
+            nc.vector.tensor_tensor(dst.rearrange("p (x u e) -> p x u e", u=2, e=2),
+                                    bank[:].bitcast(BF16).rearrange("p (u x e) -> p x u e", u=2, e=2),
+                                    other.rearrange("p (x u e) -> p x u e", u=2, e=2), op)
+
         t3s = sb("t3s", [P, T2], U8)
         t2s = sb("t2s", [P, T2], U8)
-        t1s = sb("t1s", [P, T], U8, AT_D)
+        t1s = sb("t1s", [P, T], U8, at=56 * KIB)
         plane1 = sb("plane1", [P, 2 * S + H], U8)
         plane2 = sb("plane2", [P, 2, S + H], U8)
         stage1 = sb("stage1", [P, 2 * S + H], U8)
@@ -124,169 +155,155 @@ def tile_list_maize_hybrid_placement_kernel(
         load_rows(t2s, 0, tab2_scales)
         load_rows(stage1, 2 * S, w3_scales)
         w2_raw = [load_float("w2_raw0", w2[:, cols(0, PASS)])]
-        t3w = load_words("t3w", tab3_words[0].bitcast(I32), T2, U16, AT_B)
+        t3w = load_words("t3w", tab3_words[0].bitcast(I32), T2, U16, at=26 * KIB)
         idx1 = load_list("idx1", offs)
-        load_rows(stage2, S, w1_scales)
         load_rows(t1s, 0, tab_scales)
+        t2w = load_words("t2w", words(tab2_words[0]), T2, U32, at=64 * KIB)
         w3w = load_words("w3w", words(w3_words[0]), 4 * H, U8)
-        t2w = load_words("t2w", words(tab2_words[0]), T2, U32, AT_E)
+        load_rows(stage2, S, w1_scales)
 
-        picked1 = sb("picked1", [P, 2 * S], U8, AT_A)
-        pick(picked1[:, cols(0, S)], t3s, idx3)
-        pick(picked1[:, cols(S, S)], t2s, idx2)
-        move(stage1[TOP:P, cols(0, 2 * S)], picked1[TOP:P, :])
+        picked23 = sb("picked23", [P, 2 * S], U8, at=1 * KIB)
+        pick(picked23[:, cols(0, S)], t3s, idx3)
+        pick(picked23[:, cols(S, S)], t2s, idx2)
+        move(stage1[TOP:P, cols(0, 2 * S)], picked23[TOP:P, :])
         for r in range(4):
             nc.sync.dma_start(out=plane1[r:P:32, :].bitcast(I32), in_=stage1[P - ROWS + r : P : 4, :].bitcast(I32))
         g3s, g2s, w3s = plane1[:, cols(0, S)], plane1[:, cols(S, S)], plane1[:, cols(2 * S, H)]
-        w2_raw.append(load_float("w2_raw1", w2[:, cols(PASS, PASS)], AT_A + 512))
+        w2_raw.append(load_float("w2_raw1", w2[:, cols(PASS, PASS)], above="picked23"))
 
-        g3w = sb("g3w", [P, S], U16, AT_A - 512)
+        g3w = sb("g3w", [P, S], U16, below="picked23")
         pick(g3w[:], t3w, idx3)
-        t1w = [load_words("t1w0", words(tab_words[0]), T, U32, AT_B + 1024)]
+        t1w = [load_words("t1w0", words(tab_words[0]), T, U32, above="t3w")]
 
-        w2_bf = [sb("w2_bf0", [P, PACK * PASS], BF16)]
-        w2_scales = sb("w2_scales", [P, H], U8)
-        round_rows(w2_bf[0], w2_raw[0])
+        w2_bf = [sb("w2_bf0", [P, PACK * PASS], BF16, at=52 * KIB)]
+        round_on_scalar(w2_bf[0][:], w2_raw[0][:])
 
-        picked2 = sb("picked2", [P, S], U8, AT_B + 256)
-        pick(picked2[:], t1s, idx1)
-        w2_codes = [sb("w2_codes0", [P, PASS], U32, AT_D), sb("w2_codes1", [P, PASS], U32)]
-        quantize(w2_codes[0][:], w2_scales[:, cols(0, PASS)], w2_bf[0][:])
-        move(stage2[TOP:P, cols(0, S)], picked2[TOP:P, :])
+        picked1 = sb("picked1", [P, S], U8, at=50 * KIB)
+        pick(picked1[:], t1s, idx1)
+        w2_codes = [sb("w2_codes0", [P, PASS], U32, on=("t1s", 0)), sb("w2_codes1", [P, PASS], U32, at=16 * KIB)]
+        w2_scales = [sb("w2_scales0", [P, PASS], U8)]
+        quantize(w2_codes[0][:], w2_scales[0][:], w2_bf[0][:])
+        move(stage2[TOP:P, cols(0, S)], picked1[TOP:P, :])
         for q in range(4):
             nc.sync.dma_start(out=plane2[cols(32 * q, 4), :, :].bitcast(I32),
                               in_=stage2[cols(TOP + 8 * q, 8), :].bitcast(I32))
-        t1w.append(load_words("t1w1", words(tab_words[1]), T, U32, AT_B - 7424))
+        t1w.append(load_words("t1w1", words(tab_words[1]), T, U32, below="picked1"))
         g2w = sb("g2w", [P, S], U32)
         pick(g2w[:], t2w, idx2)
-        w1w = [load_words("w1w%d" % a, w1_words[a].bitcast(I32), 2 * H, U8, AT_E + 64 + 2 * H * a) for a in range(2)]
-        w2_bf.append(sb("w2_bf1", [P, PACK * PASS], BF16, AT_E - 4032))
-        round_on_gpsimd(w2_bf[1], w2_raw[1], 3 * P)
+        w2_bf.append(sb("w2_bf1", [P, PACK * PASS], BF16, on=("w2_bf0", 0)))
+        for c in range(4):
+            round_on_gpsimd(strip(w2_bf[1], c), w2_raw[1][:, :, cols(P * c)])
 
-        def season_sum(jt, b):
-            bank = new_bank("low")
+        def season_sum(jt, b, number):
+            bank = bank_at(number)
             nc.tensor.matmul_mx(out=bank[:], lhsT=g3w[:, cols(P * jt)].bitcast(FP4X4), lhsT_scale=g3s[:, cols(P * jt)],
                                 rhs=w3w[:, cols(4 * PASS * b, 4 * PASS)].bitcast(FP8X4),
                                 rhs_scale=w3s[:, cols(PASS * b, PASS)], start=True, stop=True)
             return bank
 
-        def soil_sum(jt, b):
-            bank = new_bank("high")
+        def soil_sum(jt, b, number):
+            bank = bank_at(number)
             nc.tensor.matmul_mx(out=bank[:], lhsT=g2w[:, cols(P * jt)].bitcast(FP8X4), lhsT_scale=g2s[:, cols(P * jt)],
-                                rhs=w2_codes[b][:].bitcast(FP8X4), rhs_scale=w2_scales[:, cols(PASS * b, PASS)],
-                                start=True, stop=True)
+                                rhs=w2_codes[b][:].bitcast(FP8X4), rhs_scale=w2_scales[b][:], start=True, stop=True)
             return bank
 
         def seed_pass(bank, a, jt, b):
+            opening = b
             nc.tensor.matmul_mx(out=bank[:], lhsT=g1w[a][:, cols(P * jt)].bitcast(FP8X4),
                                 lhsT_scale=plane2[:, a, cols(P * jt)],
                                 rhs=w1w[a][:, cols(2 * PASS * b, 2 * PASS)].bitcast(FP4X4),
-                                rhs_scale=plane2[:, a, cols(S + PASS * b, PASS)], start=(a == 0), stop=(a == 1))
+                                rhs_scale=plane2[:, a, cols(S + PASS * b, PASS)], start=(a == opening), stop=(a != opening))
 
-        def strip(tile, jt, count=1):
-            return tile[:, cols(PASS * jt, PASS * count)]
-
-        season = [sb("season0", [P, NJ * PASS], BF16, AT_C)]
-        for jt in range(NJ):
-            evacuate(strip(season[0], jt), season_sum(jt, 0))
-        better0 = sb("better0", [P, NJ * PASS], BF16, AT_F + 4096)
-        for jt in range(NJ):
-            combine(strip(better0, jt), soil_sum(jt, 0), strip(season[0], jt), ALU.max)
-        w4_raw = [load_float("w4_raw0", w4[cols(0, PASS), :], AT_C)]
-        season.append(sb("season1", [P, NJ * PASS], BF16))
-        for jt in range(NJ):
-            evacuate(strip(season[1], jt), season_sum(jt, 1))
-        round_rows(w2_bf[1], w2_raw[1], 3 * P, P)
-        quantize(w2_codes[1][:], w2_scales[:, cols(PASS, PASS)], w2_bf[1][:])
-
-        g1w = [sb("g1w0", [P, S], U32, AT_E - 4032)]
-        pick(g1w[0][:], t1w[0], idx1)
-        w4_raw.append(load_float("w4_raw1", w4[cols(PASS, PASS), :], AT_B + 1024))
-        soil1 = sb("soil1", [P, NJ * PASS], BF16, AT_D + 8192)
-        for jt in range(NJ):
-            evacuate(strip(soil1, jt), soil_sum(jt, 1))
-        g1w.append(sb("g1w1", [P, S], U32))
-        pick(g1w[1][:], t1w[1], idx1)
-        base_sb = sb("base_sb", [P, N // P, S], F32, AT_B - 15552)
-        nc.sync.dma_start(out=base_sb[:], in_=base.rearrange("(c p) j -> p c j", p=P))
-        better1 = []
+        season0 = [sb("season0%d" % jt, [P, PASS], BF16, at=(100, 105, 108, 97)[jt] * KIB) for jt in range(NJ)]
+        season1 = sb("season1", [P, NJ * PASS], BF16)
+        better0 = [sb("better0%d" % jt, [P, PASS], BF16, at=(88 + jt) * KIB) for jt in range(NJ)]
+        season_rows = [tile[:] for tile in season0] + [strip(season1, jt) for jt in range(NJ)]
+        for step in range(2 * NJ):
+            evacuate(season_rows[step], season_sum(step % NJ, step // NJ, step % NJ))
+            jt = step - 1
+            if 0 <= jt < NJ:
+                combine(better0[jt][:], soil_sum(jt, 0, 4 + jt), season0[jt][:], ALU.max)
+        w1w = [load_words("w1w0", w1_words[0].bitcast(I32), 2 * H, U8, below="season00"),
+               load_words("w1w1", w1_words[1].bitcast(I32), 2 * H, U8, below="season01")]
+        w4_raw = [load_float("w4_raw0", w4[cols(0, PASS), :], above="season02")]
+        season1_turned = sb("season1_turned", [P, PACK * S], BF16, at=20 * KIB)
         for pair in range(2):
-            better1.append(sb("better1%d" % pair, [P, 2 * PASS], BF16, AT_B - 7360 + 2048 * pair))
-            nc.vector.tensor_tensor(better1[pair][:], strip(soil1, 2 * pair, 2), strip(season[1], 2 * pair, 2), ALU.max)
+            copy_turned(strip(season1_turned, 2 * pair, 2), turn(season1, pair, 4 + pair))
 
-        seed_banks = {}
-        for b, jt in [(0, jt) for jt in range(NJ)] + [(1, 0), (1, 1)]:
-            seed_banks[b, jt] = new_bank("high" if b else "low")
-            seed_pass(seed_banks[b, jt], 0, jt, b)
-        for b, jt in [(0, 0), (1, 0), (0, 1), (1, 1), (0, 2), (0, 3)]:
-            seed_pass(seed_banks[b, jt], 1, jt, b)
+        w2_scales.append(sb("w2_scales1", [P, PASS], U8, on=("season03", 0)))
+        quantize(w2_codes[1][:], w2_scales[1][:], w2_bf[1][:])
+        soil1 = sb("soil1", [P, NJ * PASS], BF16)
+        for jt in range(NJ):
+            evacuate(strip(soil1, jt), soil_sum(jt, 1, (0, 1, 4, 5)[jt]))
+        g1w = [sb("g1w0", [P, S], U32, on=("w2_bf1", 0)), sb("g1w1", [P, S], U32)]
+        pick(g1w[0][:], t1w[0], idx1)
+        w4_raw.append(load_float("w4_raw1", w4[cols(PASS, PASS), :], on=("t1w0", 0)))
+        seed0_banks = [bank_at(number) for number in (6, 7, 2, 3)]
+        for jt in range(NJ):
+            seed_pass(seed0_banks[jt], 0, jt, 0)
+        pick(g1w[1][:], t1w[1], idx1)
+        base_sb = sb("base_sb", [P, N // P, S], F32, on=("t1w1", LAP))
+        nc.sync.dma_start(out=base_sb[:], in_=base.rearrange("(c p) j -> p c j", p=P))
+        better1 = [sb("better1%d" % pair, [P, 2 * PASS], BF16, at=(92 + 2 * pair) * KIB) for pair in range(2)]
+        h0_rows = sb("h0_rows", [P, NJ * PASS], BF16, at=80 * KIB)
+        seed1 = sb("seed1", [P, NJ * PASS], BF16, at=84 * KIB)
+        h = [sb("h%d" % b, [P, PACK * S], BF16) for b in range(2)]
 
-        h_rows = [sb("h_rows%d" % b, [P, NJ * PASS], BF16, AT_F + 4096 * b) for b in range(NB)]
-        h = [sb("h%d" % b, [P, PACK * S], BF16) for b in range(NB)]
-        h_codes = sb("h_codes", [P, NB, S], U32)
-        w4_codes = sb("w4_codes", [P, NB, N], U32)
+        def copy_seed_of_half1(jt, number):
+            bank = bank_at(number)
+            for a in (1, 0):
+                seed_pass(bank, a, jt, 1)
+            evacuate(strip(seed1, jt), bank)
 
-        def turn(b, pair):
-            bank = new_bank("high")
-            for slot in range(4):
-                nc.tensor.transpose(bank[:, cols(P * slot)],
-                                    h_rows[b][:].bitcast(F32)[:, cols(PASS * pair + P * slot)], identity[:])
-            nc.scalar.copy(out=h[b][:].bitcast(F32)[:, cols(PASS * pair, PASS)].rearrange("p (a j u) -> p a j u", a=2, u=2),
-                           in_=bank[:].rearrange("p (a u j) -> p a j u", a=2, u=2))
+        def better_of_half1(pair):
+            combine_turned(better1[pair][:], turn(soil1, pair, 6 + pair), strip(season1_turned, 2 * pair, 2), ALU.max)
 
-        def quantize_w4(b, first, count, grouped):
-            quantize(w4_codes[:, b, cols(P * first, P * count)], w4_scales[:, b, cols(P * first, P * count)], grouped[:, :])
+        def limit_half0(jt):
+            seed_pass(seed0_banks[jt], 1, jt, 0)
+            combine(strip(h0_rows, jt), seed0_banks[jt], better0[jt][:], ALU.min)
 
-        def round_w4_tile(b, c, offset):
-            grouped = sb("w4_bf%d%d" % (b, c), [P, PACK * P], BF16, offset)
-            nc.scalar.copy(out=grouped[:].rearrange("p (u v i) -> p u i v", v=4, i=PACK),
-                           in_=w4_raw[b][:, :, cols(P * c)].rearrange("p i (u v) -> p u i v", v=4))
-            return grouped
+        w4_bf0 = sb("w4_bf0", [P, PACK * PASS], BF16)
+        for c in range(3):
+            round_on_gpsimd(strip(w4_bf0, c), w4_raw[0][:, :, cols(P * c)])
+        for jt in range(NJ):
+            limit_half0(jt)
+        copy_seed_of_half1(0, 0)
+        copy_seed_of_half1(1, 1)
+        round_on_scalar(strip(w4_bf0, 3), w4_raw[0][:, :, cols(P * 3)])
+        for pair in range(2):
+            better_of_half1(pair)
+        for pair in range(2):
+            copy_turned(strip(h[0], 2 * pair, 2), turn(h0_rows, pair, 2 + pair))
+        copy_seed_of_half1(2, 4)
+        copy_seed_of_half1(3, 5)
+
+        h_codes = [sb("h_codes%d" % b, [P, S], U32) for b in range(2)]
+        h_scales = [sb("h_scales%d" % b, [P, S], U8, on=("season1_turned", S * b)) for b in range(2)]
+        w4_codes = [sb("w4_codes%d" % b, [P, N], U32) for b in range(2)]
+        w4_scales = [sb("w4_scales%d" % b, [P, N], U8, on=("season1_turned", 2 * S + N * b)) for b in range(2)]
 
         def output_pass(c, b):
-            nc.tensor.matmul_mx(out=banks[c][:], lhsT=w4_codes[:, b, cols(P * c)].bitcast(FP8X4),
-                                lhsT_scale=w4_scales[:, b, cols(P * c)], rhs=h_codes[:, b, :].bitcast(FP8X4),
-                                rhs_scale=h_scales[:, b, :], start=(b == 0), stop=(b == 1))
-
-        w4_bf0 = sb("w4_bf0", [P, PACK * 2 * P], BF16, AT_D + 8192)
-        round_on_gpsimd(w4_bf0, w4_raw[0], 2 * P)
-        for jt in range(NJ):
-            combine(strip(h_rows[0], jt), seed_banks[0, jt], strip(better0, jt), ALU.min)
-        seed1 = [sb("seed1%d" % pair, [P, 2 * PASS], BF16, AT_F + 12288 + 2048 * pair) for pair in range(2)]
-        for jt in range(NJ):
-            if jt > 1:
-                seed_banks[1, jt] = new_bank("low")
-                for a in range(2):
-                    seed_pass(seed_banks[1, jt], a, jt, 1)
-            evacuate(strip(seed1[jt // 2], jt % 2), seed_banks[1, jt])
-        for pair in range(2):
-            turn(0, pair)
-        w4_third = round_w4_tile(0, 2, AT_F)
-        for pair in range(2):
-            nc.vector.tensor_tensor(strip(h_rows[1], 2 * pair, 2), seed1[pair][:], better1[pair][:], ALU.min)
-        for pair in range(2):
-            turn(1, pair)
-        h_scales = sb("h_scales", [P, NB, S], U8, AT_F + 12288)
-        w4_scales = sb("w4_scales", [P, NB, N], U8, AT_F + 14336)
-        quantize(h_codes[:, 0, :], h_scales[:, 0, :], h[0][:])
-        w4_last = sb("w4_last", [P, PACK * P], BF16, AT_F + 15360)
-        nc.vector.tensor_copy(out=w4_last[:].rearrange("p (u v i) -> p u i v", v=4, i=PACK),
-                              in_=w4_raw[0][:, :, cols(3 * P)].rearrange("p i (u v) -> p u i v", v=4))
-        quantize_w4(0, 0, 2, w4_bf0)
-        quantize_w4(0, 2, 1, w4_third)
-        quantize_w4(0, 3, 1, w4_last)
-        banks = [new_bank("low") for c in range(N // P)]
-        for c in range(N // P):
-            output_pass(c, 0)
-        quantize(h_codes[:, 1, :], h_scales[:, 1, :], h[1][:])
+            nc.tensor.matmul_mx(out=out_banks[c][:], lhsT=w4_codes[b][:, cols(P * c)].bitcast(FP8X4),
+                                lhsT_scale=w4_scales[b][:, cols(P * c)], rhs=h_codes[b][:].bitcast(FP8X4),
+                                rhs_scale=h_scales[b][:], start=(b == 0), stop=(b == 1))
 
         def finish(c):
             res = sb("res%d" % c, [P, S], F32)
-            nc.vector.tensor_tensor(res[:], banks[c][:], base_sb[:, c, :], ALU.add)
+            nc.vector.tensor_tensor(res[:], out_banks[c][:], base_sb[:, c, :], ALU.add)
             nc.sync.dma_start(out=out[cols(P * c), :], in_=res[:])
 
+        quantize(w4_codes[0][:], w4_scales[0][:], w4_bf0[:])
+        quantize(h_codes[0][:], h_scales[0][:], h[0][:])
+        for pair in range(2):
+            combine_turned(strip(h[1], 2 * pair, 2), turn(seed1, pair, 6 + pair), better1[pair][:], ALU.min)
+        out_banks = [bank_at(number) for number in range(N // P)]
         for c in range(N // P):
-            quantize_w4(1, c, 1, round_w4_tile(1, c, AT_F + 4096 + 1024 * c))
+            output_pass(c, 0)
+        w4_bf1 = sb("w4_bf1", [P, PACK * PASS], BF16, on=("w1w0", 0))
+        quantize(h_codes[1][:], h_scales[1][:], h[1][:])
+        for c in range(N // P):
+            round_on_scalar(strip(w4_bf1, c), w4_raw[1][:, :, cols(P * c)])
+            quantize(w4_codes[1][:, cols(P * c)], w4_scales[1][:, cols(P * c)], strip(w4_bf1, c))
             output_pass(c, 1)
             if c > 0:
                 finish(c - 1)

@@ -25,6 +25,8 @@ ROWS = 16
 TOP = 96
 BANK = 2048
 LAP = 64
+RUN = 8
+HALF = S // 2
 KIB = 1024
 
 
@@ -102,20 +104,40 @@ def tile_list_maize_hybrid_placement_kernel(
             nc.gpsimd.tensor_scalar(out=grouped.rearrange("p (c i) -> p c i", i=PACK), in0=raw.rearrange("p i c -> p c i"),
                                     scalar1=1.0, scalar2=0.0, op0=ALU.mult, op1=ALU.add)
 
-        def paired(bank):
-            return bank[:].rearrange("j (p u e) -> j u p e", u=2, e=2)
+        def deal_on_scalar(grouped, raw, t):
+            nc.scalar.copy(out=grouped.rearrange("p (g u v i) -> p g u i v", u=2, v=4, i=PACK),
+                           in_=raw[:].rearrange("p i (g t u v) -> p t g u i v", t=PACK, u=2, v=4)[:, t])
 
-        def as_pairs(ap):
-            return ap.rearrange("j (u p e) -> j u p e", u=2, e=2)
+        def deal_on_gpsimd(grouped, raw, t):
+            nc.gpsimd.tensor_scalar(out=grouped.rearrange("p (g c i) -> p g c i", c=RUN, i=PACK),
+                                    in0=raw[:].rearrange("p i (g t c) -> p t g c i", t=PACK, c=RUN)[:, t],
+                                    scalar1=1.0, scalar2=0.0, op0=ALU.mult, op1=ALU.add)
+
+        def deal_words(dst, src, run):
+            nc.vector.tensor_copy(out=dst.bitcast(I32).rearrange("p (b t g c) -> p b t g c", t=PACK, g=ROWS, c=run),
+                                  in_=src.bitcast(I32).rearrange("p (b g t c) -> p b t g c", t=PACK, g=ROWS, c=run))
+
+        def load_dealt_rows(name, rows, **place):
+            raw = sb(name, [P, PACK, N], F32, **place)
+            for t in range(PACK):
+                nc.sync.dma_start(out=raw[:, t, :], in_=rows.rearrange("(g t i) n -> t g i n", t=PACK, i=RUN)[t])
+            return raw
 
         def strip(tile, jt, count=1):
             return tile[:, cols(PASS * jt, PASS * count)]
 
-        def evacuate(rounded, bank):
-            nc.scalar.copy(out=as_pairs(rounded), in_=paired(bank))
+        def woven(bank):
+            return bank[:].rearrange("p (e x) -> p x e", e=2)
 
-        def combine(dst, bank, other, op):
-            nc.vector.tensor_tensor(as_pairs(dst), paired(bank), as_pairs(other), op)
+        def as_pairs(ap):
+            return ap.rearrange("p (x e) -> p x e", e=2)
+
+        def evacuate(rounded, bank):
+            nc.scalar.copy(out=as_pairs(rounded), in_=woven(bank))
+
+        def evacuate_seed(rounded, bank):
+            nc.scalar.copy(out=rounded.rearrange("j (u g i e) -> j u g i e", u=2, i=RUN, e=2),
+                           in_=bank[:].rearrange("j (g u e i) -> j u g i e", u=2, i=RUN, e=2))
 
         def turn(rows, pair, number):
             bank = bank_at(number)
@@ -125,14 +147,10 @@ def tile_list_maize_hybrid_placement_kernel(
                                         rows[:].bitcast(F32)[:, cols(P * (4 * pair + 2 * a + u))], identity[:])
             return bank
 
-        def copy_turned(dst, bank):
-            nc.scalar.copy(out=dst.bitcast(F32).rearrange("p (x u) -> p x u", u=2),
-                           in_=bank[:].rearrange("p (u x) -> p x u", u=2))
-
-        def combine_turned(dst, bank, other, op):
+        def limit(dst, bank, better):
             nc.vector.tensor_tensor(dst.rearrange("p (x u e) -> p x u e", u=2, e=2),
                                     bank[:].bitcast(BF16).rearrange("p (u x e) -> p x u e", u=2, e=2),
-                                    other.rearrange("p (x u e) -> p x u e", u=2, e=2), op)
+                                    better.rearrange("p (u x e) -> p x u e", u=2, e=2), ALU.min)
 
         t3s = sb("t3s", [P, T2], U8)
         t2s = sb("t2s", [P, T2], U8)
@@ -144,6 +162,8 @@ def tile_list_maize_hybrid_placement_kernel(
         nc.vector.memset(t3s[0 : P - ROWS, :].bitcast(I32), 0)
         nc.vector.memset(t2s[0 : P - ROWS, :].bitcast(I32), 0)
         nc.vector.memset(t1s[0:TOP, :].bitcast(I32), 0)
+        w3s_raw = sb("w3s_raw", [P, H], U8)
+        nc.gpsimd.memset(w3s_raw[TOP : P - ROWS, :].bitcast(I32), 0)
         nc.gpsimd.memset(plane1[:].bitcast(I32), 0)
         nc.gpsimd.memset(plane2[:].bitcast(I32), 0)
         identity = sb("identity", [P, P], F32)
@@ -153,17 +173,18 @@ def tile_list_maize_hybrid_placement_kernel(
         load_rows(t3s, 0, tab3_scales)
         idx2 = load_list("idx2", offs2)
         load_rows(t2s, 0, tab2_scales)
-        load_rows(stage1, 2 * S, w3_scales)
+        load_rows(w3s_raw, 0, w3_scales)
         w2_raw = [load_float("w2_raw0", w2[:, cols(0, PASS)])]
         t3w = load_words("t3w", tab3_words[0].bitcast(I32), T2, U16, at=26 * KIB)
         idx1 = load_list("idx1", offs)
         load_rows(t1s, 0, tab_scales)
+        w3_raw = load_words("w3_raw", words(w3_words[0]), 4 * H, U8, at=50 * KIB)
         t2w = load_words("t2w", words(tab2_words[0]), T2, U32, at=64 * KIB)
-        w3w = load_words("w3w", words(w3_words[0]), 4 * H, U8)
         load_rows(stage2, S, w1_scales)
 
         picked23 = sb("picked23", [P, 2 * S], U8, at=1 * KIB)
         pick(picked23[:, cols(0, S)], t3s, idx3)
+        deal_words(stage1[TOP:P, cols(2 * S, H)], w3s_raw[TOP:P, :], RUN // 4)
         pick(picked23[:, cols(S, S)], t2s, idx2)
         move(stage1[TOP:P, cols(0, 2 * S)], picked23[TOP:P, :])
         for r in range(4):
@@ -175,10 +196,13 @@ def tile_list_maize_hybrid_placement_kernel(
         pick(g3w[:], t3w, idx3)
         t1w = [load_words("t1w0", words(tab_words[0]), T, U32, above="t3w")]
 
-        w2_bf = [sb("w2_bf0", [P, PACK * PASS], BF16, at=52 * KIB)]
-        round_on_scalar(w2_bf[0][:], w2_raw[0][:])
+        w2_bf = [sb("w2_bf0", [P, PACK * PASS], BF16, at=60 * KIB)]
+        for t in range(PACK):
+            deal_on_scalar(strip(w2_bf[0], t), w2_raw[0], t)
+        w3w = sb("w3w", [P, 4 * H], U8)
+        deal_words(w3w[:], w3_raw[:], RUN)
 
-        picked1 = sb("picked1", [P, S], U8, at=50 * KIB)
+        picked1 = sb("picked1", [P, S], U8, on=("w3_raw", 0))
         pick(picked1[:], t1s, idx1)
         w2_codes = [sb("w2_codes0", [P, PASS], U32, on=("t1s", 0)), sb("w2_codes1", [P, PASS], U32, at=16 * KIB)]
         w2_scales = [sb("w2_scales0", [P, PASS], U8)]
@@ -192,23 +216,29 @@ def tile_list_maize_hybrid_placement_kernel(
         pick(g2w[:], t2w, idx2)
         w2_bf.append(sb("w2_bf1", [P, PACK * PASS], BF16, on=("w2_bf0", 0)))
         for c in range(4):
-            round_on_gpsimd(strip(w2_bf[1], c), w2_raw[1][:, :, cols(P * c)])
+            deal_on_gpsimd(strip(w2_bf[1], c), w2_raw[1], c)
 
-        def season_sum(jt, b, number):
+        def season_sum(k, b, number):
             bank = bank_at(number)
-            nc.tensor.matmul_mx(out=bank[:], lhsT=g3w[:, cols(P * jt)].bitcast(FP4X4), lhsT_scale=g3s[:, cols(P * jt)],
-                                rhs=w3w[:, cols(4 * PASS * b, 4 * PASS)].bitcast(FP8X4),
-                                rhs_scale=w3s[:, cols(PASS * b, PASS)], start=True, stop=True)
+            for e in range(2):
+                t = 2 * (k % 2) + e
+                nc.tensor.matmul_mx(out=bank[:, cols(HALF * e, HALF)], lhsT=w3w[:, cols(4 * (PASS * b + P * t), 4 * P)].bitcast(FP8X4),
+                                    lhsT_scale=w3s[:, cols(PASS * b + P * t)],
+                                    rhs=g3w[:, cols(HALF * (k // 2), HALF)].bitcast(FP4X4),
+                                    rhs_scale=g3s[:, cols(HALF * (k // 2), HALF)], start=True, stop=True)
             return bank
 
-        def soil_sum(jt, b, number):
+        def soil_sum(k, b, number):
             bank = bank_at(number)
-            nc.tensor.matmul_mx(out=bank[:], lhsT=g2w[:, cols(P * jt)].bitcast(FP8X4), lhsT_scale=g2s[:, cols(P * jt)],
-                                rhs=w2_codes[b][:].bitcast(FP8X4), rhs_scale=w2_scales[b][:], start=True, stop=True)
+            for e in range(2):
+                t = 2 * (k % 2) + e
+                nc.tensor.matmul_mx(out=bank[:, cols(HALF * e, HALF)], lhsT=w2_codes[b][:, cols(P * t)].bitcast(FP8X4),
+                                    lhsT_scale=w2_scales[b][:, cols(P * t)],
+                                    rhs=g2w[:, cols(HALF * (k // 2), HALF)].bitcast(FP8X4),
+                                    rhs_scale=g2s[:, cols(HALF * (k // 2), HALF)], start=True, stop=True)
             return bank
 
-        def seed_pass(bank, a, jt, b):
-            opening = b
+        def seed_pass(bank, a, jt, b, opening):
             nc.tensor.matmul_mx(out=bank[:], lhsT=g1w[a][:, cols(P * jt)].bitcast(FP8X4),
                                 lhsT_scale=plane2[:, a, cols(P * jt)],
                                 rhs=w1w[a][:, cols(2 * PASS * b, 2 * PASS)].bitcast(FP4X4),
@@ -216,71 +246,60 @@ def tile_list_maize_hybrid_placement_kernel(
 
         season0 = [sb("season0%d" % jt, [P, PASS], BF16, at=(100, 105, 108, 97)[jt] * KIB) for jt in range(NJ)]
         season1 = sb("season1", [P, NJ * PASS], BF16)
-        better0 = [sb("better0%d" % jt, [P, PASS], BF16, at=(88 + jt) * KIB) for jt in range(NJ)]
+        better0 = [sb("better0%d" % pair, [P, 2 * PASS], BF16, at=(88 + 2 * pair) * KIB) for pair in range(2)]
         season_rows = [tile[:] for tile in season0] + [strip(season1, jt) for jt in range(NJ)]
         for step in range(2 * NJ):
             evacuate(season_rows[step], season_sum(step % NJ, step // NJ, step % NJ))
             jt = step - 1
             if 0 <= jt < NJ:
-                combine(better0[jt][:], soil_sum(jt, 0, 4 + jt), season0[jt][:], ALU.max)
+                nc.vector.tensor_tensor(as_pairs(strip(better0[jt // 2], jt % 2)), woven(soil_sum(jt, 0, 4 + jt)),
+                                        as_pairs(season0[jt][:]), ALU.max)
         w1w = [load_words("w1w0", w1_words[0].bitcast(I32), 2 * H, U8, below="season00"),
                load_words("w1w1", w1_words[1].bitcast(I32), 2 * H, U8, below="season01")]
-        w4_raw = [load_float("w4_raw0", w4[cols(0, PASS), :], above="season02")]
-        season1_turned = sb("season1_turned", [P, PACK * S], BF16, at=20 * KIB)
-        for pair in range(2):
-            copy_turned(strip(season1_turned, 2 * pair, 2), turn(season1, pair, 4 + pair))
+        w4_raw = [load_dealt_rows("w4_raw0", w4[cols(0, PASS), :], above="season02")]
 
         w2_scales.append(sb("w2_scales1", [P, PASS], U8, on=("season03", 0)))
         quantize(w2_codes[1][:], w2_scales[1][:], w2_bf[1][:])
         soil1 = sb("soil1", [P, NJ * PASS], BF16)
         for jt in range(NJ):
-            evacuate(strip(soil1, jt), soil_sum(jt, 1, (0, 1, 4, 5)[jt]))
+            evacuate(strip(soil1, jt), soil_sum(jt, 1, jt))
         g1w = [sb("g1w0", [P, S], U32, on=("w2_bf1", 0)), sb("g1w1", [P, S], U32)]
         pick(g1w[0][:], t1w[0], idx1)
-        w4_raw.append(load_float("w4_raw1", w4[cols(PASS, PASS), :], on=("t1w0", 0)))
-        seed0_banks = [bank_at(number) for number in (6, 7, 2, 3)]
-        for jt in range(NJ):
-            seed_pass(seed0_banks[jt], 0, jt, 0)
-        pick(g1w[1][:], t1w[1], idx1)
+        w4_raw.append(load_dealt_rows("w4_raw1", w4[cols(PASS, PASS), :], on=("t1w0", 0)))
+        seed0_banks = [bank_at(number) for number in (6, 7, 4, 5)]
+        for jt in range(2):
+            seed_pass(seed0_banks[jt], 0, jt, 0, 0)
+        for half in range(2):
+            nc.vector.tensor_copy(g1w[1][:, cols(S // 2 * half, S // 2)],
+                                  t1w[1][:].indirect(idx1[:, cols(S // 32 * half, S // 32)]))
         base_sb = sb("base_sb", [P, N // P, S], F32, on=("t1w1", LAP))
         nc.sync.dma_start(out=base_sb[:], in_=base.rearrange("(c p) j -> p c j", p=P))
-        better1 = [sb("better1%d" % pair, [P, 2 * PASS], BF16, at=(92 + 2 * pair) * KIB) for pair in range(2)]
-        h0_rows = sb("h0_rows", [P, NJ * PASS], BF16, at=80 * KIB)
-        seed1 = sb("seed1", [P, NJ * PASS], BF16, at=84 * KIB)
+        better1 = sb("better1", [P, NJ * PASS], BF16, below="t1w1")
+        for pair in range(2):
+            nc.vector.tensor_tensor(strip(better1, 2 * pair, 2), strip(soil1, 2 * pair, 2), strip(season1, 2 * pair, 2), ALU.max)
+        seed = [sb("seed%d" % b, [P, NJ * PASS], BF16, at=(80 + 4 * b) * KIB) for b in range(2)]
         h = [sb("h%d" % b, [P, PACK * S], BF16) for b in range(2)]
 
-        def copy_seed_of_half1(jt, number):
-            bank = bank_at(number)
-            for a in (1, 0):
-                seed_pass(bank, a, jt, 1)
-            evacuate(strip(seed1, jt), bank)
-
-        def better_of_half1(pair):
-            combine_turned(better1[pair][:], turn(soil1, pair, 6 + pair), strip(season1_turned, 2 * pair, 2), ALU.max)
-
-        def limit_half0(jt):
-            seed_pass(seed0_banks[jt], 1, jt, 0)
-            combine(strip(h0_rows, jt), seed0_banks[jt], better0[jt][:], ALU.min)
-
-        w4_bf0 = sb("w4_bf0", [P, PACK * PASS], BF16)
-        for c in range(3):
-            round_on_gpsimd(strip(w4_bf0, c), w4_raw[0][:, :, cols(P * c)])
+        w4_bf0 = [sb("w4_bf00", [P, PACK * 2 * P], BF16)]
+        for c in range(2):
+            round_on_gpsimd(strip(w4_bf0[0], c), w4_raw[0][:, :, cols(P * c)])
         for jt in range(NJ):
-            limit_half0(jt)
-        copy_seed_of_half1(0, 0)
-        copy_seed_of_half1(1, 1)
-        round_on_scalar(strip(w4_bf0, 3), w4_raw[0][:, :, cols(P * 3)])
-        for pair in range(2):
-            better_of_half1(pair)
-        for pair in range(2):
-            copy_turned(strip(h[0], 2 * pair, 2), turn(h0_rows, pair, 2 + pair))
-        copy_seed_of_half1(2, 4)
-        copy_seed_of_half1(3, 5)
+            seed_pass(seed0_banks[jt], 1, jt, 0, 0)
+            if jt < 2:
+                seed_pass(seed0_banks[jt + 2], 0, jt + 2, 0, 0)
+            evacuate_seed(strip(seed[0], jt), seed0_banks[jt])
+        for jt in range(NJ):
+            bank = bank_at(jt)
+            for a in (1, 0):
+                seed_pass(bank, a, jt, 1, 1)
+            evacuate_seed(strip(seed[1], jt), bank)
+            if jt < 2:
+                limit(strip(h[0], 2 * jt, 2), turn(seed[0], jt, 6 + jt), better0[jt][:])
 
         h_codes = [sb("h_codes%d" % b, [P, S], U32) for b in range(2)]
-        h_scales = [sb("h_scales%d" % b, [P, S], U8, on=("season1_turned", S * b)) for b in range(2)]
+        h_scales = [sb("h_scales%d" % b, [P, S], U8, on=("seed0", S * b)) for b in range(2)]
         w4_codes = [sb("w4_codes%d" % b, [P, N], U32) for b in range(2)]
-        w4_scales = [sb("w4_scales%d" % b, [P, N], U8, on=("season1_turned", 2 * S + N * b)) for b in range(2)]
+        w4_scales = [sb("w4_scales%d" % b, [P, N], U8, on=("seed0", 2 * S + N * b)) for b in range(2)]
 
         def output_pass(c, b):
             nc.tensor.matmul_mx(out=out_banks[c][:], lhsT=w4_codes[b][:, cols(P * c)].bitcast(FP8X4),
@@ -292,11 +311,15 @@ def tile_list_maize_hybrid_placement_kernel(
             nc.vector.tensor_tensor(res[:], out_banks[c][:], base_sb[:, c, :], ALU.add)
             nc.sync.dma_start(out=out[cols(P * c), :], in_=res[:])
 
-        quantize(w4_codes[0][:], w4_scales[0][:], w4_bf0[:])
+        w4_bf0.append(sb("w4_bf01", [P, PACK * 2 * P], BF16, on=("better01", 0)))
+        nc.vector.tensor_copy(out=w4_bf0[1][:].rearrange("p (u v i) -> p u i v", v=4, i=PACK),
+                              in_=w4_raw[0][:, :, cols(2 * P, 2 * P)].rearrange("p i (u v) -> p u i v", v=4))
         quantize(h_codes[0][:], h_scales[0][:], h[0][:])
+        for half in range(2):
+            quantize(w4_codes[0][:, cols(2 * P * half, 2 * P)], w4_scales[0][:, cols(2 * P * half, 2 * P)], w4_bf0[half][:])
         for pair in range(2):
-            combine_turned(strip(h[1], 2 * pair, 2), turn(seed1, pair, 6 + pair), better1[pair][:], ALU.min)
-        out_banks = [bank_at(number) for number in range(N // P)]
+            limit(strip(h[1], 2 * pair, 2), turn(seed[1], pair, 4 + pair), strip(better1, 2 * pair, 2))
+        out_banks = [bank_at(number) for number in (6, 7, 0, 1)]
         for c in range(N // P):
             output_pass(c, 0)
         w4_bf1 = sb("w4_bf1", [P, PACK * PASS], BF16, on=("w1w0", 0))

@@ -26,7 +26,6 @@ TOP = 96
 BANK = 2048
 LAP = 64
 RUN = 8
-HALF = S // 2
 KIB = 1024
 
 
@@ -127,10 +126,10 @@ def tile_list_maize_hybrid_placement_kernel(
             return tile[:, cols(PASS * jt, PASS * count)]
 
         def woven(bank):
-            return bank[:].rearrange("p (e x) -> p x e", e=2)
+            return bank[:].rearrange("p (t x) -> p x t", t=PACK)
 
         def as_pairs(ap):
-            return ap.rearrange("p (x e) -> p x e", e=2)
+            return ap.rearrange("p (x t) -> p x t", t=PACK)
 
         def evacuate(rounded, bank):
             nc.scalar.copy(out=as_pairs(rounded), in_=woven(bank))
@@ -139,18 +138,18 @@ def tile_list_maize_hybrid_placement_kernel(
             nc.scalar.copy(out=rounded.rearrange("j (u g i e) -> j u g i e", u=2, i=RUN, e=2),
                            in_=bank[:].rearrange("j (g u e i) -> j u g i e", u=2, i=RUN, e=2))
 
-        def turn(rows, pair, number):
+        def turn(rows, number):
             bank = bank_at(number)
             for u in range(2):
                 for a in range(2):
                     nc.tensor.transpose(bank[:, cols(P * (2 * u + a))],
-                                        rows[:].bitcast(F32)[:, cols(P * (4 * pair + 2 * a + u))], identity[:])
+                                        rows[:].bitcast(F32)[:, cols(P * (2 * a + u))], identity[:])
             return bank
 
         def limit(dst, bank, better):
             nc.vector.tensor_tensor(dst.rearrange("p (x u e) -> p x u e", u=2, e=2),
                                     bank[:].bitcast(BF16).rearrange("p (u x e) -> p x u e", u=2, e=2),
-                                    better.rearrange("p (u x e) -> p x u e", u=2, e=2), ALU.min)
+                                    better.rearrange("p (x u e) -> p x u e", u=2, e=2), ALU.min)
 
         t3s = sb("t3s", [P, T2], U8)
         t2s = sb("t2s", [P, T2], U8)
@@ -202,40 +201,36 @@ def tile_list_maize_hybrid_placement_kernel(
         w3w = sb("w3w", [P, 4 * H], U8)
         deal_words(w3w[:], w3_raw[:], RUN)
 
-        picked1 = sb("picked1", [P, S], U8, on=("w3_raw", 0))
-        pick(picked1[:], t1s, idx1)
-        w2_codes = [sb("w2_codes0", [P, PASS], U32, on=("t1s", 0)), sb("w2_codes1", [P, PASS], U32, at=16 * KIB)]
+        t1w.append(load_words("t1w1", words(tab_words[1]), T, U32, below="w3_raw"))
+        w2_codes = [sb("w2_codes0", [P, PASS], U32, on=("w3_raw", LAP)), sb("w2_codes1", [P, PASS], U32)]
         w2_scales = [sb("w2_scales0", [P, PASS], U8)]
         quantize(w2_codes[0][:], w2_scales[0][:], w2_bf[0][:])
+        g2w = sb("g2w", [P, S], U32)
+        pick(g2w[:], t2w, idx2)
+        picked1 = sb("picked1", [P, S], U8, on=("t2w", 0))
+        pick(picked1[:], t1s, idx1)
         move(stage2[TOP:P, cols(0, S)], picked1[TOP:P, :])
         for q in range(4):
             nc.sync.dma_start(out=plane2[cols(32 * q, 4), :, :].bitcast(I32),
                               in_=stage2[cols(TOP + 8 * q, 8), :].bitcast(I32))
-        t1w.append(load_words("t1w1", words(tab_words[1]), T, U32, below="picked1"))
-        g2w = sb("g2w", [P, S], U32)
-        pick(g2w[:], t2w, idx2)
         w2_bf.append(sb("w2_bf1", [P, PACK * PASS], BF16, on=("w2_bf0", 0)))
         for c in range(4):
             deal_on_gpsimd(strip(w2_bf[1], c), w2_raw[1], c)
 
         def season_sum(k, b, number):
             bank = bank_at(number)
-            for e in range(2):
-                t = 2 * (k % 2) + e
-                nc.tensor.matmul_mx(out=bank[:, cols(HALF * e, HALF)], lhsT=w3w[:, cols(4 * (PASS * b + P * t), 4 * P)].bitcast(FP8X4),
-                                    lhsT_scale=w3s[:, cols(PASS * b + P * t)],
-                                    rhs=g3w[:, cols(HALF * (k // 2), HALF)].bitcast(FP4X4),
-                                    rhs_scale=g3s[:, cols(HALF * (k // 2), HALF)], start=True, stop=True)
+            for t in range(PACK):
+                nc.tensor.matmul_mx(out=bank[:, cols(P * t)], lhsT=w3w[:, cols(4 * (PASS * b + P * t), 4 * P)].bitcast(FP8X4),
+                                    lhsT_scale=w3s[:, cols(PASS * b + P * t)], rhs=g3w[:, cols(P * k)].bitcast(FP4X4),
+                                    rhs_scale=g3s[:, cols(P * k)], start=True, stop=True)
             return bank
 
         def soil_sum(k, b, number):
             bank = bank_at(number)
-            for e in range(2):
-                t = 2 * (k % 2) + e
-                nc.tensor.matmul_mx(out=bank[:, cols(HALF * e, HALF)], lhsT=w2_codes[b][:, cols(P * t)].bitcast(FP8X4),
-                                    lhsT_scale=w2_scales[b][:, cols(P * t)],
-                                    rhs=g2w[:, cols(HALF * (k // 2), HALF)].bitcast(FP8X4),
-                                    rhs_scale=g2s[:, cols(HALF * (k // 2), HALF)], start=True, stop=True)
+            for t in range(PACK):
+                nc.tensor.matmul_mx(out=bank[:, cols(P * t)], lhsT=w2_codes[b][:, cols(P * t)].bitcast(FP8X4),
+                                    lhsT_scale=w2_scales[b][:, cols(P * t)], rhs=g2w[:, cols(P * k)].bitcast(FP8X4),
+                                    rhs_scale=g2s[:, cols(P * k)], start=True, stop=True)
             return bank
 
         def seed_pass(bank, a, jt, b, opening):
@@ -244,29 +239,33 @@ def tile_list_maize_hybrid_placement_kernel(
                                 rhs=w1w[a][:, cols(2 * PASS * b, 2 * PASS)].bitcast(FP4X4),
                                 rhs_scale=plane2[:, a, cols(S + PASS * b, PASS)], start=(a == opening), stop=(a != opening))
 
-        season0 = [sb("season0%d" % jt, [P, PASS], BF16, at=(100, 105, 108, 97)[jt] * KIB) for jt in range(NJ)]
-        season1 = sb("season1", [P, NJ * PASS], BF16)
-        better0 = [sb("better0%d" % pair, [P, 2 * PASS], BF16, at=(88 + 2 * pair) * KIB) for pair in range(2)]
-        season_rows = [tile[:] for tile in season0] + [strip(season1, jt) for jt in range(NJ)]
+        season0 = [sb("season0%d" % jt, [P, PASS], BF16, at=(100 + 5 * jt) * KIB) for jt in range(2)]
+        season = sb("season", [P, 6 * PASS], BF16)
+        soil = sb("soil", [P, 4 * PASS], BF16, at=88 * KIB)
+        better_first = sb("better_first", [P, 2 * PASS], BF16)
+        season_rows = [tile[:] for tile in season0] + [strip(season, k) for k in range(6)]
         for step in range(2 * NJ):
             evacuate(season_rows[step], season_sum(step % NJ, step // NJ, step % NJ))
-            jt = step - 1
-            if 0 <= jt < NJ:
-                nc.vector.tensor_tensor(as_pairs(strip(better0[jt // 2], jt % 2)), woven(soil_sum(jt, 0, 4 + jt)),
+            jt = step - 2
+            if 0 <= jt < 2:
+                nc.vector.tensor_tensor(as_pairs(strip(better_first, jt)), woven(soil_sum(jt, 0, 4 + jt)),
                                         as_pairs(season0[jt][:]), ALU.max)
         w1w = [load_words("w1w0", w1_words[0].bitcast(I32), 2 * H, U8, below="season00"),
                load_words("w1w1", w1_words[1].bitcast(I32), 2 * H, U8, below="season01")]
-        w4_raw = [load_dealt_rows("w4_raw0", w4[cols(0, PASS), :], above="season02")]
+        w4_raw = [load_dealt_rows("w4_raw0", w4[cols(0, PASS), :], above="season01")]
 
-        w2_scales.append(sb("w2_scales1", [P, PASS], U8, on=("season03", 0)))
+        w2_scales.append(sb("w2_scales1", [P, PASS], U8, on=("season01", LAP)))
         quantize(w2_codes[1][:], w2_scales[1][:], w2_bf[1][:])
-        soil1 = sb("soil1", [P, NJ * PASS], BF16)
-        for jt in range(NJ):
-            evacuate(strip(soil1, jt), soil_sum(jt, 1, jt))
+        late_banks = (6, 7, 2, 3)
+        for k in range(2):
+            evacuate(strip(soil, k), soil_sum(2 + k, 0, k))
+        for k in range(2):
+            evacuate(strip(soil, 2 + k), soil_sum(k, 1, late_banks[k]))
+        last_soil = [soil_sum(k, 1, late_banks[k]) for k in range(2, NJ)]
         g1w = [sb("g1w0", [P, S], U32, on=("w2_bf1", 0)), sb("g1w1", [P, S], U32)]
         pick(g1w[0][:], t1w[0], idx1)
         w4_raw.append(load_dealt_rows("w4_raw1", w4[cols(PASS, PASS), :], on=("t1w0", 0)))
-        seed0_banks = [bank_at(number) for number in (6, 7, 4, 5)]
+        seed0_banks = [bank_at(number) for number in (4, 5, 0, 1)]
         for jt in range(2):
             seed_pass(seed0_banks[jt], 0, jt, 0, 0)
         for half in range(2):
@@ -274,32 +273,37 @@ def tile_list_maize_hybrid_placement_kernel(
                                   t1w[1][:].indirect(idx1[:, cols(S // 32 * half, S // 32)]))
         base_sb = sb("base_sb", [P, N // P, S], F32, on=("t1w1", LAP))
         nc.sync.dma_start(out=base_sb[:], in_=base.rearrange("(c p) j -> p c j", p=P))
-        better1 = sb("better1", [P, NJ * PASS], BF16, below="t1w1")
-        for pair in range(2):
-            nc.vector.tensor_tensor(strip(better1, 2 * pair, 2), strip(soil1, 2 * pair, 2), strip(season1, 2 * pair, 2), ALU.max)
-        seed = [sb("seed%d" % b, [P, NJ * PASS], BF16, at=(80 + 4 * b) * KIB) for b in range(2)]
+        better_late = sb("better_late", [P, 6 * PASS], BF16, below="t1w1")
+        for k in range(2):
+            nc.vector.tensor_tensor(as_pairs(strip(better_late, 4 + k)), woven(last_soil[k]), as_pairs(strip(season, 4 + k)), ALU.max)
+        nc.vector.tensor_tensor(strip(better_late, 0, 4), soil[:], strip(season, 0, 4), ALU.max)
+        better = [better_first[:]] + [strip(better_late, 2 * pair, 2) for pair in range(3)]
+        seed = [sb("seed%d" % k, [P, 2 * PASS], BF16, at=(80 + 2 * k) * KIB) for k in range(NJ)]
         h = [sb("h%d" % b, [P, PACK * S], BF16) for b in range(2)]
 
-        w4_bf0 = [sb("w4_bf00", [P, PACK * 2 * P], BF16)]
-        for c in range(2):
-            round_on_gpsimd(strip(w4_bf0[0], c), w4_raw[0][:, :, cols(P * c)])
+        w4_bf0 = [sb("w4_bf00", [P, PACK * 2 * P], BF16, on=("soil", 0))]
+        nc.vector.tensor_copy(out=w4_bf0[0][:].rearrange("p (u v i) -> p u i v", v=4, i=PACK),
+                              in_=w4_raw[0][:, :, cols(0, 2 * P)].rearrange("p i (u v) -> p u i v", v=4))
         for jt in range(NJ):
             seed_pass(seed0_banks[jt], 1, jt, 0, 0)
             if jt < 2:
                 seed_pass(seed0_banks[jt + 2], 0, jt + 2, 0, 0)
-            evacuate_seed(strip(seed[0], jt), seed0_banks[jt])
+            evacuate_seed(strip(seed[jt // 2], jt % 2), seed0_banks[jt])
         for jt in range(NJ):
-            bank = bank_at(jt)
+            bank = bank_at(late_banks[jt])
             for a in (1, 0):
                 seed_pass(bank, a, jt, 1, 1)
-            evacuate_seed(strip(seed[1], jt), bank)
+            evacuate_seed(strip(seed[2 + jt // 2], jt % 2), bank)
             if jt < 2:
-                limit(strip(h[0], 2 * jt, 2), turn(seed[0], jt, 6 + jt), better0[jt][:])
+                limit(strip(h[0], 2 * jt, 2), turn(seed[jt], 4 + jt), better[jt])
+        w4_bf0.append(sb("w4_bf01", [P, PACK * 2 * P], BF16, on=("seed0", 0)))
+        for c in range(2):
+            round_on_gpsimd(strip(w4_bf0[1], c), w4_raw[0][:, :, cols(P * (2 + c))])
 
         h_codes = [sb("h_codes%d" % b, [P, S], U32) for b in range(2)]
-        h_scales = [sb("h_scales%d" % b, [P, S], U8, on=("seed0", S * b)) for b in range(2)]
+        h_scales = [sb("h_scales%d" % b, [P, S], U8, on=("seed1", S * b)) for b in range(2)]
         w4_codes = [sb("w4_codes%d" % b, [P, N], U32) for b in range(2)]
-        w4_scales = [sb("w4_scales%d" % b, [P, N], U8, on=("seed0", 2 * S + N * b)) for b in range(2)]
+        w4_scales = [sb("w4_scales%d" % b, [P, N], U8, on=("seed1", 2 * S + N * b)) for b in range(2)]
 
         def output_pass(c, b):
             nc.tensor.matmul_mx(out=out_banks[c][:], lhsT=w4_codes[b][:, cols(P * c)].bitcast(FP8X4),
@@ -311,23 +315,20 @@ def tile_list_maize_hybrid_placement_kernel(
             nc.vector.tensor_tensor(res[:], out_banks[c][:], base_sb[:, c, :], ALU.add)
             nc.sync.dma_start(out=out[cols(P * c), :], in_=res[:])
 
-        w4_bf0.append(sb("w4_bf01", [P, PACK * 2 * P], BF16, on=("better01", 0)))
-        nc.vector.tensor_copy(out=w4_bf0[1][:].rearrange("p (u v i) -> p u i v", v=4, i=PACK),
-                              in_=w4_raw[0][:, :, cols(2 * P, 2 * P)].rearrange("p i (u v) -> p u i v", v=4))
         quantize(h_codes[0][:], h_scales[0][:], h[0][:])
         for half in range(2):
             quantize(w4_codes[0][:, cols(2 * P * half, 2 * P)], w4_scales[0][:, cols(2 * P * half, 2 * P)], w4_bf0[half][:])
         for pair in range(2):
-            limit(strip(h[1], 2 * pair, 2), turn(seed[1], pair, 4 + pair), strip(better1, 2 * pair, 2))
-        out_banks = [bank_at(number) for number in (6, 7, 0, 1)]
+            limit(strip(h[1], 2 * pair, 2), turn(seed[2 + pair], pair), better[2 + pair])
+        out_banks = [bank_at(4 + c) for c in range(N // P)]
         for c in range(N // P):
             output_pass(c, 0)
         w4_bf1 = sb("w4_bf1", [P, PACK * PASS], BF16, on=("w1w0", 0))
+        for half in range(2):
+            round_on_scalar(strip(w4_bf1, 2 * half, 2), w4_raw[1][:, :, cols(2 * P * half, 2 * P)])
+        quantize(w4_codes[1][:, cols(0, 2 * P)], w4_scales[1][:, cols(0, 2 * P)], strip(w4_bf1, 0, 2))
         quantize(h_codes[1][:], h_scales[1][:], h[1][:])
+        quantize(w4_codes[1][:, cols(2 * P, 2 * P)], w4_scales[1][:, cols(2 * P, 2 * P)], strip(w4_bf1, 2, 2))
         for c in range(N // P):
-            round_on_scalar(strip(w4_bf1, c), w4_raw[1][:, :, cols(P * c)])
-            quantize(w4_codes[1][:, cols(P * c)], w4_scales[1][:, cols(P * c)], strip(w4_bf1, c))
             output_pass(c, 1)
-            if c > 0:
-                finish(c - 1)
-        finish(N // P - 1)
+            finish(c)

@@ -25,7 +25,6 @@ ROWS = 16
 TOP = 96
 BANK = 2048
 LAP = 64
-RUN = 8
 KIB = 1024
 
 
@@ -103,24 +102,14 @@ def tile_list_maize_hybrid_placement_kernel(
             nc.gpsimd.tensor_scalar(out=grouped.rearrange("p (c i) -> p c i", i=PACK), in0=raw.rearrange("p i c -> p c i"),
                                     scalar1=1.0, scalar2=0.0, op0=ALU.mult, op1=ALU.add)
 
-        def deal_on_scalar(grouped, raw, t):
-            nc.scalar.copy(out=grouped.rearrange("p (g u v i) -> p g u i v", u=2, v=4, i=PACK),
-                           in_=raw[:].rearrange("p i (g t u v) -> p t g u i v", t=PACK, u=2, v=4)[:, t])
+        def deal_on_scalar(grouped, raw):
+            nc.scalar.copy(out=grouped[:].rearrange("p (t m i) -> p m i t", t=PACK, i=PACK),
+                           in_=raw[:].rearrange("p i (m t) -> p m i t", t=PACK))
 
-        def deal_on_gpsimd(grouped, raw, t):
-            nc.gpsimd.tensor_scalar(out=grouped.rearrange("p (g c i) -> p g c i", c=RUN, i=PACK),
-                                    in0=raw[:].rearrange("p i (g t c) -> p t g c i", t=PACK, c=RUN)[:, t],
+        def deal_on_gpsimd(grouped, raw, first, count):
+            nc.gpsimd.tensor_scalar(out=grouped[:].rearrange("p (t m i) -> p m t i", t=PACK, i=PACK)[:, cols(first, count)],
+                                    in0=raw[:].rearrange("p i (m t) -> p m t i", t=PACK)[:, cols(first, count)],
                                     scalar1=1.0, scalar2=0.0, op0=ALU.mult, op1=ALU.add)
-
-        def deal_words(dst, src, run):
-            nc.vector.tensor_copy(out=dst.bitcast(I32).rearrange("p (b t g c) -> p b t g c", t=PACK, g=ROWS, c=run),
-                                  in_=src.bitcast(I32).rearrange("p (b g t c) -> p b t g c", t=PACK, g=ROWS, c=run))
-
-        def load_dealt_rows(name, rows, **place):
-            raw = sb(name, [P, PACK, N], F32, **place)
-            for t in range(PACK):
-                nc.sync.dma_start(out=raw[:, t, :], in_=rows.rearrange("(g t i) n -> t g i n", t=PACK, i=RUN)[t])
-            return raw
 
         def strip(tile, jt, count=1):
             return tile[:, cols(PASS * jt, PASS * count)]
@@ -135,8 +124,8 @@ def tile_list_maize_hybrid_placement_kernel(
             nc.scalar.copy(out=as_pairs(rounded), in_=woven(bank))
 
         def evacuate_seed(rounded, bank):
-            nc.scalar.copy(out=rounded.rearrange("j (u g i e) -> j u g i e", u=2, i=RUN, e=2),
-                           in_=bank[:].rearrange("j (g u e i) -> j u g i e", u=2, i=RUN, e=2))
+            nc.scalar.copy(out=rounded.rearrange("j (u p e) -> j u p e", u=2, e=2),
+                           in_=bank[:].rearrange("j (p u e) -> j u p e", u=2, e=2))
 
         def turn(rows, number):
             bank = bank_at(number)
@@ -162,7 +151,7 @@ def tile_list_maize_hybrid_placement_kernel(
         nc.vector.memset(t2s[0 : P - ROWS, :].bitcast(I32), 0)
         nc.vector.memset(t1s[0:TOP, :].bitcast(I32), 0)
         w3s_raw = sb("w3s_raw", [P, H], U8)
-        nc.gpsimd.memset(w3s_raw[TOP : P - ROWS, :].bitcast(I32), 0)
+        nc.gpsimd.memset(w3s_raw[0 : P - ROWS, :].bitcast(I32), 0)
         nc.gpsimd.memset(plane1[:].bitcast(I32), 0)
         nc.gpsimd.memset(plane2[:].bitcast(I32), 0)
         identity = sb("identity", [P, P], F32)
@@ -183,7 +172,8 @@ def tile_list_maize_hybrid_placement_kernel(
 
         picked23 = sb("picked23", [P, 2 * S], U8, at=1 * KIB)
         pick(picked23[:, cols(0, S)], t3s, idx3)
-        deal_words(stage1[TOP:P, cols(2 * S, H)], w3s_raw[TOP:P, :], RUN // 4)
+        nc.vector.tensor_copy(out=stage1[:, cols(2 * S, H)].rearrange("p (b t m) -> p b t m", t=PACK, m=P),
+                              in_=w3s_raw[:].rearrange("p (b m t) -> p b t m", t=PACK, m=P))
         pick(picked23[:, cols(S, S)], t2s, idx2)
         move(stage1[TOP:P, cols(0, 2 * S)], picked23[TOP:P, :])
         for r in range(4):
@@ -196,10 +186,10 @@ def tile_list_maize_hybrid_placement_kernel(
         t1w = [load_words("t1w0", words(tab_words[0]), T, U32, above="t3w")]
 
         w2_bf = [sb("w2_bf0", [P, PACK * PASS], BF16, at=60 * KIB)]
-        for t in range(PACK):
-            deal_on_scalar(strip(w2_bf[0], t), w2_raw[0], t)
+        deal_on_scalar(w2_bf[0], w2_raw[0])
         w3w = sb("w3w", [P, 4 * H], U8)
-        deal_words(w3w[:], w3_raw[:], RUN)
+        nc.vector.tensor_copy(out=w3w[:].bitcast(I32).rearrange("p (b t m) -> p b m t", t=PACK, m=P),
+                              in_=w3_raw[:].bitcast(I32).rearrange("p (b m t) -> p b m t", t=PACK, m=P))
 
         t1w.append(load_words("t1w1", words(tab_words[1]), T, U32, below="w3_raw"))
         w2_codes = [sb("w2_codes0", [P, PASS], U32, on=("w3_raw", LAP)), sb("w2_codes1", [P, PASS], U32)]
@@ -215,7 +205,7 @@ def tile_list_maize_hybrid_placement_kernel(
                               in_=stage2[cols(TOP + 8 * q, 8), :].bitcast(I32))
         w2_bf.append(sb("w2_bf1", [P, PACK * PASS], BF16, on=("w2_bf0", 0)))
         for c in range(4):
-            deal_on_gpsimd(strip(w2_bf[1], c), w2_raw[1], c)
+            deal_on_gpsimd(w2_bf[1], w2_raw[1], 32 * c, 32)
 
         def season_sum(k, b, number):
             bank = bank_at(number)
@@ -239,33 +229,29 @@ def tile_list_maize_hybrid_placement_kernel(
                                 rhs=w1w[a][:, cols(2 * PASS * b, 2 * PASS)].bitcast(FP4X4),
                                 rhs_scale=plane2[:, a, cols(S + PASS * b, PASS)], start=(a == opening), stop=(a != opening))
 
-        season0 = [sb("season0%d" % jt, [P, PASS], BF16, at=(100 + 5 * jt) * KIB) for jt in range(2)]
-        season = sb("season", [P, 6 * PASS], BF16)
-        soil = sb("soil", [P, 4 * PASS], BF16, at=88 * KIB)
-        better_first = sb("better_first", [P, 2 * PASS], BF16)
-        season_rows = [tile[:] for tile in season0] + [strip(season, k) for k in range(6)]
+        season0 = [sb("season0%d" % jt, [P, PASS], BF16, at=(100, 105, 96, 97)[jt] * KIB) for jt in range(NJ)]
+        season1 = sb("season1", [P, NJ * PASS], BF16)
+        soil1 = sb("soil1", [P, NJ * PASS], BF16, at=88 * KIB)
+        better0 = sb("better0", [P, NJ * PASS], BF16)
+        season_rows = [tile[:] for tile in season0] + [strip(season1, k) for k in range(NJ)]
         for step in range(2 * NJ):
-            evacuate(season_rows[step], season_sum(step % NJ, step // NJ, step % NJ))
+            evacuate(season_rows[step], season_sum(step % NJ, step // NJ, step if step < NJ else step % 2))
             jt = step - 2
-            if 0 <= jt < 2:
-                nc.vector.tensor_tensor(as_pairs(strip(better_first, jt)), woven(soil_sum(jt, 0, 4 + jt)),
+            if 0 <= jt < NJ:
+                nc.vector.tensor_tensor(as_pairs(strip(better0, jt)), woven(soil_sum(jt, 0, 4 + jt)),
                                         as_pairs(season0[jt][:]), ALU.max)
         w1w = [load_words("w1w0", w1_words[0].bitcast(I32), 2 * H, U8, below="season00"),
                load_words("w1w1", w1_words[1].bitcast(I32), 2 * H, U8, below="season01")]
-        w4_raw = [load_dealt_rows("w4_raw0", w4[cols(0, PASS), :], above="season01")]
+        w4_raw = [load_float("w4_raw0", w4[cols(0, PASS), :], above="season01")]
 
-        w2_scales.append(sb("w2_scales1", [P, PASS], U8, on=("season01", LAP)))
+        w2_scales.append(sb("w2_scales1", [P, PASS], U8, on=("season02", 0)))
         quantize(w2_codes[1][:], w2_scales[1][:], w2_bf[1][:])
-        late_banks = (6, 7, 2, 3)
-        for k in range(2):
-            evacuate(strip(soil, k), soil_sum(2 + k, 0, k))
-        for k in range(2):
-            evacuate(strip(soil, 2 + k), soil_sum(k, 1, late_banks[k]))
-        last_soil = [soil_sum(k, 1, late_banks[k]) for k in range(2, NJ)]
+        for k in range(NJ):
+            evacuate(strip(soil1, k), soil_sum(k, 1, (k + 2) % NJ))
         g1w = [sb("g1w0", [P, S], U32, on=("w2_bf1", 0)), sb("g1w1", [P, S], U32)]
         pick(g1w[0][:], t1w[0], idx1)
-        w4_raw.append(load_dealt_rows("w4_raw1", w4[cols(PASS, PASS), :], on=("t1w0", 0)))
-        seed0_banks = [bank_at(number) for number in (4, 5, 0, 1)]
+        w4_raw.append(load_float("w4_raw1", w4[cols(PASS, PASS), :], on=("t1w0", 0)))
+        seed0_banks = [bank_at(number) for number in range(4, 8)]
         for jt in range(2):
             seed_pass(seed0_banks[jt], 0, jt, 0, 0)
         for half in range(2):
@@ -273,15 +259,13 @@ def tile_list_maize_hybrid_placement_kernel(
                                   t1w[1][:].indirect(idx1[:, cols(S // 32 * half, S // 32)]))
         base_sb = sb("base_sb", [P, N // P, S], F32, on=("t1w1", LAP))
         nc.sync.dma_start(out=base_sb[:], in_=base.rearrange("(c p) j -> p c j", p=P))
-        better_late = sb("better_late", [P, 6 * PASS], BF16, below="t1w1")
-        for k in range(2):
-            nc.vector.tensor_tensor(as_pairs(strip(better_late, 4 + k)), woven(last_soil[k]), as_pairs(strip(season, 4 + k)), ALU.max)
-        nc.vector.tensor_tensor(strip(better_late, 0, 4), soil[:], strip(season, 0, 4), ALU.max)
-        better = [better_first[:]] + [strip(better_late, 2 * pair, 2) for pair in range(3)]
+        better1 = sb("better1", [P, NJ * PASS], BF16, below="t1w1")
+        nc.vector.tensor_tensor(better1[:], soil1[:], season1[:], ALU.max)
+        better = [strip(tile, 2 * pair, 2) for tile in (better0, better1) for pair in range(2)]
         seed = [sb("seed%d" % k, [P, 2 * PASS], BF16, at=(80 + 2 * k) * KIB) for k in range(NJ)]
         h = [sb("h%d" % b, [P, PACK * S], BF16) for b in range(2)]
 
-        w4_bf0 = [sb("w4_bf00", [P, PACK * 2 * P], BF16, on=("soil", 0))]
+        w4_bf0 = [sb("w4_bf00", [P, PACK * 2 * P], BF16, on=("soil1", 0))]
         nc.vector.tensor_copy(out=w4_bf0[0][:].rearrange("p (u v i) -> p u i v", v=4, i=PACK),
                               in_=w4_raw[0][:, :, cols(0, 2 * P)].rearrange("p i (u v) -> p u i v", v=4))
         for jt in range(NJ):
@@ -290,7 +274,7 @@ def tile_list_maize_hybrid_placement_kernel(
                 seed_pass(seed0_banks[jt + 2], 0, jt + 2, 0, 0)
             evacuate_seed(strip(seed[jt // 2], jt % 2), seed0_banks[jt])
         for jt in range(NJ):
-            bank = bank_at(late_banks[jt])
+            bank = bank_at((jt + 2) % NJ)
             for a in (1, 0):
                 seed_pass(bank, a, jt, 1, 1)
             evacuate_seed(strip(seed[2 + jt // 2], jt % 2), bank)
@@ -319,8 +303,8 @@ def tile_list_maize_hybrid_placement_kernel(
         for half in range(2):
             quantize(w4_codes[0][:, cols(2 * P * half, 2 * P)], w4_scales[0][:, cols(2 * P * half, 2 * P)], w4_bf0[half][:])
         for pair in range(2):
-            limit(strip(h[1], 2 * pair, 2), turn(seed[2 + pair], pair), better[2 + pair])
-        out_banks = [bank_at(4 + c) for c in range(N // P)]
+            limit(strip(h[1], 2 * pair, 2), turn(seed[2 + pair], 6 + pair), better[2 + pair])
+        out_banks = [bank_at(number) for number in (4, 5, 2, 3)]
         for c in range(N // P):
             output_pass(c, 0)
         w4_bf1 = sb("w4_bf1", [P, PACK * PASS], BF16, on=("w1w0", 0))

@@ -172,9 +172,9 @@ def tile_list_maize_hybrid_placement_kernel(
 
         picked23 = sb("picked23", [P, 2 * S], U8, at=1 * KIB)
         pick(picked23[:, cols(0, S)], t3s, idx3)
+        pick(picked23[:, cols(S, S)], t2s, idx2)
         nc.vector.tensor_copy(out=stage1[:, cols(2 * S, H)].rearrange("p (b t m) -> p b t m", t=PACK, m=P),
                               in_=w3s_raw[:].rearrange("p (b m t) -> p b t m", t=PACK, m=P))
-        pick(picked23[:, cols(S, S)], t2s, idx2)
         move(stage1[TOP:P, cols(0, 2 * S)], picked23[TOP:P, :])
         for r in range(4):
             nc.sync.dma_start(out=plane1[r:P:32, :].bitcast(I32), in_=stage1[P - ROWS + r : P : 4, :].bitcast(I32))
@@ -194,9 +194,9 @@ def tile_list_maize_hybrid_placement_kernel(
         t1w.append(load_words("t1w1", words(tab_words[1]), T, U32, below="w3_raw"))
         w2_codes = [sb("w2_codes0", [P, PASS], U32, on=("w3_raw", LAP)), sb("w2_codes1", [P, PASS], U32)]
         w2_scales = [sb("w2_scales0", [P, PASS], U8)]
-        quantize(w2_codes[0][:], w2_scales[0][:], w2_bf[0][:])
         g2w = sb("g2w", [P, S], U32)
         pick(g2w[:], t2w, idx2)
+        quantize(w2_codes[0][:], w2_scales[0][:], w2_bf[0][:])
         picked1 = sb("picked1", [P, S], U8, on=("t2w", 0))
         pick(picked1[:], t1s, idx1)
         move(stage2[TOP:P, cols(0, S)], picked1[TOP:P, :])
@@ -259,14 +259,14 @@ def tile_list_maize_hybrid_placement_kernel(
                                   t1w[1][:].indirect(idx1[:, cols(S // 32 * half, S // 32)]))
         base_sb = sb("base_sb", [P, N // P, S], F32, on=("t1w1", LAP))
         nc.sync.dma_start(out=base_sb[:], in_=base.rearrange("(c p) j -> p c j", p=P))
-        better1 = sb("better1", [P, NJ * PASS], BF16, below="t1w1")
-        nc.vector.tensor_tensor(better1[:], soil1[:], season1[:], ALU.max)
+        better1 = sb("better1", [P, (NJ + 2) * PASS], BF16, below="t1w1")
+        nc.vector.tensor_tensor(strip(better1, 0, NJ), soil1[:], season1[:], ALU.max)
         better = [strip(tile, 2 * pair, 2) for tile in (better0, better1) for pair in range(2)]
         seed = [sb("seed%d" % k, [P, 2 * PASS], BF16, at=(80 + 2 * k) * KIB) for k in range(NJ)]
         h = [sb("h%d" % b, [P, PACK * S], BF16) for b in range(2)]
 
-        w4_bf0 = [sb("w4_bf00", [P, PACK * 2 * P], BF16, on=("soil1", 0))]
-        nc.vector.tensor_copy(out=w4_bf0[0][:].rearrange("p (u v i) -> p u i v", v=4, i=PACK),
+        w4_bf0 = [strip(better1, NJ, 2)]
+        nc.vector.tensor_copy(out=w4_bf0[0].rearrange("p (u v i) -> p u i v", v=4, i=PACK),
                               in_=w4_raw[0][:, :, cols(0, 2 * P)].rearrange("p i (u v) -> p u i v", v=4))
         for jt in range(NJ):
             seed_pass(seed0_banks[jt], 1, jt, 0, 0)
@@ -280,9 +280,9 @@ def tile_list_maize_hybrid_placement_kernel(
             evacuate_seed(strip(seed[2 + jt // 2], jt % 2), bank)
             if jt < 2:
                 limit(strip(h[0], 2 * jt, 2), turn(seed[jt], 4 + jt), better[jt])
-        w4_bf0.append(sb("w4_bf01", [P, PACK * 2 * P], BF16, on=("seed0", 0)))
+        w4_bf0.append(sb("w4_bf01", [P, PACK * 2 * P], BF16, on=("seed0", 0))[:])
         for c in range(2):
-            round_on_gpsimd(strip(w4_bf0[1], c), w4_raw[0][:, :, cols(P * (2 + c))])
+            round_on_gpsimd(w4_bf0[1][:, cols(PASS * c, PASS)], w4_raw[0][:, :, cols(P * (2 + c))])
 
         h_codes = [sb("h_codes%d" % b, [P, S], U32) for b in range(2)]
         h_scales = [sb("h_scales%d" % b, [P, S], U8, on=("seed1", S * b)) for b in range(2)]
@@ -299,9 +299,9 @@ def tile_list_maize_hybrid_placement_kernel(
             nc.vector.tensor_tensor(res[:], out_banks[c][:], base_sb[:, c, :], ALU.add)
             nc.sync.dma_start(out=out[cols(P * c), :], in_=res[:])
 
+        quantize(w4_codes[0][:, cols(0, 2 * P)], w4_scales[0][:, cols(0, 2 * P)], w4_bf0[0])
         quantize(h_codes[0][:], h_scales[0][:], h[0][:])
-        for half in range(2):
-            quantize(w4_codes[0][:, cols(2 * P * half, 2 * P)], w4_scales[0][:, cols(2 * P * half, 2 * P)], w4_bf0[half][:])
+        quantize(w4_codes[0][:, cols(2 * P, 2 * P)], w4_scales[0][:, cols(2 * P, 2 * P)], w4_bf0[1])
         for pair in range(2):
             limit(strip(h[1], 2 * pair, 2), turn(seed[2 + pair], 6 + pair), better[2 + pair])
         out_banks = [bank_at(number) for number in (4, 5, 2, 3)]

@@ -25,6 +25,7 @@ ROWS = 16
 TOP = 96
 BANK = 2048
 LAP = 64
+HALF = S // 2
 KIB = 1024
 
 
@@ -115,10 +116,10 @@ def tile_list_maize_hybrid_placement_kernel(
             return tile[:, cols(PASS * jt, PASS * count)]
 
         def woven(bank):
-            return bank[:].rearrange("p (t x) -> p x t", t=PACK)
+            return bank[:].rearrange("p (e x) -> p x e", e=2)
 
         def as_pairs(ap):
-            return ap.rearrange("p (x t) -> p x t", t=PACK)
+            return ap.rearrange("p (x e) -> p x e", e=2)
 
         def evacuate(rounded, bank):
             nc.scalar.copy(out=as_pairs(rounded), in_=woven(bank))
@@ -138,7 +139,7 @@ def tile_list_maize_hybrid_placement_kernel(
         def limit(dst, bank, better):
             nc.vector.tensor_tensor(dst.rearrange("p (x u e) -> p x u e", u=2, e=2),
                                     bank[:].bitcast(BF16).rearrange("p (u x e) -> p x u e", u=2, e=2),
-                                    better.rearrange("p (x u e) -> p x u e", u=2, e=2), ALU.min)
+                                    better.rearrange("p (u x e) -> p x u e", u=2, e=2), ALU.min)
 
         t3s = sb("t3s", [P, T2], U8)
         t2s = sb("t2s", [P, T2], U8)
@@ -209,18 +210,23 @@ def tile_list_maize_hybrid_placement_kernel(
 
         def season_sum(k, b, number):
             bank = bank_at(number)
-            for t in range(PACK):
-                nc.tensor.matmul_mx(out=bank[:, cols(P * t)], lhsT=w3w[:, cols(4 * (PASS * b + P * t), 4 * P)].bitcast(FP8X4),
-                                    lhsT_scale=w3s[:, cols(PASS * b + P * t)], rhs=g3w[:, cols(P * k)].bitcast(FP4X4),
-                                    rhs_scale=g3s[:, cols(P * k)], start=True, stop=True)
+            for e in range(2):
+                t = 2 * (k % 2) + e
+                nc.tensor.matmul_mx(out=bank[:, cols(HALF * e, HALF)],
+                                    lhsT=w3w[:, cols(4 * (PASS * b + P * t), 4 * P)].bitcast(FP8X4),
+                                    lhsT_scale=w3s[:, cols(PASS * b + P * t)],
+                                    rhs=g3w[:, cols(HALF * (k // 2), HALF)].bitcast(FP4X4),
+                                    rhs_scale=g3s[:, cols(HALF * (k // 2), HALF)], start=True, stop=True)
             return bank
 
         def soil_sum(k, b, number):
             bank = bank_at(number)
-            for t in range(PACK):
-                nc.tensor.matmul_mx(out=bank[:, cols(P * t)], lhsT=w2_codes[b][:, cols(P * t)].bitcast(FP8X4),
-                                    lhsT_scale=w2_scales[b][:, cols(P * t)], rhs=g2w[:, cols(P * k)].bitcast(FP8X4),
-                                    rhs_scale=g2s[:, cols(P * k)], start=True, stop=True)
+            for e in range(2):
+                t = 2 * (k % 2) + e
+                nc.tensor.matmul_mx(out=bank[:, cols(HALF * e, HALF)], lhsT=w2_codes[b][:, cols(P * t)].bitcast(FP8X4),
+                                    lhsT_scale=w2_scales[b][:, cols(P * t)],
+                                    rhs=g2w[:, cols(HALF * (k // 2), HALF)].bitcast(FP8X4),
+                                    rhs_scale=g2s[:, cols(HALF * (k // 2), HALF)], start=True, stop=True)
             return bank
 
         def seed_pass(bank, a, jt, b, opening):
@@ -289,10 +295,12 @@ def tile_list_maize_hybrid_placement_kernel(
         w4_codes = [sb("w4_codes%d" % b, [P, N], U32) for b in range(2)]
         w4_scales = [sb("w4_scales%d" % b, [P, N], U8, on=("seed1", 2 * S + N * b)) for b in range(2)]
 
-        def output_pass(c, b):
-            nc.tensor.matmul_mx(out=out_banks[c][:], lhsT=w4_codes[b][:, cols(P * c)].bitcast(FP8X4),
-                                lhsT_scale=w4_scales[b][:, cols(P * c)], rhs=h_codes[b][:].bitcast(FP8X4),
-                                rhs_scale=h_scales[b][:], start=(b == 0), stop=(b == 1))
+        def output_pass(c, b, first=0, count=S):
+            nc.tensor.matmul_mx(out=out_banks[c][:, cols(first, count)], lhsT=w4_codes[b][:, cols(P * c)].bitcast(FP8X4),
+                                lhsT_scale=w4_scales[b][:, cols(P * c)],
+                                rhs=h_codes[b][:, cols(first, count)].bitcast(FP8X4),
+                                rhs_scale=h_scales[b][:, cols(first, count)], start=(b == 0),
+                                stop=(b == 1 and first + count == S))
 
         def finish(c):
             res = sb("res%d" % c, [P, S], F32)
@@ -310,9 +318,15 @@ def tile_list_maize_hybrid_placement_kernel(
         w4_bf1 = sb("w4_bf1", [P, PACK * PASS], BF16, on=("w1w0", 0))
         for half in range(2):
             round_on_scalar(strip(w4_bf1, 2 * half, 2), w4_raw[1][:, :, cols(2 * P * half, 2 * P)])
+        quantize(h_codes[1][:, cols(0, 2 * P)], h_scales[1][:, cols(0, 2 * P)], strip(h[1], 0, 2))
         quantize(w4_codes[1][:, cols(0, 2 * P)], w4_scales[1][:, cols(0, 2 * P)], strip(w4_bf1, 0, 2))
-        quantize(h_codes[1][:], h_scales[1][:], h[1][:])
+        for c in range(2):
+            output_pass(c, 1, 0, 2 * P)
+        quantize(h_codes[1][:, cols(2 * P, 2 * P)], h_scales[1][:, cols(2 * P, 2 * P)], strip(h[1], 2, 2))
         quantize(w4_codes[1][:, cols(2 * P, 2 * P)], w4_scales[1][:, cols(2 * P, 2 * P)], strip(w4_bf1, 2, 2))
         for c in range(N // P):
-            output_pass(c, 1)
+            if c < 2:
+                output_pass(c, 1, 2 * P, 2 * P)
+            else:
+                output_pass(c, 1)
             finish(c)

@@ -265,15 +265,15 @@ def tile_list_maize_hybrid_placement_kernel(
                                   t1w[1][:].indirect(idx1[:, cols(S // 32 * half, S // 32)]))
         base_sb = sb("base_sb", [P, N // P, S], F32, on=("t1w1", LAP))
         nc.sync.dma_start(out=base_sb[:], in_=base.rearrange("(c p) j -> p c j", p=P))
-        better1 = sb("better1", [P, (NJ + 2) * PASS], BF16, below="t1w1")
+        better1 = sb("better1", [P, (NJ + 1) * PASS], BF16, below="t1w1")
         nc.vector.tensor_tensor(strip(better1, 0, NJ), soil1[:], season1[:], ALU.max)
         better = [strip(tile, 2 * pair, 2) for tile in (better0, better1) for pair in range(2)]
         seed = [sb("seed%d" % k, [P, 2 * PASS], BF16, at=(80 + 2 * k) * KIB) for k in range(NJ)]
         h = [sb("h%d" % b, [P, PACK * S], BF16) for b in range(2)]
 
-        w4_bf0 = [strip(better1, NJ, 2)]
+        w4_bf0 = [strip(better1, NJ)]
         nc.vector.tensor_copy(out=w4_bf0[0].rearrange("p (u v i) -> p u i v", v=4, i=PACK),
-                              in_=w4_raw[0][:, :, cols(0, 2 * P)].rearrange("p i (u v) -> p u i v", v=4))
+                              in_=w4_raw[0][:, :, cols(0)].rearrange("p i (u v) -> p u i v", v=4))
         for jt in range(NJ):
             seed_pass(seed0_banks[jt], 1, jt, 0, 0)
             if jt < 2:
@@ -286,9 +286,9 @@ def tile_list_maize_hybrid_placement_kernel(
             evacuate_seed(strip(seed[2 + jt // 2], jt % 2), bank)
             if jt < 2:
                 limit(strip(h[0], 2 * jt, 2), turn(seed[jt], 4 + jt), better[jt])
-        w4_bf0.append(sb("w4_bf01", [P, PACK * 2 * P], BF16, on=("seed0", 0))[:])
-        for c in range(2):
-            round_on_gpsimd(w4_bf0[1][:, cols(PASS * c, PASS)], w4_raw[0][:, :, cols(P * (2 + c))])
+        w4_bf0.append(sb("w4_bf01", [P, PACK * 3 * P], BF16, on=("soil1", 0))[:])
+        for c in range(3):
+            round_on_gpsimd(w4_bf0[1][:, cols(PASS * c, PASS)], w4_raw[0][:, :, cols(P * (1 + c))])
 
         h_codes = [sb("h_codes%d" % b, [P, S], U32) for b in range(2)]
         h_scales = [sb("h_scales%d" % b, [P, S], U8, on=("seed1", S * b)) for b in range(2)]
@@ -307,9 +307,9 @@ def tile_list_maize_hybrid_placement_kernel(
             nc.vector.tensor_tensor(res[:], out_banks[c][:], base_sb[:, c, :], ALU.add)
             nc.sync.dma_start(out=out[cols(P * c), :], in_=res[:])
 
-        quantize(w4_codes[0][:, cols(0, 2 * P)], w4_scales[0][:, cols(0, 2 * P)], w4_bf0[0])
+        quantize(w4_codes[0][:, cols(0)], w4_scales[0][:, cols(0)], w4_bf0[0])
         quantize(h_codes[0][:], h_scales[0][:], h[0][:])
-        quantize(w4_codes[0][:, cols(2 * P, 2 * P)], w4_scales[0][:, cols(2 * P, 2 * P)], w4_bf0[1])
+        quantize(w4_codes[0][:, cols(P, 3 * P)], w4_scales[0][:, cols(P, 3 * P)], w4_bf0[1])
         for pair in range(2):
             limit(strip(h[1], 2 * pair, 2), turn(seed[2 + pair], 6 + pair), better[2 + pair])
         out_banks = [bank_at(number) for number in (4, 5, 2, 3)]

@@ -83,7 +83,7 @@ def tile_list_maize_hybrid_placement_kernel(
 
         def load_rows(tile, first, src):
             passes, width = src.shape[0], src.shape[2]
-            nc.sync.dma_start(out=tile[P - passes * ROWS : P, cols(first, width)].bitcast(I32),
+            nc.scalar.dma_start(out=tile[P - passes * ROWS : P, cols(first, width)].bitcast(I32),
                               in_=src.bitcast(I32).rearrange("a q c -> q a c"))
 
         def pick(got, window, idx):

@@ -103,9 +103,9 @@ def tile_list_maize_hybrid_placement_kernel(
             nc.gpsimd.tensor_scalar(out=grouped.rearrange("p (c i) -> p c i", i=PACK), in0=raw.rearrange("p i c -> p c i"),
                                     scalar1=1.0, scalar2=0.0, op0=ALU.mult, op1=ALU.add)
 
-        def deal_on_scalar(grouped, raw):
-            nc.scalar.copy(out=grouped[:].rearrange("p (t m i) -> p m i t", t=PACK, i=PACK),
-                           in_=raw[:].rearrange("p i (m t) -> p m i t", t=PACK))
+        def deal_on_scalar(grouped, raw, first=0, count=P):
+            nc.scalar.copy(out=grouped[:].rearrange("p (t m i) -> p m i t", t=PACK, i=PACK)[:, cols(first, count)],
+                           in_=raw[:].rearrange("p i (m t) -> p m i t", t=PACK)[:, cols(first, count)])
 
         def deal_on_gpsimd(grouped, raw, first, count):
             nc.gpsimd.tensor_scalar(out=grouped[:].rearrange("p (t m i) -> p m t i", t=PACK, i=PACK)[:, cols(first, count)],
@@ -204,8 +204,8 @@ def tile_list_maize_hybrid_placement_kernel(
         for q in range(4):
             nc.sync.dma_start(out=plane2[cols(32 * q, 4), :, :].bitcast(I32),
                               in_=stage2[cols(TOP + 8 * q, 8), :].bitcast(I32))
-        w2_bf.append(sb("w2_bf1", [P, PACK * PASS], BF16, on=("w2_bf0", 0)))
-        for c in range(4):
+        w2_bf.append(sb("w2_bf1", [P, PACK * PASS], BF16, above="picked1"))
+        for c in range(3):
             deal_on_gpsimd(w2_bf[1], w2_raw[1], 32 * c, 32)
 
         def season_sum(k, b, number):
@@ -242,6 +242,8 @@ def tile_list_maize_hybrid_placement_kernel(
         season_rows = [tile[:] for tile in season0] + [strip(season1, k) for k in range(NJ)]
         for step in range(2 * NJ):
             evacuate(season_rows[step], season_sum(step % NJ, step // NJ, step if step < NJ else step % 2))
+            if step == 5:
+                deal_on_scalar(w2_bf[1], w2_raw[1], 96, 32)
             jt = step - 2
             if 0 <= jt < NJ:
                 nc.vector.tensor_tensor(as_pairs(strip(better0, jt)), woven(soil_sum(jt, 0, 4 + jt)),

from contextlib import ExitStack

import concourse.mybir as mybir
from concourse.masks import make_identity

K, K2, H, N, T, T2, S = 1024, 512, 1024, 512, 2048, 1024, 512
FLOPS = 2 * S * H * (K + K2 + K2 + N)

F32 = mybir.dt.float32
BF16 = mybir.dt.bfloat16
I32 = mybir.dt.int32
U32 = mybir.dt.uint32
U16 = mybir.dt.uint16
U8 = mybir.dt.uint8
FP8X4 = mybir.dt.float8_e4m3fn_x4
FP4X4 = mybir.dt.float4_e2m1fn_x4
ALU = mybir.AluOpType
BYTES_OF = {F32: 4, BF16: 2, U32: 4, U16: 2, U8: 1}

P = 128
PACK = 4
PASS = 512
NJ = S // P
ROWS = 16
TOP = 96
BANK = 2048
LAP = 64
HALF = S // 2
KIB = 1024


def tile_list_maize_hybrid_placement_kernel(
    tc, tab_words, tab_scales, tab2_words, tab2_scales, tab3_words, tab3_scales, offs, offs2, offs3,
    w1_words, w1_scales, w2, w3_words, w3_scales, w4, base, out,
):
    nc = tc.nc
    with ExitStack() as ctx:
        keep = ctx.enter_context(tc.tile_pool(name="keep", bufs=1))
        shared = ctx.enter_context(tc.tile_pool(name="shared", bufs=1))
        psum = ctx.enter_context(tc.psum_pool(name="psum", bufs=1))
        span = {}
        banks_made = []

        def sb(name, shape, dtype, at=None, on=None, above=None, below=None):
            size = BYTES_OF[dtype]
            for extent in shape[1:]:
                size = size * extent
            if on is not None:
                at = span[on[0]][0] + on[1]
            if above is not None:
                at = span[above][1] - LAP
            if below is not None:
                at = span[below][0] + LAP - size
            if at is None:
                return keep.tile(shape, dtype, name=name, align_bytes=64)
            span[name] = (at, at + size)
            return shared.tile(shape, dtype, name=name, align_bytes=64, offset=at)

        def bank_at(number):
            banks_made.append(number)
            return psum.tile([P, PASS], F32, name="bank%d" % len(banks_made), offset=BANK * number)

        def cols(first, count=P):
            return slice(first, first + count)

        def words(src):
            return src.rearrange("p t i -> p (t i)").bitcast(I32)

        def load_float(name, rows, **place):
            raw = sb(name, [P, PACK, PASS], F32, **place)
            nc.sync.dma_start(out=raw[:], in_=rows.rearrange("(p i) c -> p i c", i=PACK))
            return raw

        def load_words(name, src, width, dtype, **place):
            raw = sb(name, [P, width], dtype, **place)
            nc.sync.dma_start(out=raw[:].bitcast(I32), in_=src)
            return raw

        def load_list(name, src):
            idx = sb(name, [P, S // 16], U16)
            nc.sync.dma_start(idx[:], src)
            return idx

        def load_rows(tile, first, src):
            passes, width = src.shape[0], src.shape[2]
            nc.scalar.dma_start(out=tile[P - passes * ROWS : P, cols(first, width)].bitcast(I32),
                              in_=src.bitcast(I32).rearrange("a q c -> q a c"))

        def pick(got, window, idx):
            nc.vector.tensor_copy(got, window[:].indirect(idx[:]))

        def move(dst, src):
            nc.vector.tensor_copy(out=dst.bitcast(I32), in_=src.bitcast(I32))

        def quantize(codes, scales, grouped):
            nc.vector.quantize_mx(out=codes.bitcast(FP8X4), scales=scales, in_=grouped)

        def round_on_scalar(grouped, raw):
            nc.scalar.copy(out=grouped.rearrange("p (u v i) -> p u i v", v=4, i=PACK),
                           in_=raw.rearrange("p i (u v) -> p u i v", v=4))

        def round_on_gpsimd(grouped, raw):
            nc.gpsimd.tensor_scalar(out=grouped.rearrange("p (c i) -> p c i", i=PACK), in0=raw.rearrange("p i c -> p c i"),
                                    scalar1=1.0, scalar2=0.0, op0=ALU.mult, op1=ALU.add)

        def deal_on_scalar(grouped, raw, first=0, count=P):
            nc.scalar.copy(out=grouped[:].rearrange("p (t m i) -> p m i t", t=PACK, i=PACK)[:, cols(first, count)],
                           in_=raw[:].rearrange("p i (m t) -> p m i t", t=PACK)[:, cols(first, count)])

        def deal_on_gpsimd(grouped, raw, first, count):
            nc.gpsimd.tensor_scalar(out=grouped[:].rearrange("p (t m i) -> p m t i", t=PACK, i=PACK)[:, cols(first, count)],
                                    in0=raw[:].rearrange("p i (m t) -> p m t i", t=PACK)[:, cols(first, count)],
                                    scalar1=1.0, scalar2=0.0, op0=ALU.mult, op1=ALU.add)

        def strip(tile, jt, count=1):
            return tile[:, cols(PASS * jt, PASS * count)]

        def woven(bank):
            return bank[:].rearrange("p (e x) -> p x e", e=2)

        def as_pairs(ap):
            return ap.rearrange("p (x e) -> p x e", e=2)

        def evacuate(rounded, bank):
            nc.scalar.copy(out=as_pairs(rounded), in_=woven(bank))

        def evacuate_seed(rounded, bank):
            nc.scalar.copy(out=rounded.rearrange("j (u p e) -> j u p e", u=2, e=2),
                           in_=bank[:].rearrange("j (p u e) -> j u p e", u=2, e=2))

        def turn(rows, number):
            bank = bank_at(number)
            for u in range(2):
                for a in range(2):
                    nc.tensor.transpose(bank[:, cols(P * (2 * u + a))],
                                        rows[:].bitcast(F32)[:, cols(P * (2 * a + u))], identity[:])
            return bank

        def limit(dst, bank, better):
            nc.vector.tensor_tensor(dst.rearrange("p (x u e) -> p x u e", u=2, e=2),
                                    bank[:].bitcast(BF16).rearrange("p (u x e) -> p x u e", u=2, e=2),
                                    better.rearrange("p (u x e) -> p x u e", u=2, e=2), ALU.min)

        t3s = sb("t3s", [P, T2], U8)
        t2s = sb("t2s", [P, T2], U8)
        t1s = sb("t1s", [P, T], U8, at=56 * KIB)
        plane1 = sb("plane1", [P, 2 * S + H], U8)
        plane2 = sb("plane2", [P, 2, S + H], U8)
        stage1 = sb("stage1", [P, 2 * S + H], U8)
        stage2 = sb("stage2", [P, S + H], U8)
        nc.vector.memset(t3s[0 : P - ROWS, :].bitcast(I32), 0)
        nc.vector.memset(t2s[0 : P - ROWS, :].bitcast(I32), 0)
        nc.vector.memset(t1s[0:TOP, :].bitcast(I32), 0)
        w3s_raw = sb("w3s_raw", [P, H], U8)
        nc.gpsimd.memset(w3s_raw[0 : P - ROWS, :].bitcast(I32), 0)
        nc.gpsimd.memset(plane1[:].bitcast(I32), 0)
        nc.gpsimd.memset(plane2[:].bitcast(I32), 0)
        identity = sb("identity", [P, P], F32)
        make_identity(nc, identity[:])

        idx3 = load_list("idx3", offs3)
        load_rows(t3s, 0, tab3_scales)
        idx2 = load_list("idx2", offs2)
        load_rows(t2s, 0, tab2_scales)
        load_rows(w3s_raw, 0, w3_scales)
        w2_raw = [load_float("w2_raw0", w2[:, cols(0, PASS)])]
        t3w = load_words("t3w", tab3_words[0].bitcast(I32), T2, U16, at=26 * KIB)
        idx1 = load_list("idx1", offs)
        load_rows(t1s, 0, tab_scales)
        w3_raw = load_words("w3_raw", words(w3_words[0]), 4 * H, U8, at=50 * KIB)
        t2w = load_words("t2w", words(tab2_words[0]), T2, U32, at=64 * KIB)
        load_rows(stage2, S, w1_scales)

        picked23 = sb("picked23", [P, 2 * S], U8, at=1 * KIB)
        pick(picked23[:, cols(0, S)], t3s, idx3)
        pick(picked23[:, cols(S, S)], t2s, idx2)
        nc.vector.tensor_copy(out=stage1[:, cols(2 * S, H)].rearrange("p (b t m) -> p b t m", t=PACK, m=P),
                              in_=w3s_raw[:].rearrange("p (b m t) -> p b t m", t=PACK, m=P))
        move(stage1[TOP:P, cols(0, 2 * S)], picked23[TOP:P, :])
        for r in range(4):
            nc.sync.dma_start(out=plane1[r:P:32, :].bitcast(I32), in_=stage1[P - ROWS + r : P : 4, :].bitcast(I32))
        g3s, g2s, w3s = plane1[:, cols(0, S)], plane1[:, cols(S, S)], plane1[:, cols(2 * S, H)]
        w2_raw.append(load_float("w2_raw1", w2[:, cols(PASS, PASS)], above="picked23"))

        g3w = sb("g3w", [P, S], U16, below="picked23")
        pick(g3w[:], t3w, idx3)
        t1w = [load_words("t1w0", words(tab_words[0]), T, U32, above="t3w")]

        w2_bf = [sb("w2_bf0", [P, PACK * PASS], BF16, at=60 * KIB)]
        deal_on_scalar(w2_bf[0], w2_raw[0])
        w3w = sb("w3w", [P, 4 * H], U8)
        nc.vector.tensor_copy(out=w3w[:].bitcast(I32).rearrange("p (b t m) -> p b m t", t=PACK, m=P),
                              in_=w3_raw[:].bitcast(I32).rearrange("p (b m t) -> p b m t", t=PACK, m=P))

        t1w.append(load_words("t1w1", words(tab_words[1]), T, U32, below="w3_raw"))
        w2_codes = [sb("w2_codes0", [P, PASS], U32, on=("w3_raw", LAP)), sb("w2_codes1", [P, PASS], U32)]
        w2_scales = [sb("w2_scales0", [P, PASS], U8)]
        g2w = sb("g2w", [P, S], U32)
        pick(g2w[:], t2w, idx2)
        quantize(w2_codes[0][:], w2_scales[0][:], w2_bf[0][:])
        picked1 = sb("picked1", [P, S], U8, on=("t2w", 0))
        pick(picked1[:], t1s, idx1)
        move(stage2[TOP:P, cols(0, S)], picked1[TOP:P, :])
        for q in range(4):
            nc.sync.dma_start(out=plane2[cols(32 * q, 4), :, :].bitcast(I32),
                              in_=stage2[cols(TOP + 8 * q, 8), :].bitcast(I32))
        w2_bf.append(sb("w2_bf1", [P, PACK * PASS], BF16, above="picked1"))
        for c in range(3):
            deal_on_gpsimd(w2_bf[1], w2_raw[1], 32 * c, 32)

        def season_sum(k, b, number):
            bank = bank_at(number)
            for e in range(2):
                t = 2 * (k % 2) + e
                nc.tensor.matmul_mx(out=bank[:, cols(HALF * e, HALF)],
                                    lhsT=w3w[:, cols(4 * (PASS * b + P * t), 4 * P)].bitcast(FP8X4),
                                    lhsT_scale=w3s[:, cols(PASS * b + P * t)],
                                    rhs=g3w[:, cols(HALF * (k // 2), HALF)].bitcast(FP4X4),
                                    rhs_scale=g3s[:, cols(HALF * (k // 2), HALF)], start=True, stop=True)
            return bank

        def soil_sum(k, b, number):
            bank = bank_at(number)
            for e in range(2):
                t = 2 * (k % 2) + e
                nc.tensor.matmul_mx(out=bank[:, cols(HALF * e, HALF)], lhsT=w2_codes[b][:, cols(P * t)].bitcast(FP8X4),
                                    lhsT_scale=w2_scales[b][:, cols(P * t)],
                                    rhs=g2w[:, cols(HALF * (k // 2), HALF)].bitcast(FP8X4),
                                    rhs_scale=g2s[:, cols(HALF * (k // 2), HALF)], start=True, stop=True)
            return bank

        def seed_pass(bank, a, jt, b, opening):
            nc.tensor.matmul_mx(out=bank[:], lhsT=g1w[a][:, cols(P * jt)].bitcast(FP8X4),
                                lhsT_scale=plane2[:, a, cols(P * jt)],
                                rhs=w1w[a][:, cols(2 * PASS * b, 2 * PASS)].bitcast(FP4X4),
                                rhs_scale=plane2[:, a, cols(S + PASS * b, PASS)], start=(a == opening), stop=(a != opening))

        season0 = [sb("season0%d" % jt, [P, PASS], BF16, at=(100, 105, 96, 97)[jt] * KIB) for jt in range(NJ)]
        season1 = sb("season1", [P, NJ * PASS], BF16)
        soil1 = sb("soil1", [P, NJ * PASS], BF16, at=88 * KIB)
        better0 = sb("better0", [P, NJ * PASS], BF16)
        season_rows = [tile[:] for tile in season0] + [strip(season1, k) for k in range(NJ)]
        for step in range(2 * NJ):
            evacuate(season_rows[step], season_sum(step % NJ, step // NJ, step if step < NJ else step % 2))
            if step == 5:
                deal_on_scalar(w2_bf[1], w2_raw[1], 96, 32)
            jt = step - 2
            if 0 <= jt < NJ:
                nc.vector.tensor_tensor(as_pairs(strip(better0, jt)), woven(soil_sum(jt, 0, 4 + jt)),
                                        as_pairs(season0[jt][:]), ALU.max)
        w1w = [load_words("w1w0", w1_words[0].bitcast(I32), 2 * H, U8, below="season00"),
               load_words("w1w1", w1_words[1].bitcast(I32), 2 * H, U8, below="season01")]
        w4_raw = [load_float("w4_raw0", w4[cols(0, PASS), :], above="season01")]

        w2_scales.append(sb("w2_scales1", [P, PASS], U8, on=("season02", 0)))
        quantize(w2_codes[1][:], w2_scales[1][:], w2_bf[1][:])
        for k in range(NJ):
            evacuate(strip(soil1, k), soil_sum(k, 1, (k + 2) % NJ))
        g1w = [sb("g1w0", [P, S], U32, on=("w2_bf1", 0)), sb("g1w1", [P, S], U32)]
        pick(g1w[0][:], t1w[0], idx1)
        w4_raw.append(load_float("w4_raw1", w4[cols(PASS, PASS), :], on=("t1w0", 0)))
        seed0_banks = [bank_at(number) for number in range(4, 8)]
        for jt in range(2):
            seed_pass(seed0_banks[jt], 0, jt, 0, 0)
        for half in range(2):
            nc.vector.tensor_copy(g1w[1][:, cols(S // 2 * half, S // 2)],
                                  t1w[1][:].indirect(idx1[:, cols(S // 32 * half, S // 32)]))
        base_sb = sb("base_sb", [P, N // P, S], F32, on=("t1w1", LAP))
        nc.sync.dma_start(out=base_sb[:], in_=base.rearrange("(c p) j -> p c j", p=P))
        better1 = sb("better1", [P, (NJ + 1) * PASS], BF16, below="t1w1")
        nc.vector.tensor_tensor(strip(better1, 0, NJ), soil1[:], season1[:], ALU.max)
        better = [strip(tile, 2 * pair, 2) for tile in (better0, better1) for pair in range(2)]
        seed = [sb("seed%d" % k, [P, 2 * PASS], BF16, at=(80 + 2 * k) * KIB) for k in range(NJ)]
        h = [sb("h%d" % b, [P, PACK * S], BF16) for b in range(2)]

        w4_bf0 = [strip(better1, NJ)]
        nc.vector.tensor_copy(out=w4_bf0[0].rearrange("p (u v i) -> p u i v", v=4, i=PACK),
                              in_=w4_raw[0][:, :, cols(0)].rearrange("p i (u v) -> p u i v", v=4))
        for jt in range(NJ):
            seed_pass(seed0_banks[jt], 1, jt, 0, 0)
            if jt < 2:
                seed_pass(seed0_banks[jt + 2], 0, jt + 2, 0, 0)
            evacuate_seed(strip(seed[jt // 2], jt % 2), seed0_banks[jt])
        for jt in range(NJ):
            bank = bank_at((jt + 2) % NJ)
            for a in (1, 0):
                seed_pass(bank, a, jt, 1, 1)
            evacuate_seed(strip(seed[2 + jt // 2], jt % 2), bank)
            if jt < 2:
                limit(strip(h[0], 2 * jt, 2), turn(seed[jt], 4 + jt), better[jt])
        w4_bf0.append(sb("w4_bf01", [P, PACK * 3 * P], BF16, on=("soil1", 0))[:])
        for c in range(3):
            round_on_gpsimd(w4_bf0[1][:, cols(PASS * c, PASS)], w4_raw[0][:, :, cols(P * (1 + c))])

        h_codes = [sb("h_codes%d" % b, [P, S], U32) for b in range(2)]
        h_scales = [sb("h_scales%d" % b, [P, S], U8, on=("seed1", S * b)) for b in range(2)]
        w4_codes = [sb("w4_codes%d" % b, [P, N], U32) for b in range(2)]
        w4_scales = [sb("w4_scales%d" % b, [P, N], U8, on=("seed1", 2 * S + N * b)) for b in range(2)]

        def output_pass(c, b, first=0, count=S):
            nc.tensor.matmul_mx(out=out_banks[c][:, cols(first, count)], lhsT=w4_codes[b][:, cols(P * c)].bitcast(FP8X4),
                                lhsT_scale=w4_scales[b][:, cols(P * c)],
                                rhs=h_codes[b][:, cols(first, count)].bitcast(FP8X4),
                                rhs_scale=h_scales[b][:, cols(first, count)], start=(b == 0),
                                stop=(b == 1 and first + count == S))

        def finish(c):
            res = sb("res%d" % c, [P, S], F32)
            nc.vector.tensor_tensor(res[:], out_banks[c][:], base_sb[:, c, :], ALU.add)
            nc.sync.dma_start(out=out[cols(P * c), :], in_=res[:])

        quantize(w4_codes[0][:, cols(0)], w4_scales[0][:, cols(0)], w4_bf0[0])
        quantize(h_codes[0][:], h_scales[0][:], h[0][:])
        quantize(w4_codes[0][:, cols(P, 3 * P)], w4_scales[0][:, cols(P, 3 * P)], w4_bf0[1])
        for pair in range(2):
            limit(strip(h[1], 2 * pair, 2), turn(seed[2 + pair], 6 + pair), better[2 + pair])
        out_banks = [bank_at(number) for number in (4, 5, 2, 3)]
        for c in range(N // P):
            output_pass(c, 0)
        w4_bf1 = sb("w4_bf1", [P, PACK * PASS], BF16, on=("w1w0", 0))
        for half in range(2):
            round_on_scalar(strip(w4_bf1, 2 * half, 2), w4_raw[1][:, :, cols(2 * P * half, 2 * P)])
        quantize(h_codes[1][:, cols(0, 2 * P)], h_scales[1][:, cols(0, 2 * P)], strip(h[1], 0, 2))
        quantize(w4_codes[1][:, cols(0, 2 * P)], w4_scales[1][:, cols(0, 2 * P)], strip(w4_bf1, 0, 2))
        for c in range(2):
            output_pass(c, 1, 0, 2 * P)
        quantize(h_codes[1][:, cols(2 * P, 2 * P)], h_scales[1][:, cols(2 * P, 2 * P)], strip(h[1], 2, 2))
        quantize(w4_codes[1][:, cols(2 * P, 2 * P)], w4_scales[1][:, cols(2 * P, 2 * P)], strip(w4_bf1, 2, 2))
        for c in range(N // P):
            if c < 2:
                output_pass(c, 1, 2 * P, 2 * P)
            else:
                output_pass(c, 1)
            finish(c)
